import numpy as np, ml_dtypes
CORES = [3,7,11,15,131,135,139,143]
N = 8
BF = ml_dtypes.bfloat16
W, C, S, RO, B = 2048, 256, 2, 4, 8
def parts(rng):
    x = rng.integers(122, 135, (N, 8, 16, W), dtype=np.int16)
    far = rng.random((N, 8, 16, W), dtype=np.float32) < rng.choice(np.array([0.02, 0.06, 0.1]), (N, 8, 16, 1))
    far = far | (rng.random((N, 8, 1, W)) < 0.02)
    x = np.where(far, rng.integers(0, 256, (N, 8, 16, W), dtype=np.int16), x)
    return x, rng.integers(0, W, (N, 8, 16, C)), rng.integers(0, 4096, (N, 8, 16, 1)), rng.integers(-160, 161, (N, 8, RO, S, C))
def pack(x, c, w, sl):
    return {"xt": np.ascontiguousarray(np.reshape(x, (N, 128, W))).astype(np.float32).astype(BF), "ch": np.ascontiguousarray(np.reshape(c, (N, 128, C))).astype(np.int32),
            "wt": np.ascontiguousarray(np.reshape(w, (N, 128, 1))).astype(np.int32), "sl": np.ascontiguousarray(np.reshape(sl, (N, 8, RO * S * C))).astype(np.int32)}
def setup_inputs(rng):
    return pack(*parts(rng))
def setup_inputs_spread(rng):
    x = np.minimum((np.exp2(8 * rng.random((N, 8, 1, W))) * rng.random((N, 8, 16, W), dtype=np.float32)).astype(np.int16), 255)
    x = np.where(rng.random((N, 8, 16, 1)) < 0.4, 255 - x, x)
    c = np.minimum((W * rng.random((N, 8, 16, C)) ** rng.choice(np.array([0.25, 1.0, 3.0]), (N, 8, 1, C))).astype(np.int64), W - 1)
    w = np.minimum(np.exp2(12 * rng.random((N, 8, 16, 1))).astype(np.int64) - 1, 4095)
    return pack(x, c, w, rng.integers(-255, 256, (N, 8, RO, S, C)))
def setup_inputs_ends(rng):
    b = np.zeros((N, 8, 16, W), bool); sh = int(rng.integers(0, 4))
    for r in range(N):
        for g in range(8):
            md = 4 if g == 7 else (g + r + sh) % 4
            if md == 0: b[r, g] = rng.random((1, W)) < 0.042
            elif md == 1: b[r, g] = rng.random((16, W)) < rng.choice(np.array([0.042, 0.5, 0.958]), (16, 1))
            elif md == 2: b[r, g] = rng.random((1, W)) < 0.958
            elif md == 3: b[r, g] = rng.random((16, W)) < 0.042
            else:
                b[r, g] = rng.random((1, W)) < 0.042; b[r, g, 15] = rng.random(W) < 0.042
    b[:, 7, :, 0] = False; b[:, 7, :, W - 1] = True
    c = np.where(rng.random((N, 8, 16, C)) < rng.choice(np.array([0.0, 0.0625, 0.5, 0.5, 0.9375, 1.0]), (N, 8, 1, C)), W - 1, 0)
    c[:, :, :, 0] = 0; c[:, 7, :, C - 2] = W - 1
    k = np.arange(16); nm = np.where(k % 2 == 0, W - 1, 0); nx = (((nm * 16) >> 6) + nm + 613 * k) & (W - 1)
    c[:, 7, :, C - 1] = nm
    last, first = b[N - 1, 7], b[0, 7]
    last[:, nx] = False; last[:15, nx[0]] = True; last[15, nx] = True
    first[:, nx] = False; first[:, nx[0]] = True
    w = 4095 * rng.integers(0, 2, (N, 8, 16, 1)); w[:, 1, 0] = 0; w[:, 1, 1] = 4095; w[0, 0] = 0; w[N - 1, 7] = 4095
    sl = 510 * rng.integers(0, 2, (N, 8, RO, S, C)) - 255; sl[N - 1, 7, 0, 0, C - 1] = -255
    return pack(255 * b.astype(np.int16), c, w, sl)
def setup_inputs_corners(rng):
    x, c, w, sl = parts(rng); i = np.arange(C)
    x[1, 0] = 255 * rng.integers(0, 2, (16, W))
    pin = 5 * C + int(rng.integers(0, C)) if W == 4096 else -1
    for a, m in ((0, int(rng.choice(np.array([31, 32, 33, 8 * C - 1])))), (2, 8 * C)):
        x[a] = rng.integers(0, 256, (8, 16, 1)); x[a, 7, 15] = 255; x[a, 7, 14] = 0
        ways = np.stack([np.zeros((8, C), np.int64), np.full((8, C), W - 1), np.tile(B * i, (8, 1)), np.tile(B * i + B - 1, (8, 1)), rng.integers(0, W, (8, C))])
        c[a] = np.take_along_axis(ways, rng.integers(0, 5, (1, 8, C)), 0).reshape(8, 1, C)
        o = rng.permutation(8 * C)
        if a == 0: o = o[o != pin]
        h = np.zeros(8 * C, bool); h[o[:m]] = True
        sl[a, :, 0] = -255; sl[a, :, 0, 0] = np.where(h.reshape(8, C), 0, -255)
    if N > 4: x[4, :4] = rng.integers(0, 256, (4, 16, 1))
    c[1, 5] = 0; c[1, 6] = W - 1
    for a in (1, 3):
        sl[a] = rng.choice(np.array([-255, -1, 0, 1, 255]), (8, RO, S, C))
        c[a, :5] = np.where(rng.random((5, 1, C)) < 0.5, B * i + (B - 1) * rng.integers(0, 2, (5, 16, C)), c[a, :5])
    w[:, 1] = 0; w[:, 2] = 4095; w[:, 3, :15] = 0; w[:, 3, 15] = 4095; w[:, 4] = 1
    for g, low in ((0, 0), (6, 4095)):
        v = rng.integers(220, 256, 16); v[14] = 2; v[15] = 1
        z = rng.integers(3500, 4096, 16); z[14] = rng.integers(0, 2048); z[15] = 0
        z[15] = (low - int(np.sum(v * z))) & 4095
        if (int(np.sum(v * z)) >> 12) & 1 == 0: z[14] += 2048
        x[0, g] = v.reshape(16, 1); w[0, g] = z.reshape(16, 1)
    if pin >= 0:
        p = int(rng.integers(0, 16)); x[0, 5, p] = 1; w[0, 5] = 0; w[0, 5, p] = 4075
        first = (((c[0, 5] * 4075) >> 6) + c[0, 5]) & (W - 1)
        c[0, 5] = np.where(first == 2557, 0, c[0, 5]); c[0, 5, :, pin - 5 * C] = 4093; sl[0, 5, 0, 0, pin - 5 * C] = 0
        nx = (2557 + 613 * np.arange(16)) & (W - 1); own = x[1, 5]; own[:, nx] = rng.integers(122, 135, (16, 1))
    return pack(x, c, w, sl)
def setup_inputs_ties(rng):
    x = rng.integers(0, 254, (N, 8, 16, 1), dtype=np.int16) + 2 * (rng.random((N, 8, 16, W), dtype=np.float32) < rng.choice(np.array([0.02, 0.05]), (N, 8, 16, 1))).astype(np.int16)
    c = rng.integers(0, W, (N, 8, 16, C)); few = np.take_along_axis(c, rng.integers(0, 4, (N, 8, 16, C)), 2)
    c = np.where(rng.random((N, 8, 1, C)) < 0.5, few, c); sl = rng.integers(-3, 4, (N, 8, RO, S, C))
    x[0] = rng.integers(0, 256, (8, 16, 1)); x[2, :2] = rng.integers(0, 256, (2, 16, 1)); c[0] = rng.integers(0, W, (8, 1, C))
    x[1, :, 15] = rng.integers(0, 254, (8, 1)) + 2 * (np.arange(W) & 1)
    h = np.zeros(8 * C, bool); h[rng.permutation(8 * C)[:26 + 2 * int(rng.integers(0, 3)) + 32 * int(rng.integers(0, C // 4))]] = True
    sl[0, :, 0] = -1; sl[0, :, 0, 0] = np.where(h.reshape(8, C), 0, -1)
    return pack(x, c, rng.integers(0, 4096, (N, 8, 16, 1)), sl)
def check_inputs(d):
    bad = []
    for k, lo, hi in (("xt", 0, 255), ("ch", 0, W - 1), ("wt", 0, 4095), ("sl", -255, 255)):
        v = np.asarray(d[k]).astype(np.float64)
        if not (np.min(v) >= lo and np.max(v) <= hi): bad.append("range of " + k)
        if not np.all(v == np.floor(v)): bad.append("whole numbers in " + k)
    return bad
def look(tab, c):
    v = np.take_along_axis(tab, c.reshape(8, 1, 16 * C), 2).reshape(8, 16, 16, C)
    y = np.max(v, axis=2).astype(np.int64); m = np.min(v, axis=2).astype(np.int64)
    return y, np.add.reduce(y - m, axis=1)
def reference(xt, ch, wt, sl):
    X = xt.astype(np.float32).astype(np.int32).reshape(N, 8, 16, W); c = ch.astype(np.int64).reshape(N, 8, 16, C)
    w = wt.astype(np.int64).reshape(N, 8, 16, 1); slack = sl.astype(np.int64).reshape(N, 8, RO, S, C)
    kappa = np.zeros(N, np.int64); k613 = (613 * np.arange(16)).reshape(1, 16, 1)
    for t in range(RO):
        states, tops, wrong = [], [], []
        for r in range(N):
            q = (r + 1 + t % (N - 1)) % N
            s = c[r]; y, e = look(X[r], s); eq = look(X[q], s)[1]
            fs, fy = s, y; right = np.ones((8, C), bool)
            for j in range(S):
                u = np.add.reduce(w[r] * y, axis=1) & 4095
                n = (((s * u[:, None, :]) >> 6) + s + k613 + 77 * j + kappa[r]) & (W - 1)
                yn, en = look(X[r], n); qn = look(X[q], n)[1]; a = slack[r, :, t, j]
                guess = en <= e + a; true = en + qn <= e + eq + a
                go = (right & true)[:, None, :]; fs = np.where(go, n, fs); fy = np.where(go, yn, fy)
                right = right & (guess == true)
                on = guess[:, None, :]; s = np.where(on, n, s); y = np.where(on, yn, y); e = np.where(guess, en, e); eq = np.where(guess, qn, eq)
            states.append(fs); tops.append(fy); wrong.append(np.count_nonzero(~right) & 31)
        for r in range(N):
            place = (B * np.arange(C)[None, :] + (np.add.reduce(w[r] * tops[r], axis=1) & (B - 1)))[:, None, :]
            old = np.take_along_axis(X[r], place, 2)
            np.put_along_axis(X[r], place, ((old + tops[r]) >> 1).astype(np.int32), 2)
        c = np.stack(states); kappa = np.array(wrong, np.int64)
    return {"yc": c.reshape(N, 128, C).astype(np.float32), "yx": X.reshape(N, 128, W).astype(np.float32).astype(BF)}

@@ -1,0 +1,495 @@
+from concourse.mybir import AluOpType, AxisListType, ActivationFunctionType
+
+R, NC, HC = 4, 256, 128
+HN = 16 * HC
+NG = 6
+
+SCRATCH = {
+    "tab0": ("sbuf", [128, 2048], "bfloat16"), "tab1": ("sbuf", [128, 2048], "bfloat16"),
+    "mxw": ("sbuf", [128, 7 * HN], "bfloat16"),
+    "mno": ("sbuf", [128, 2 * HN], "bfloat16"),
+    "pmx": ("sbuf", [128, 4 * HN], "bfloat16"), "pmn": ("sbuf", [128, 4 * HN], "bfloat16"),
+    "mkx": ("sbuf", [128, HN], "bfloat16"), "mkn": ("sbuf", [128, HN], "bfloat16"),
+    "outl": ("sbuf", [128, R * 3 * NC], "uint16"), "inl": ("sbuf", [128, R * 3 * NC], "uint16"),
+    "ro": ("sbuf", [128, R * 48], "float32"), "rin": ("sbuf", [128, R * 48], "float32"),
+    "chi": ("sbuf", [128, NC], "int32"), "wti": ("sbuf", [128, 1], "int32"), "sli": ("sbuf", [128, 2048], "int32"),
+    "slb": ("sbuf", [128, 2048], "bfloat16"), "al": ("sbuf", [128, 128], "float32"),
+    "ones": ("sbuf", [128, 144], "bfloat16"), "blk0": ("sbuf", [128, 144], "bfloat16"), "blk": ("sbuf", [128, 144], "bfloat16"),
+    "qo": ("sbuf", [128, 144], "bfloat16"), "qn": ("sbuf", [128, 144], "bfloat16"), "q7": ("sbuf", [128, 144], "bfloat16"),
+    "qg": ("sbuf", [128, 144], "bfloat16"),
+    "wh": ("sbuf", [128, 128], "bfloat16"), "wl": ("sbuf", [128, 128], "bfloat16"),
+    "sm": ("sbuf", [128, 768], "float32"), "smi": ("sbuf", [128, 256], "int32"),
+    "rt": ("sbuf", [128, 16], "bfloat16"), "fo": ("sbuf", [128, 48], "uint16"), "so": ("sbuf", [128, 16], "uint16"),
+    "fy": ("sbuf", [128, NC], "bfloat16"), "xs": ("sbuf", [128, NC], "int32"), "xh": ("sbuf", [128, NC], "int32"),
+    "nx": ("sbuf", [128, NC], "int32"), "ycf": ("sbuf", [128, NC], "float32"),
+    "nw0": ("sbuf", [128, 4 * NC], "int32"), "nw1": ("sbuf", [128, 4 * NC], "int32"),
+}
+for _k in range(NG):
+    SCRATCH["gb%d" % _k] = ("sbuf", [128, HN], "bfloat16")
+for _h in range(2):
+    for _k in ("ua", "ub", "uc", "ud"):
+        SCRATCH["%s%d" % (_k, _h)] = ("sbuf", [128, HC], "int32")
+for _k in range(8):
+    SCRATCH["p%d" % _k] = ("psum", [128, 512], "float32")
+
+DMAS = ["dch", "dwt", "dsl", "dx0", "dx1", "dc0", "dc1", "dc2", "dyx0", "dyx1", "dyc"]
+SEMAPHORES = ["qv", "qs", "qt", "qg", "loc"] + DMAS
+SEMAPHORES += ["l%d%d%d" % (t, k, h) for t in range(R) for k in range(3) for h in range(2)]
+SEMAPHORES += ["r%d%d" % (t, k) for t in range(R) for k in range(2)]
+
+
+def rank_program(g, core, T, topo):
+    rank = T.rank_of(core)
+    if rank is None:
+        return
+    A, F = AluOpType, ActivationFunctionType
+    N = len(T.cores)
+    eng = {"v": g.vector, "s": g.scalar, "t": g.tensor, "g": g, "y": g.sync}
+    count = {"v": 0, "s": 0, "t": 0, "g": 0}
+    clock = {q: {} for q in eng}
+    acc = {}
+    nloc = [0]
+
+    def view(name, lo, hi, step=1, parts=None):
+        t = T[name]
+        if step == 1:
+            ap = t[:, lo:hi] if parts is None else t[0:parts, lo:hi]
+        else:
+            ap = t[:, lo:hi:step] if parts is None else t[0:parts, lo:hi:step]
+        return (ap, name, lo, hi)
+
+    def sub(v, lo, n):
+        return view(v[1], v[2] + lo, v[2] + lo + n)
+
+    def ind(win, off):
+        return (win[0].indirect(off[0]), win, off)
+
+    def learn(q, ck):
+        c = clock[q]
+        for s, v in ck.items():
+            if c.get(s, 0) < v:
+                c[s] = v
+
+    def flat(vs):
+        out = []
+        for v in vs:
+            out += [v[1], v[2]] if len(v) == 3 else [v]
+        return out
+
+    def region(v):
+        if v[1][0] == "p" and len(v[1]) == 2:
+            return v[1], 0, 512, True
+        return v[1], v[2], v[3], False
+
+    def before(q, reads, writes):
+        need, cks = {}, []
+        for vs, w in ((reads, False), (writes, True)):
+            for v in flat(vs):
+                name, lo, hi, ps = region(v)
+                for a in acc.get(name, ()):
+                    if a[0] < hi and lo < a[1]:
+                        if ps and q == "t" and a[3] == "t":
+                            continue
+                        if w or a[2] or (ps and a[3] != q):
+                            need[a[4]] = max(need.get(a[4], 0), a[5])
+                            cks.append((a[4], a[6]))
+        for s in sorted(need):
+            if clock[q].get(s, 0) < need[s] and not any(o != s and ck.get(s, 0) >= need[s] for o, ck in cks):
+                eng[q].wait_ge(T.sem[s], need[s])
+                clock[q][s] = need[s]
+        for _, ck in cks:
+            learn(q, ck)
+
+    def after(q, reads, writes, sem, val):
+        ck = dict(clock[q])
+        ck[sem] = val
+        for vs, w in ((reads, False), (writes, True)):
+            for v in flat(vs):
+                name, lo, hi, ps = region(v)
+                lst = acc.setdefault(name, [])
+                if w:
+                    lst[:] = [a for a in lst if not (lo <= a[0] and a[1] <= hi) or (ps and a[3] == q and not a[2])]
+                lst.append((lo, hi, w, q, sem, val, ck))
+
+    def op(q, call, reads, writes):
+        before(q, reads, writes)
+        ins = call()
+        count[q] += 1
+        ins.then_inc(T.sem["q" + q], 1)
+        after(q, reads, writes, "q" + q, count[q])
+
+    def dma(q, sem, out, in_, reads, writes):
+        before(q, reads, writes)
+        eng[q].dma_start(out, in_).then_inc(T.sem[sem], 16)
+        after(q, reads, writes, sem, 16)
+
+    def cp(out, in_):
+        op("v", lambda: g.vector.tensor_copy(out[0], in_[0]), [in_], [out])
+
+    def tt(out, a, b, o):
+        op("v", lambda: g.vector.tensor_tensor(out[0], a[0], b[0], o), [a, b], [out])
+
+    def ts(out, a, s1, o1, s2=None, o2=None):
+        col = isinstance(s1, tuple)
+        rd = [a, s1] if col else [a]
+        x1 = s1[0] if col else s1
+        if o2 is None:
+            op("v", lambda: g.vector.tensor_scalar(out[0], a[0], x1, None, o1), rd, [out])
+        else:
+            op("v", lambda: g.vector.tensor_scalar(out[0], a[0], x1, s2, o1, o2), rd, [out])
+
+    def fill(out, c):
+        op("v", lambda: g.vector.memset(out[0], c), [], [out])
+
+    def mms(out, pairs, start, stop):
+        def call():
+            ins = None
+            for k, (l, r) in enumerate(pairs):
+                ins = g.tensor.matmul(out[0], l[0], r[0], start and k == 0, stop and k == len(pairs) - 1)
+            return ins
+        rd = [l for l, _ in pairs] + [r for _, r in pairs]
+        op("t", call, rd, [out])
+
+    def send(dst, src, land, sem):
+        before("g", [src], [])
+        d = T.cores[dst]
+        es = topo.engines(core, d)[:8]
+        rid, pid = topo.addr(d, core)
+        g.remote_dma(T[land][:, src[2]:src[3]], src[0], T.sem[sem], T.sem.loc, pid, rid, sum(1 << e for e in es))
+        nloc[0] += len(es)
+
+    def landed(src, land, lo, hi, sem):
+        n = len(topo.engines(T.cores[src], core)[:8])
+        acc.setdefault(land, []).append((lo, hi, True, "x", sem, n, {sem: n}))
+
+    cols, nxt = {}, {"sm": 0, "smi": 0}
+
+    def small(name, n, buf="sm"):
+        if name not in cols:
+            cols[name] = (buf, nxt[buf])
+            nxt[buf] += n + (n & 1)
+        b, o = cols[name]
+        return view(b, o, o + n)
+
+    def partner(t):
+        return (rank + 1 + t % (N - 1)) % N
+
+    def asker(t):
+        return (rank - 1 - t % (N - 1)) % N
+
+    def lists(t, k, h=None, buf="outl"):
+        lo = (t * 3 + k) * NC
+        return view(buf, lo, lo + NC) if h is None else view(buf, lo + h * HC, lo + h * HC + HC)
+
+    def send_list(t, k, h=None):
+        send(partner(t), lists(t, k, h), "inl", "l%d%d%d" % (t, k, h or 0))
+
+    def send_spans(t, k):
+        lo = t * 48
+        send(asker(t), view("ro", lo, lo + 32) if k == 0 else view("ro", lo + 32, lo + 48), "rin", "r%d%d" % (t, k))
+
+    for t in range(R):
+        for k in range(3):
+            for h in ((None,) if k == 0 else (0, 1)):
+                v = lists(t, k, h, "inl")
+                landed(asker(t), "inl", v[2], v[3], "l%d%d%d" % (t, k, h or 0))
+        landed(partner(t), "rin", t * 48, t * 48 + 32, "r%d0" % t)
+        landed(partner(t), "rin", t * 48 + 32, t * 48 + 48, "r%d1" % t)
+
+    def names(t, slot, h=None):
+        b, lo = "nw%d" % (t % 2), slot * NC
+        return view(b, lo, lo + NC) if h is None else view(b, lo + h * HC, lo + h * HC + HC)
+
+    dma("y", "dch", T.chi[:], T.ch[:], [], [view("chi", 0, NC)])
+    dma("s", "dx0", T.tab0[:], T.xt[:], [], [view("tab0", 0, 2048)])
+    dma("y", "dwt", T.wti[:], T.wt[:], [], [view("wti", 0, 1)])
+    dma("y", "dsl", T.sli[0:8, :], T.sl[:], [], [view("sli", 0, 2048)])
+    fill(view("ones", 0, 144), 1.0)
+    fill(view("mkx", 0, HN), 1.0)
+    fill(view("mkn", 0, HN), 0.0)
+    fill(view("mkx", 0, HN, 16), 0.0)
+    fill(view("mkn", 0, HN, 16), 512.0)
+    cp(lists(0, 0), view("chi", 0, NC))
+    cp(names(0, 0), view("chi", 0, NC))
+
+    pidx, ic, pm = small("pidx", 8, "smi"), small("ic", 8, "smi"), small("pm", 16, "smi")
+    ones, blk = view("ones", 0, 144), view("blk", 0, 144)
+    op("g", lambda: g.affine_select(T.blk0[:], T.ones[:], [[-16, 9], [0, 16]], A.is_ge, 0.0, 0, 1), [ones], [view("blk0", 0, 144)])
+    op("g", lambda: g.affine_select(T.blk[:], T.blk0[:], [[16, 9], [0, 16]], A.is_ge, 0.0, 15, -1), [view("blk0", 0, 144)], [blk])
+    op("g", lambda: g.affine_select(T.qo[:], T.blk[:], [[0, 9], [1, 16]], A.is_equal, 0.0, -15, 0), [blk], [view("qo", 0, 144)])
+    op("g", lambda: g.iota(pidx[0], [[0, 8]], 0, 1), [], [pidx])
+    op("g", lambda: g.iota(ic[0], [[16, 8]], 0, 0), [], [ic])
+    op("g", lambda: g.affine_select(T.qg[:], T.ones[:], [[1, 144]], A.is_equal, 0.0, -15, -16), [ones], [view("qg", 0, 144)])
+    send_list(0, 0)
+
+    wti = view("wti", 0, 1)
+    for mask, col, src, dst, n in ((4032, "fa", "blk", "wh", 128), (63, "fb", "blk", "wl", 128), (7, "fc", "qo", "q7", 144)):
+        i = small(col + "i", 1, "smi")
+        f = small(col, 1)
+        ts(i, wti, mask, A.bitwise_and)
+        cp(f, i)
+        ts(view(dst, 0, n), view(src, 0, n), f, A.mult)
+    ts(view("qn", 0, 144), view("qo", 0, 144), -1.0, A.mult)
+    ts(sub(pm, 0, 8), pidx, 15, A.bitwise_and)
+    ib, cb, base, d2, tmp, fl = (small(n, 48) for n in ("ib", "cb", "base", "d2", "tmp", "fl"))
+    inn, iv, inq = sub(ib, 0, 16), small("iv", 16), small("inq", 16)
+    tt(sub(inn, 0, 8), sub(pm, 0, 8), ic, A.add)
+    ts(sub(inn, 8, 8), sub(inn, 0, 8), float(HC), A.add)
+    ts(sub(ib, 16, 16), inn, 16.0, A.mult, 15.0, A.add)
+    ts(sub(cb, 16, 16), inn, 16.0, A.mult, 15.0 + 4 * HN, A.add)
+    ts(iv, inn, 8.0, A.mult)
+    ts(inq, inn, 3.0 * NC, A.add, 1.0 / NC, A.mult)
+    k6, k613, c0 = small("k6", 2, "smi"), small("k613", 1), small("c0", 1)
+    ts(sub(k6, 0, 1), sub(pm, 0, 1), 613.0, A.mult)
+    ts(sub(k6, 1, 1), sub(k6, 0, 1), 2047, A.bitwise_and)
+    cp(k613, sub(k6, 1, 1))
+    cp(c0, sub(k6, 1, 1))
+    for t in range(2):
+        fill(names(t, 2), 0)
+
+    op("v", lambda: g.vector.tensor_copy(T.slb[0:8, :], T.sli[0:8, :]), [view("sli", 0, 2048)], [view("slb", 0, 2048)])
+    mms(view("p7", 0, 128), [(view("qg", 15 - j, 143 - j, 1, 8), view("slb", j, 2048, 16, 8)) for j in range(16)], True, True)
+
+    ring, where = [0], {}
+
+    def gather(key, t, off, chunks=1):
+        b = "gb%d" % (ring[0] % NG)
+        ring[0] += 1
+        w = HC // chunks
+        for c in range(chunks):
+            src = ind(view("tab%d" % (t % 2), 0, 2048), sub(off, c * w, w))
+            dst = view(b, c * w * 16, (c + 1) * w * 16)
+            op("s", lambda: g.scalar.activation(dst[0], src[0], F.Copy), [src], [dst])
+        where[key] = (b, chunks)
+
+    def scan(key, out, least, chunks=None):
+        b, n = where[key]
+        w = HN // n
+        o0, o1 = (A.max, A.min) if least else (A.mult, A.max)
+        for c in (range(n) if chunks is None else chunks):
+            d0, d1 = view("mkn" if least else "mkx", 0, w), view(b, c * w, (c + 1) * w)
+            o = view(out[0], out[1] + c * w, out[1] + (c + 1) * w)
+            op("v", lambda: g.vector.tensor_tensor_scan(o[0], d0[0], d1[0], 0.0, o0, o1), [d0, d1], [o])
+
+    def own(slot, h=0):
+        return ("mxw", (slot * 2 + h) * HN)
+
+    def own_min(h=0):
+        return ("mno", h * HN)
+
+    def urep(h, slot):
+        b, o = own(slot, h)
+        y = view(b, o + 15, o + HN, 16)
+        mms(view("p%d" % h, 0, HC), [(view("wh", 0, 128), y), (view("wl", 0, 128), y)], True, True)
+
+    def tolist(bank, col, q, src, n, start, stop):
+        b, o = src
+        mms(view(bank, col, col + 8 * n),
+            [(view(q, 15 - j, 143 - j), view(b, o + 16 * j + 15, o + n * HN, 256)) for j in range(16)], start, stop)
+
+    def span_max(bank, col, src, n):
+        tolist(bank, col, "qo", src, n, True, False)
+
+    def span_min(bank, col, src, n):
+        tolist(bank, col, "qn", src, n, False, True)
+
+    def low3(slot):
+        tolist("p7", slot * 16, "q7", own(slot), 2, True, True)
+
+    def ptab(k, least):
+        return ("pmn" if least else "pmx", (k % 2) * 2 * HN)
+
+    def pscan(k, h, least):
+        b, o = ptab(k, least)
+        scan("P%d%d" % (k, h), (b, o + h * HN), least)
+
+    def proposal(t, h, slot):
+        ua, ub, uc, ud = (view("%s%d" % (k, h), 0, HC) for k in ("ua", "ub", "uc", "ud"))
+        cp(ua, view("p%d" % h, 0, HC))
+        ts(ub, ua, 4095, A.bitwise_and)
+        tt(uc, ub, names(t, slot, h), A.mult)
+        tt(ud, uc, view("p2", h * HC, (h + 1) * HC), A.add)
+        ts(names(t, slot + 1, h), ud, 6, A.arith_shift_right, 2047, A.bitwise_and)
+
+    es, en, ths, h0, de, dq, z, d0, e0, esa, th1, q1, w1, thb, hq, m2, h1, eq, du = (
+        small(n, 16) for n in ("es", "en", "ths", "h0", "de", "dq", "z", "d0", "e0", "esa", "th1", "q1", "w1", "thb", "hq", "m2", "h1",
+                               "eq", "du"))
+    ui, u7 = small("ui", 48, "smi"), small("u7", 48, "smi")
+    kn, ki, kk = small("kn", 1), small("ki", 1, "smi"), small("kk", 1, "smi")
+
+    def slack(t, j):
+        return view("al", (t * 2 + j) * 16, (t * 2 + j) * 16 + 16)
+
+    def second(t, h):
+        h8, q8, so = sub(h0, 8 * h, 8), sub(hq, 8 * h, 8), view("so", 8 * h, 8 * h + 8)
+        tt(h8, view("p3", 8 * h, 8 * h + 8), sub(ths, 8 * h, 8), A.is_le)
+        tt(q8, sub(inq, 8 * h, 8), h8, A.subtract)
+        ts(so, q8, float(NC), A.mult)
+        cp(lists(t, 2, h), ind(view("nw%d" % (t % 2), 0, 4 * NC), so))
+        send_list(t, 2, h)
+
+    for t in range(R):
+        cur, new = "tab%d" % (t % 2), "tab%d" % ((t + 1) % 2)
+        gather("L00", t, lists(t, 0, 0), 2)
+        gather("L01", t, lists(t, 0, 1))
+        if t:
+            cp(names(t, 0), lists(t, 0))
+            op("v", lambda: g.vector.tensor_reduce(kn[0], T.p7[:, 64:80], AxisListType.X, A.add), [view("p7", 64, 80)], [kn])
+            ts(ki, kn, -1.0, A.mult, float(8 * NC), A.add)
+            ts(kk, ki, 31, A.bitwise_and)
+            tt(c0, k613, kk, A.add)
+        ts(view("p2", 0, NC), names(t, 0), c0, A.add, 64.0, A.mult)
+        scan("L00", own(0, 0), False, [0])
+        scan("L00", own_min(0), True, [0])
+        scan("L00", own(0, 0), False, [1])
+        urep(0, 0)
+        scan("L00", own_min(0), True, [1])
+        proposal(t, 0, 0)
+        cp(lists(t, 1, 0), names(t, 1, 0))
+        send_list(t, 1, 0)
+        gather("P00", t, lists(t, 0, 0, "inl"))
+        gather("L10", t, lists(t, 1, 0))
+        scan("L01", own(0, 1), False)
+        urep(1, 0)
+        span_max("p4", 0, own(0), 2)
+        scan("L01", own_min(1), True)
+        span_min("p4", 0, own_min(), 2)
+        proposal(t, 1, 0)
+        cp(lists(t, 1, 1), names(t, 1, 1))
+        send_list(t, 1, 1)
+        if t == 0:
+            dma("y", "dx1", T[new][:], T.xt[:], [names(t, 1, 1)], [view(new, 0, 2048)])
+            cp(view("al", 0, 128), view("p7", 0, 128))
+        else:
+            dma("y", "dc%d" % (t - 1), T[new][:], T[cur][:], [view(cur, 0, 2048), names(t, 1, 1)], [view(new, 0, 2048)])
+        gather("L11", t, lists(t, 1, 1))
+        gather("P01", t, lists(t, 0, 1, "inl"))
+        nx = view("nx", 0, NC)
+        ts(nx, names(t, 1), 77.0, A.add)
+        ts(names(t, 3), nx, 2047, A.bitwise_and)
+        ts(view("p2", 0, NC), nx, c0, A.add, 64.0, A.mult)
+        pscan(0, 0, False)
+        pscan(0, 0, True)
+        cp(es, view("p4", 0, 16))
+        tt(ths, es, slack(t, 0), A.add)
+        low3(0)
+        for h in range(2):
+            k = "L1%d" % h
+            if h == 0:
+                scan(k, own(1, h), False)
+            urep(h, 1)
+            span_max("p3", 8 * h, own(1, h), 1)
+            scan(k, own_min(h), True)
+            span_min("p3", 8 * h, own_min(h), 1)
+            proposal(t, h, 1)
+            if h == 0:
+                scan("L11", own(1, 1), False)
+            else:
+                pscan(0, 1, False)
+            second(t, h)
+            gather("P1%d" % h, t, lists(t, 1, h, "inl"))
+        low3(1)
+        span_max("p6", 0, ptab(0, False), 2)
+        pscan(0, 1, True)
+        span_min("p6", 0, ptab(0, True), 2)
+        pscan(1, 0, False)
+        pscan(1, 0, True)
+        gather("P20", t, lists(t, 2, 0, "inl"))
+        gather("P21", t, lists(t, 2, 1, "inl"))
+        tt(de, view("p3", 0, 16), es, A.subtract)
+        tt(esa, es, slack(t, 1), A.add)
+        tt(q1, h0, de, A.mult)
+        tt(th1, esa, q1, A.add)
+        cp(sub(ui, 0, 32), view("p7", 0, 32))
+        ts(sub(u7, 0, 32), sub(ui, 0, 32), 7, A.bitwise_and)
+        tt(du, sub(u7, 16, 16), sub(u7, 0, 16), A.subtract)
+        if t == R - 1:
+            ts(sub(iv, 8, 8), sub(iv, 8, 8), -1024.0, A.add)
+        tt(sub(ib, 32, 16), iv, sub(u7, 0, 16), A.add)
+        ts(sub(cb, 0, 16), hq, float(NC), A.mult)
+        pscan(1, 1, False)
+        span_max("p6", 16, ptab(1, False), 2)
+        pscan(1, 1, True)
+        span_min("p6", 16, ptab(1, True), 2)
+        gather("L20", t, lists(t, 2, 0), 2)
+        gather("L21", t, lists(t, 2, 1), 2)
+        pscan(2, 0, False)
+        cp(view("ro", t * 48, t * 48 + 32), view("p6", 0, 32))
+        send_spans(t, 0)
+        pscan(2, 0, True)
+        pscan(2, 1, False)
+        span_max("p6", 32, ptab(2, False), 2)
+        pscan(2, 1, True)
+        span_min("p6", 32, ptab(2, True), 2)
+        scan("L20", own(2, 0), False)
+        span_max("p5", 0, own(2, 0), 1)
+        cp(view("ro", t * 48 + 32, t * 48 + 48), view("p6", 32, 48))
+        send_spans(t, 1)
+        scan("L20", own_min(0), True)
+        span_min("p5", 0, own_min(0), 1)
+        scan("L21", own(2, 1), False)
+        low3(2)
+        scan("L21", own(3), True)
+        tolist("p5", 8, "qo", own(2, 1), 2, True, True)
+        qs, qn, qx = (view("rin", t * 48 + 16 * k, t * 48 + 16 * k + 16) for k in range(3))
+        tt(dq, qn, qs, A.subtract)
+        tt(z, de, dq, A.add)
+        tt(d0, z, slack(t, 0), A.is_le)
+        tt(w1, esa, qs, A.add)
+        tt(q1, h0, z, A.mult)
+        tt(e0, h0, d0, A.is_equal)
+        ts(sub(tmp, 0, 16), d0, float(NC), A.mult)
+        ts(sub(tmp, 16, 16), d0, float(2 * HN), A.mult)
+        tt(sub(tmp, 32, 16), d0, du, A.mult)
+        tt(w1, w1, q1, A.add)
+        ts(thb, e0, 65536.0, A.mult, -65536.0, A.add)
+        tt(base, tmp, ib, A.add)
+        tt(w1, w1, thb, A.add)
+        tt(sub(d2, 0, 32), sub(cb, 0, 32), sub(base, 0, 32), A.subtract)
+        cp(sub(ui, 32, 16), view("p7", 32, 48))
+        ts(sub(u7, 32, 16), sub(ui, 32, 16), 7, A.bitwise_and)
+        tt(sub(cb, 32, 16), iv, sub(u7, 32, 16), A.add)
+        tt(sub(d2, 32, 16), sub(cb, 32, 16), sub(base, 32, 16), A.subtract)
+        tt(thb, w1, qx, A.subtract)
+        tt(sub(m2, 0, 8), view("p5", 0, 8), sub(thb, 0, 8), A.is_le)
+        tt(sub(z, 0, 8), view("p5", 8, 16), sub(thb, 8, 8), A.subtract)
+        tt(sub(m2, 8, 8), view("p5", 16, 24), sub(z, 0, 8), A.is_ge)
+        for k in range(3):
+            tt(sub(tmp, 16 * k, 16), m2, sub(d2, 16 * k, 16), A.mult)
+        tt(fl, tmp, base, A.add)
+        cp(view("fo", 0, 48), fl)
+        fy, xs, xh = view("fy", 0, NC), view("xs", 0, NC), view("xh", 0, NC)
+        src = ind(view("mxw", 0, 6 * HN), view("fo", 16, 32))
+        op("s", lambda: g.scalar.activation(fy[0], src[0], F.Copy), [src], [fy])
+        picked = ind(view("nw%d" % (t % 2), 0, 4 * NC), view("fo", 0, 16))
+        vo = view("fo", 32, 48)
+        if t < R - 1:
+            cp(lists(t + 1, 0), picked)
+            send_list(t + 1, 0)
+        else:
+            cp(view("ycf", 0, NC), picked)
+            dma("y", "dyc", T.yc[:], T.ycf[:], [view("ycf", 0, NC)], [])
+        parts = [(0, 1)] if t < R - 1 else [(0, 2), (1, 2)]
+        for i, n in parts:
+            w = NC // n
+            xi, hi, oi = sub(xs, i * w, w), sub(xh, i * w, w), sub(vo, i * w // 16, w // 16)
+            tt(xi, ind(view(cur, i * 8 * w, (i + 1) * 8 * w), oi), sub(fy, i * w, w), A.add)
+            ts(hi, xi, 1, A.arith_shift_right)
+            col = view(new, i * 8 * w, (i + 1) * 8 * w)
+            out = ind(col, oi)
+            op("v", lambda: g.vector.tensor_copy(out[0], hi[0]), [hi, oi], [col])
+            if n == 2:
+                dma("ys"[i], "dyx%d" % i, T.yx[:, col[2]:col[3]], col[0], [col], [])
+        if t < R - 1:
+            tt(sub(h1, 0, 8), view("p5", 0, 8), sub(th1, 0, 8), A.is_le)
+            tt(sub(z, 8, 8), view("p5", 8, 16), sub(th1, 8, 8), A.subtract)
+            tt(sub(h1, 8, 8), view("p5", 16, 24), sub(z, 8, 8), A.is_ge)
+            tt(eq, h1, m2, A.is_equal)
+            tt(view("rt", 0, 16), eq, e0, A.mult)
+            mms(view("p7", 64, 80), [(view("ones", 0, 128), view("rt", 0, 16))], True, True)
+
+    for q in "vstg":
+        g.wait_ge(T.sem["q" + q], count[q])
+    for s in DMAS:
+        g.wait_ge(T.sem[s], 16)
+    g.wait_ge(T.sem.loc, nloc[0])

@@ -1,62 +1,64 @@
-from concourse.mybir import AluOpType, AxisListType, ActivationFunctionType
+from concourse.mybir import AluOpType, ActivationFunctionType
 
-R, NC, HC = 4, 256, 128
+R, HC = 4, 128
 HN = 16 * HC
-NG = 6
+BIG = 65536.0
+MODE = "dual"
+KINDS = ("L0", "P0", "L1", "P1", "L2", "P2")
 
 SCRATCH = {
-    "tab0": ("sbuf", [128, 2048], "bfloat16"), "tab1": ("sbuf", [128, 2048], "bfloat16"),
-    "mxw": ("sbuf", [128, 7 * HN], "bfloat16"),
-    "mno": ("sbuf", [128, 2 * HN], "bfloat16"),
-    "pmx": ("sbuf", [128, 4 * HN], "bfloat16"), "pmn": ("sbuf", [128, 4 * HN], "bfloat16"),
     "mkx": ("sbuf", [128, HN], "bfloat16"), "mkn": ("sbuf", [128, HN], "bfloat16"),
-    "outl": ("sbuf", [128, R * 3 * NC], "uint16"), "inl": ("sbuf", [128, R * 3 * NC], "uint16"),
-    "ro": ("sbuf", [128, R * 48], "float32"), "rin": ("sbuf", [128, R * 48], "float32"),
-    "chi": ("sbuf", [128, NC], "int32"), "wti": ("sbuf", [128, 1], "int32"), "sli": ("sbuf", [128, 2048], "int32"),
-    "slb": ("sbuf", [128, 2048], "bfloat16"), "al": ("sbuf", [128, 128], "float32"),
+    "outl": ("sbuf", [128, R * 6 * HC], "uint16"), "inl": ("sbuf", [128, R * 6 * HC], "uint16"),
+    "ro": ("sbuf", [128, R * 80], "float32"), "rin": ("sbuf", [128, R * 80], "float32"),
+    "wti": ("sbuf", [128, 2], "int32"), "sli": ("sbuf", [128, 128], "int32"),
+    "slc": ("sbuf", [128, 128], "bfloat16"), "slb": ("sbuf", [128, 2048], "bfloat16"),
     "ones": ("sbuf", [128, 144], "bfloat16"), "blk0": ("sbuf", [128, 144], "bfloat16"), "blk": ("sbuf", [128, 144], "bfloat16"),
-    "qo": ("sbuf", [128, 144], "bfloat16"), "qn": ("sbuf", [128, 144], "bfloat16"), "q7": ("sbuf", [128, 144], "bfloat16"),
-    "qg": ("sbuf", [128, 144], "bfloat16"),
-    "wh": ("sbuf", [128, 128], "bfloat16"), "wl": ("sbuf", [128, 128], "bfloat16"),
-    "sm": ("sbuf", [128, 768], "float32"), "smi": ("sbuf", [128, 256], "int32"),
-    "rt": ("sbuf", [128, 16], "bfloat16"), "fo": ("sbuf", [128, 48], "uint16"), "so": ("sbuf", [128, 16], "uint16"),
-    "fy": ("sbuf", [128, NC], "bfloat16"), "xs": ("sbuf", [128, NC], "int32"), "xh": ("sbuf", [128, NC], "int32"),
-    "nx": ("sbuf", [128, NC], "int32"), "ycf": ("sbuf", [128, NC], "float32"),
-    "nw0": ("sbuf", [128, 4 * NC], "int32"), "nw1": ("sbuf", [128, 4 * NC], "int32"),
+    "qo": ("sbuf", [128, 144], "bfloat16"), "eye": ("sbuf", [128, 128], "bfloat16"), "swp": ("sbuf", [128, 128], "bfloat16"),
+    "shf": ("sbuf", [128, 240], "bfloat16"),
+    "c13": ("sbuf", [128, 128], "bfloat16"), "cp64": ("sbuf", [128, 128], "bfloat16"), "cm64": ("sbuf", [128, 128], "bfloat16"),
+    "ip": ("sbuf", [128, 80], "bfloat16"), "im": ("sbuf", [128, 80], "bfloat16"), "esl": ("sbuf", [128, 320], "bfloat16"),
+    "sm": ("sbuf", [128, 640], "float32"), "smi": ("sbuf", [128, 512], "int32"), "smb": ("sbuf", [128, 384], "bfloat16"),
+    "smu": ("sbuf", [128, 128], "uint16"),
 }
-for _k in range(NG):
-    SCRATCH["gb%d" % _k] = ("sbuf", [128, HN], "bfloat16")
-for _h in range(2):
-    for _k in ("ua", "ub", "uc", "ud"):
-        SCRATCH["%s%d" % (_k, _h)] = ("sbuf", [128, HC], "int32")
-for _k in range(8):
-    SCRATCH["p%d" % _k] = ("psum", [128, 512], "float32")
+for _x in "01":
+    SCRATCH["tab" + _x] = ("sbuf", [128, 2048], "bfloat16")
+    for _k in ("mx", "mn", "px", "pn"):
+        SCRATCH[_k + _x] = ("sbuf", [128, 3 * HN], "bfloat16")
+    SCRATCH["gb" + _x] = ("sbuf", [128, 6 * HN], "bfloat16")
+    SCRATCH["nw" + _x] = ("sbuf", [128, 3 * HC], "int32")
+    SCRATCH["ud" + _x] = ("sbuf", [128, 4 * HC], "int32")
+    SCRATCH["uc" + _x] = ("sbuf", [128, HC], "float32")
+    SCRATCH["fy" + _x] = ("sbuf", [128, 2 * HC], "bfloat16")
+    SCRATCH["xs" + _x] = ("sbuf", [128, 2 * HC], "int32")
+    SCRATCH["ycf" + _x] = ("sbuf", [128, HC], "float32")
+    SCRATCH["wh" + _x] = ("sbuf", [128, 128], "bfloat16")
+    SCRATCH["wl" + _x] = ("sbuf", [128, 128], "bfloat16")
+    SCRATCH["q7" + _x] = ("sbuf", [128, 144], "bfloat16")
+    for _k in "uzql":
+        SCRATCH["p" + _k + _x] = ("psum", [128, 512], "float32")
 
-DMAS = ["dch", "dwt", "dsl", "dx0", "dx1", "dc0", "dc1", "dc2", "dyx0", "dyx1", "dyc"]
+DMAS = ["dch0", "dch1", "dwt", "dsl", "dsb", "dx0", "dx1", "dc0", "dc1", "dyc0", "dyc1"]
 SEMAPHORES = ["qv", "qs", "qt", "qg", "loc"] + DMAS
-SEMAPHORES += ["l%d%d%d" % (t, k, h) for t in range(R) for k in range(3) for h in range(2)]
-SEMAPHORES += ["r%d%d" % (t, k) for t in range(R) for k in range(2)]
+SEMAPHORES += ["l%d%d%d" % (t, k, x) for t in range(R) for k in range(3) for x in range(2)]
+SEMAPHORES += ["r%d%d%d" % (t, k, x) for t in range(R) for k in range(2) for x in range(2)]
+
+PLAN = dict(cycle=0.83, gather=1.4, scatter=3.8, call=15, wake=130, message=3500, dma=3000, lead=10000, passes=4,
+            spiece=256, gpiece=1024)
+TURN = []
+TAG = [None]
 
 
 def rank_program(g, core, T, topo):
     rank = T.rank_of(core)
     if rank is None:
         return
-    A, F = AluOpType, ActivationFunctionType
+    A, F, P = AluOpType, ActivationFunctionType, PLAN
     N = len(T.cores)
     eng = {"v": g.vector, "s": g.scalar, "t": g.tensor, "g": g, "y": g.sync}
-    count = {"v": 0, "s": 0, "t": 0, "g": 0}
-    clock = {q: {} for q in eng}
-    acc = {}
-    nloc = [0]
+    prog, now = [], {"x": 1, "tag": ""}
 
-    def view(name, lo, hi, step=1, parts=None):
-        t = T[name]
-        if step == 1:
-            ap = t[:, lo:hi] if parts is None else t[0:parts, lo:hi]
-        else:
-            ap = t[:, lo:hi:step] if parts is None else t[0:parts, lo:hi:step]
-        return (ap, name, lo, hi)
+    def view(name, lo, hi, step=1, parts=128):
+        return (T[name][0:parts, lo:hi:step], name, lo, hi, (hi - lo + step - 1) // step)
 
     def sub(v, lo, n):
         return view(v[1], v[2] + lo, v[2] + lo + n)
@@ -64,110 +66,75 @@ def rank_program(g, core, T, topo):
     def ind(win, off):
         return (win[0].indirect(off[0]), win, off)
 
-    def learn(q, ck):
-        c = clock[q]
-        for s, v in ck.items():
-            if c.get(s, 0) < v:
-                c[s] = v
-
     def flat(vs):
         out = []
         for v in vs:
             out += [v[1], v[2]] if len(v) == 3 else [v]
         return out
 
-    def region(v):
-        if v[1][0] == "p" and len(v[1]) == 2:
-            return v[1], 0, 512, True
-        return v[1], v[2], v[3], False
+    def psum(v):
+        return SCRATCH[v[1]][0] == "psum"
 
-    def before(q, reads, writes):
-        need, cks = {}, []
-        for vs, w in ((reads, False), (writes, True)):
-            for v in flat(vs):
-                name, lo, hi, ps = region(v)
-                for a in acc.get(name, ()):
-                    if a[0] < hi and lo < a[1]:
-                        if ps and q == "t" and a[3] == "t":
-                            continue
-                        if w or a[2] or (ps and a[3] != q):
-                            need[a[4]] = max(need.get(a[4], 0), a[5])
-                            cks.append((a[4], a[6]))
-        for s in sorted(need):
-            if clock[q].get(s, 0) < need[s] and not any(o != s and ck.get(s, 0) >= need[s] for o, ck in cks):
-                eng[q].wait_ge(T.sem[s], need[s])
-                clock[q][s] = need[s]
-        for _, ck in cks:
-            learn(q, ck)
+    def add(q, kind, call, reads, writes, ns, lag=0.0, join=None):
+        prog.append(dict(q=q, kind=kind, call=call, reads=flat(reads), writes=flat(writes), ns=ns, lag=lag, join=join, x=now["x"],
+                         tag=now["tag"]))
 
-    def after(q, reads, writes, sem, val):
-        ck = dict(clock[q])
-        ck[sem] = val
-        for vs, w in ((reads, False), (writes, True)):
-            for v in flat(vs):
-                name, lo, hi, ps = region(v)
-                lst = acc.setdefault(name, [])
-                if w:
-                    lst[:] = [a for a in lst if not (lo <= a[0] and a[1] <= hi) or (ps and a[3] == q and not a[2])]
-                lst.append((lo, hi, w, q, sem, val, ck))
-
-    def op(q, call, reads, writes):
-        before(q, reads, writes)
-        ins = call()
-        count[q] += 1
-        ins.then_inc(T.sem["q" + q], 1)
-        after(q, reads, writes, "q" + q, count[q])
-
-    def dma(q, sem, out, in_, reads, writes):
-        before(q, reads, writes)
-        eng[q].dma_start(out, in_).then_inc(T.sem[sem], 16)
-        after(q, reads, writes, sem, 16)
+    def vec(call, out, ins, more=(), rate=None):
+        if len(ins[0]) == 3:
+            ns = 50 + out[4] * P["gather"] * P["cycle"]
+        else:
+            if rate is None:
+                rate = 0.5 if all(SCRATCH[v[1]][2] in ("bfloat16", "uint16") for v in [out] + ins) else 1
+            ns = P["call"] + max(64, rate * out[4]) * P["cycle"]
+        add("v", "op", call, ins + list(more), [out], ns)
 
     def cp(out, in_):
-        op("v", lambda: g.vector.tensor_copy(out[0], in_[0]), [in_], [out])
+        vec(lambda: g.vector.tensor_copy(out[0], in_[0]), out, [in_])
 
     def tt(out, a, b, o):
-        op("v", lambda: g.vector.tensor_tensor(out[0], a[0], b[0], o), [a, b], [out])
+        vec(lambda: g.vector.tensor_tensor(out[0], a[0], b[0], o), out, [a, b], rate=1 if len(a) == 3 or psum(a) or psum(b) else 2)
 
     def ts(out, a, s1, o1, s2=None, o2=None):
-        col = isinstance(s1, tuple)
-        rd = [a, s1] if col else [a]
-        x1 = s1[0] if col else s1
+        x1, x2 = (s[0] if isinstance(s, tuple) else s for s in (s1, s2))
+        more = [s for s in (s1, s2) if isinstance(s, tuple)]
         if o2 is None:
-            op("v", lambda: g.vector.tensor_scalar(out[0], a[0], x1, None, o1), rd, [out])
+            vec(lambda: g.vector.tensor_scalar(out[0], a[0], x1, None, o1), out, [a], more)
         else:
-            op("v", lambda: g.vector.tensor_scalar(out[0], a[0], x1, s2, o1, o2), rd, [out])
+            vec(lambda: g.vector.tensor_scalar(out[0], a[0], x1, x2, o1, o2), out, [a], more)
 
     def fill(out, c):
-        op("v", lambda: g.vector.memset(out[0], c), [], [out])
+        add("v", "op", lambda: g.vector.memset(out[0], c), [], [out], P["call"] + max(64, out[4] / 2) * P["cycle"])
 
-    def mms(out, pairs, start, stop):
+    def iota(out, pattern, base, mul):
+        add("g", "op", lambda: g.iota(out[0], pattern, base, mul), [], [out], 130 + 2 * out[4] * P["cycle"])
+
+    def select(out, in_, pattern, o, base, mul):
+        add("g", "op", lambda: g.affine_select(out[0], in_[0], pattern, o, 0.0, base, mul), [in_], [out], 170 + 2 * out[4] * P["cycle"])
+
+    def mms(out, pairs, start=True, stop=True):
         def call():
             ins = None
             for k, (l, r) in enumerate(pairs):
                 ins = g.tensor.matmul(out[0], l[0], r[0], start and k == 0, stop and k == len(pairs) - 1)
             return ins
-        rd = [l for l, _ in pairs] + [r for _, r in pairs]
-        op("t", call, rd, [out])
+        add("t", "op", call, [l for l, _ in pairs] + [r for _, r in pairs], [out], len(pairs) * max(64, out[4]) * P["cycle"])
+
+    def grouped(out, pairs, last):
+        mms(out, pairs[:-last], True, False)
+        mms(out, pairs[-last:], False, True)
+
+    def dma(q, sem, pairs, reads, writes):
+        add(q, "dma", (sem, pairs), reads, writes, 60 * len(pairs), P["dma"])
 
     def send(dst, src, land, sem):
-        before("g", [src], [])
-        d = T.cores[dst]
-        es = topo.engines(core, d)[:8]
-        rid, pid = topo.addr(d, core)
-        g.remote_dma(T[land][:, src[2]:src[3]], src[0], T.sem[sem], T.sem.loc, pid, rid, sum(1 << e for e in es))
-        nloc[0] += len(es)
+        add("g", "send", (dst, src, land, sem), [src], [view(land, src[2], src[3])], 300, P["message"])
 
-    def landed(src, land, lo, hi, sem):
-        n = len(topo.engines(T.cores[src], core)[:8])
-        acc.setdefault(land, []).append((lo, hi, True, "x", sem, n, {sem: n}))
-
-    cols, nxt = {}, {"sm": 0, "smi": 0}
+    cols, nxt = {}, {}
 
     def small(name, n, buf="sm"):
         if name not in cols:
-            cols[name] = (buf, nxt[buf])
-            nxt[buf] += n + (n & 1)
+            cols[name] = (buf, nxt.get(buf, 0))
+            nxt[buf] = nxt.get(buf, 0) + (n + 7) // 8 * 8
         b, o = cols[name]
         return view(b, o, o + n)
 
@@ -177,319 +144,416 @@ def rank_program(g, core, T, topo):
     def asker(t):
         return (rank - 1 - t % (N - 1)) % N
 
-    def lists(t, k, h=None, buf="outl"):
-        lo = (t * 3 + k) * NC
-        return view(buf, lo, lo + NC) if h is None else view(buf, lo + h * HC, lo + h * HC + HC)
+    def lists(t, k, x, buf="outl"):
+        lo = ((t * 3 + k) * 2 + x) * HC
+        return view(buf, lo, lo + HC)
 
-    def send_list(t, k, h=None):
-        send(partner(t), lists(t, k, h), "inl", "l%d%d%d" % (t, k, h or 0))
+    def spans(t, k, x, buf):
+        lo = (t * 2 + x) * 40
+        return view(buf, lo, lo + 24) if k == 0 else view(buf, lo + 24, lo + 40)
 
-    def send_spans(t, k):
-        lo = t * 48
-        send(asker(t), view("ro", lo, lo + 32) if k == 0 else view("ro", lo + 32, lo + 48), "rin", "r%d%d" % (t, k))
+    def send_list(t, k, x):
+        send(partner(t), lists(t, k, x), "inl", "l%d%d%d" % (t, k, x))
 
-    for t in range(R):
-        for k in range(3):
-            for h in ((None,) if k == 0 else (0, 1)):
-                v = lists(t, k, h, "inl")
-                landed(asker(t), "inl", v[2], v[3], "l%d%d%d" % (t, k, h or 0))
-        landed(partner(t), "rin", t * 48, t * 48 + 32, "r%d0" % t)
-        landed(partner(t), "rin", t * 48 + 32, t * 48 + 48, "r%d1" % t)
+    def names(x, slot):
+        return view("nw%d" % x, slot * HC, (slot + 1) * HC)
 
-    def names(t, slot, h=None):
-        b, lo = "nw%d" % (t % 2), slot * NC
-        return view(b, lo, lo + NC) if h is None else view(b, lo + h * HC, lo + h * HC + HC)
+    def table(x):
+        return view("tab%d" % x, 0, 2048)
 
-    dma("y", "dch", T.chi[:], T.ch[:], [], [view("chi", 0, NC)])
-    dma("s", "dx0", T.tab0[:], T.xt[:], [], [view("tab0", 0, 2048)])
-    dma("y", "dwt", T.wti[:], T.wt[:], [], [view("wti", 0, 1)])
-    dma("y", "dsl", T.sli[0:8, :], T.sl[:], [], [view("sli", 0, 2048)])
-    fill(view("ones", 0, 144), 1.0)
-    fill(view("mkx", 0, HN), 1.0)
-    fill(view("mkn", 0, HN), 0.0)
+    for x in range(2):
+        now["x"] = x
+        dma("y", "dch%d" % x, [(T["nw%d" % x][64 * h:64 * h + 64, 0:HC], T.ch[64 * x:64 * x + 64, h * HC:(h + 1) * HC]) for h in range(2)],
+            [], [names(x, 0)])
+        dma("sy"[x], "dx%d" % x, [(T["tab%d" % x][64 * h:64 * h + 64, :], T.xt[64 * x:64 * x + 64, :]) for h in range(2)], [], [table(x)])
+        cp(lists(0, 0, x), names(x, 0))
+        send_list(0, 0, x)
+    now["x"] = 0
+    dma("y", "dwt", [(T.wti[64 * h:64 * h + 64, z:z + 1], T.wt[64 * z:64 * z + 64, :]) for z in range(2) for h in range(2)],
+        [], [view("wti", 0, 2)])
+    dma("s", "dsl", [(T.sli[:], T.sl[:])], [], [view("sli", 0, 128)])
+    cp(view("slc", 0, 128), view("sli", 0, 128))
+    dma("y", "dsb", [(T.slb[0:8, :], T.slc[:])], [view("slc", 0, 128)], [view("slb", 0, 2048)])
+
+    ones, blk, qo, eye = view("ones", 0, 144), view("blk", 0, 144), view("qo", 0, 144), view("eye", 0, 128)
+    mkx, mkn = view("mkx", 0, HN), view("mkn", 0, HN)
+    fill(ones, 1.0)
+    fill(mkx, 1.0)
     fill(view("mkx", 0, HN, 16), 0.0)
-    fill(view("mkn", 0, HN, 16), 512.0)
-    cp(lists(0, 0), view("chi", 0, NC))
-    cp(names(0, 0), view("chi", 0, NC))
+    add("s", "op", lambda: g.scalar.activation(mkn[0], mkx[0], F.Identity, 512.0, -512.0), [mkx], [mkn], HN * P["cycle"])
+    for name, n, c in (("c13", 128, 2.0 ** -13), ("cp64", 128, 64.0), ("cm64", 128, -64.0), ("shf", 240, 0.0), ("esl", 320, 0.0),
+                       ("ro", R * 80, 0.0)):
+        fill(view(name, 0, n), c)
+    pidx, i16, ib, ic, ie = (small(n, w, "smi") for n, w in (("pidx", 8), ("i16", 16), ("ib", 80), ("ic", 64), ("ie", 64)))
+    iota(pidx, [[0, 8]], 0, 1)
+    select(view("blk0", 0, 144), ones, [[-16, 9], [0, 16]], A.is_ge, 0, 1)
+    select(blk, view("blk0", 0, 144), [[16, 9], [0, 16]], A.is_ge, 15, -1)
+    iota(ib, [[0, 10], [-16, 8]], 0, 1)
+    iota(i16, [[1, 16]], 0, 0)
+    iota(ic, [[-16, 8], [0, 8]], 0, 1)
+    iota(ie, [[0, 8], [-100, 2], [-1, 4]], 0, 1)
+    select(eye, sub(ones, 0, 128), [[-1, 128]], A.is_equal, 0, 1)
+    select(qo, blk, [[0, 9], [1, 16]], A.is_equal, -15, 0)
 
-    pidx, ic, pm = small("pidx", 8, "smi"), small("ic", 8, "smi"), small("pm", 16, "smi")
-    ones, blk = view("ones", 0, 144), view("blk", 0, 144)
-    op("g", lambda: g.affine_select(T.blk0[:], T.ones[:], [[-16, 9], [0, 16]], A.is_ge, 0.0, 0, 1), [ones], [view("blk0", 0, 144)])
-    op("g", lambda: g.affine_select(T.blk[:], T.blk0[:], [[16, 9], [0, 16]], A.is_ge, 0.0, 15, -1), [view("blk0", 0, 144)], [blk])
-    op("g", lambda: g.affine_select(T.qo[:], T.blk[:], [[0, 9], [1, 16]], A.is_equal, 0.0, -15, 0), [blk], [view("qo", 0, 144)])
-    op("g", lambda: g.iota(pidx[0], [[0, 8]], 0, 1), [], [pidx])
-    op("g", lambda: g.iota(ic[0], [[16, 8]], 0, 0), [], [ic])
-    op("g", lambda: g.affine_select(T.qg[:], T.ones[:], [[1, 144]], A.is_equal, 0.0, -15, -16), [ones], [view("qg", 0, 144)])
-    send_list(0, 0)
+    wti = view("wti", 0, 2)
+    wa, wb, wc, wd = (small(n, 2, "smi") for n in ("wa", "wb", "wc", "wd"))
+    fa, fb, fd = (small(n, 2) for n in ("fa", "fb", "fd"))
+    pm, k6, k7, p8 = small("pm", 8, "smi"), small("k6", 1, "smi"), small("k7", 1, "smi"), small("p8", 4, "smi")
+    kc, c01, pf, ph, il = small("kc", 2), small("c01", 2), small("pf", 1), small("ph", 1), small("il", 8)
+    mask, thr, iv = small("mask", 64), small("thr", 64), small("iv", 8)
+    at16, ivb, xo = small("at16", 8, "smb"), small("ivb", 8, "smb"), small("xo", 4, "smu")
+    ts(pm, pidx, 15, A.bitwise_and)
+    ts(p8, sub(pidx, 0, 4), 7, A.bitwise_and)
+    ts(ph, sub(pidx, 0, 1), 64.0, A.is_ge, 1024.0, A.mult)
+    ts(k6, sub(pm, 0, 1), 613.0, A.mult)
+    cp(pf, sub(pm, 0, 1))
+    cp(xo, p8)
+    ts(k7, k6, 2047, A.bitwise_and)
+    for j in range(2):
+        ts(sub(c01, j, 1), k7, 77.0 * j, A.add, 64.0, A.mult)
+    ts(kc, c01, 992.0, A.add)
+    for o, m in ((wb, 1984), (wc, 2048), (wa, 63), (wd, 7)):
+        ts(o, wti, m, A.bitwise_and)
+    tt(fb, wb, wc, A.subtract)
+    cp(fa, wa)
+    cp(fd, wd)
+    ts(ib, ib, 4, A.arith_shift_right)
+    ts(ic, ic, 4, A.arith_shift_right)
+    ts(il, sub(i16, 0, 8), 16.0, A.mult, pf, A.add)
+    ts(view("shf", 112, 128), i16, pf, A.is_equal, 4096.0, A.mult)
+    for name, s in (("ip", 1.0), ("im", -1.0)):
+        ts(view(name, 0, 16), sub(ib, 0, 16), 0.0, A.is_equal, 2.0 * s, A.mult)
+        ts(view(name, 16, 80), sub(ib, 16, 64), 0.0, A.is_equal, s, A.mult)
+    ts(mask, ic, 0.0, A.is_equal)
+    ts(thr, ic, 0.0, A.not_equal, -BIG, A.mult)
+    ts(at16, il, 16.0, A.mult)
+    ts(iv if MODE == "dma" else ivb, il, 8.0, A.mult, ph, A.add)
+    for x in range(2):
+        ts(view("wh%d" % x, 0, 128), sub(blk, 0, 128), sub(fb, x, 1), A.mult, 2.0 ** -12, A.mult)
+        ts(view("wl%d" % x, 0, 128), sub(blk, 0, 128), sub(fa, x, 1), A.mult, 2.0 ** -12, A.mult)
+        ts(view("q7%d" % x, 0, 144), qo, sub(fd, x, 1), A.mult)
+        cp(view("swp", 64 * x, 64 * x + 64), sub(eye, 64 - 64 * x, 64))
+        for h in range(2):
+            ts(view("esl", (2 * x + h) * 80 + 16, (2 * x + h) * 80 + 80), ie, 4.0 * x - 100.0 * h, A.is_equal, -1.0, A.mult)
 
-    wti = view("wti", 0, 1)
-    for mask, col, src, dst, n in ((4032, "fa", "blk", "wh", 128), (63, "fb", "blk", "wl", 128), (7, "fc", "qo", "q7", 144)):
-        i = small(col + "i", 1, "smi")
-        f = small(col, 1)
-        ts(i, wti, mask, A.bitwise_and)
-        cp(f, i)
-        ts(view(dst, 0, n), view(src, 0, n), f, A.mult)
-    ts(view("qn", 0, 144), view("qo", 0, 144), -1.0, A.mult)
-    ts(sub(pm, 0, 8), pidx, 15, A.bitwise_and)
-    ib, cb, base, d2, tmp, fl = (small(n, 48) for n in ("ib", "cb", "base", "d2", "tmp", "fl"))
-    inn, iv, inq = sub(ib, 0, 16), small("iv", 16), small("inq", 16)
-    tt(sub(inn, 0, 8), sub(pm, 0, 8), ic, A.add)
-    ts(sub(inn, 8, 8), sub(inn, 0, 8), float(HC), A.add)
-    ts(sub(ib, 16, 16), inn, 16.0, A.mult, 15.0, A.add)
-    ts(sub(cb, 16, 16), inn, 16.0, A.mult, 15.0 + 4 * HN, A.add)
-    ts(iv, inn, 8.0, A.mult)
-    ts(inq, inn, 3.0 * NC, A.add, 1.0 / NC, A.mult)
-    k6, k613, c0 = small("k6", 2, "smi"), small("k613", 1), small("c0", 1)
-    ts(sub(k6, 0, 1), sub(pm, 0, 1), 613.0, A.mult)
-    ts(sub(k6, 1, 1), sub(k6, 0, 1), 2047, A.bitwise_and)
-    cp(k613, sub(k6, 1, 1))
-    cp(c0, sub(k6, 1, 1))
-    for t in range(2):
-        fill(names(t, 2), 0)
+    def look(t, x, kind):
+        k, own = int(kind[1]), kind[0] == "L"
+        at, off = KINDS.index(kind) * HN, lists(t, k, x, "outl" if own else "inl")
 
-    op("v", lambda: g.vector.tensor_copy(T.slb[0:8, :], T.sli[0:8, :]), [view("sli", 0, 2048)], [view("slb", 0, 2048)])
-    mms(view("p7", 0, 128), [(view("qg", 15 - j, 143 - j, 1, 8), view("slb", j, 2048, 16, 8)) for j in range(16)], True, True)
+        def gather(lo, n):
+            src, dst = ind(table(x), sub(off, lo // 16, n // 16)), view("gb%d" % x, at + lo, at + lo + n)
+            return lambda: g.scalar.activation(dst[0], src[0], F.Copy), [src], [dst], 65 + n * P["gather"] * P["cycle"]
 
-    ring, where = [0], {}
+        def scan(least):
+            o0, o1 = (A.max, A.min) if least else (A.mult, A.max)
 
-    def gather(key, t, off, chunks=1):
-        b = "gb%d" % (ring[0] % NG)
-        ring[0] += 1
-        w = HC // chunks
-        for c in range(chunks):
-            src = ind(view("tab%d" % (t % 2), 0, 2048), sub(off, c * w, w))
-            dst = view(b, c * w * 16, (c + 1) * w * 16)
-            op("s", lambda: g.scalar.activation(dst[0], src[0], F.Copy), [src], [dst])
-        where[key] = (b, chunks)
+            def make(lo, n):
+                d0, d1 = view("mkn" if least else "mkx", 0, n), view("gb%d" % x, at + lo, at + lo + n)
+                o = view(("m" if own else "p") + ("n%d" if least else "x%d") % x, k * HN + lo, k * HN + lo + n)
+                return lambda: g.vector.tensor_tensor_scan(o[0], d0[0], d1[0], 0.0, o0, o1), [d0, d1], [o], P["call"] + n / 2 * P["cycle"]
+            return make
+        for q, make, n in (("s", gather, P["gpiece"]), ("v", scan(False), P["spiece"]), ("v", scan(True), P["spiece"])):
+            for lo in range(0, HN, n):
+                add(q, "op", *make(lo, n), join=(make, lo, n))
 
-    def scan(key, out, least, chunks=None):
-        b, n = where[key]
-        w = HN // n
-        o0, o1 = (A.max, A.min) if least else (A.mult, A.max)
-        for c in (range(n) if chunks is None else chunks):
-            d0, d1 = view("mkn" if least else "mkx", 0, w), view(b, c * w, (c + 1) * w)
-            o = view(out[0], out[1] + c * w, out[1] + (c + 1) * w)
-            op("v", lambda: g.vector.tensor_tensor_scan(o[0], d0[0], d1[0], 0.0, o0, o1), [d0, d1], [o])
+    def res(buf, x, k):
+        return view("%s%d" % (buf, x), k * HN + 15, (k + 1) * HN, 16)
 
-    def own(slot, h=0):
-        return ("mxw", (slot * 2 + h) * HN)
+    def span(side, x, k, sign, lo, hi):
+        p, m = view("ip", lo, hi), view("im", lo, hi)
+        return [(res(side + "x", x, k), p if sign > 0 else m), (res(side + "n", x, k), m if sign > 0 else p)]
 
-    def own_min(h=0):
-        return ("mno", h * HN)
+    def slack(t, j, x, lo, hi):
+        o = (t * 2 + j) * 2 * HC
+        return [(view("slb", o + h * HC, o + (h + 1) * HC, 1, 8), view("esl", (2 * x + h) * 80 + lo, (2 * x + h) * 80 + hi, 1, 8))
+                for h in range(2)]
 
-    def urep(h, slot):
-        b, o = own(slot, h)
-        y = view(b, o + 15, o + HN, 16)
-        mms(view("p%d" % h, 0, HC), [(view("wh", 0, 128), y), (view("wl", 0, 128), y)], True, True)
+    def to_list(x, col, r):
+        out = view("pl%d" % x, col, col + 8)
+        grouped(out, [(eye, at16)] + [(view("shf", 112 - 16 * b, 240 - 16 * b), view(r[1], r[2] + b, r[3], 8)) for b in range(8)], 8)
+        return out
 
-    def tolist(bank, col, q, src, n, start, stop):
-        b, o = src
-        mms(view(bank, col, col + 8 * n),
-            [(view(q, 15 - j, 143 - j), view(b, o + 16 * j + 15, o + n * HN, 256)) for j in range(16)], start, stop)
+    def product(x, k, out):
+        y, v, hi, uc = res("mx", x, k), view("pu%d" % x, 0, HC), view("ud%d" % x, HC, 2 * HC), view("uc%d" % x, 0, HC)
+        grouped(v, [(view("c13", 0, 128), sub(ones, 0, HC)), (view("wh%d" % x, 0, 128), y), (view("wl%d" % x, 0, 128), y)], 2)
+        ts(hi, v, 2.0 ** -13 - 0.5 - 1.0 / 64, A.add)
+        tt(v, v, hi, A.subtract)
+        tt(uc, v, names(x, k), A.mult)
+        ts(out, uc, 4096.0, A.mult, sub(c01, k, 1), A.add)
 
-    def span_max(bank, col, src, n):
-        tolist(bank, col, "qo", src, n, True, False)
+    def kappa():
+        kv, kr = small("kv", 16), small("kr", 1)
+        d0, d1 = sub(ones, 0, 16), view("pq0", 64, 80)
+        vec(lambda: g.vector.tensor_tensor_scan(kv[0], d0[0], d1[0], -992.0, A.mult, A.add), kv, [d0, d1])
+        ts(kr, sub(kv, 15, 1), 1.5 * 2.0 ** 34, A.add, -1.5 * 2.0 ** 34, A.add)
+        ts(c01, kc, sub(kv, 15, 1), A.add, kr, A.subtract)
 
-    def span_min(bank, col, src, n):
-        tolist(bank, col, "qn", src, n, False, True)
+    def stream(t, x):
+        def sv(name, n, buf="sm"):
+            return small("%s%d" % (name, x), n, buf)
 
-    def low3(slot):
-        tolist("p7", slot * 16, "q7", own(slot), 2, True, True)
-
-    def ptab(k, least):
-        return ("pmn" if least else "pmx", (k % 2) * 2 * HN)
-
-    def pscan(k, h, least):
-        b, o = ptab(k, least)
-        scan("P%d%d" % (k, h), (b, o + h * HN), least)
-
-    def proposal(t, h, slot):
-        ua, ub, uc, ud = (view("%s%d" % (k, h), 0, HC) for k in ("ua", "ub", "uc", "ud"))
-        cp(ua, view("p%d" % h, 0, HC))
-        ts(ub, ua, 4095, A.bitwise_and)
-        tt(uc, ub, names(t, slot, h), A.mult)
-        tt(ud, uc, view("p2", h * HC, (h + 1) * HC), A.add)
-        ts(names(t, slot + 1, h), ud, 6, A.arith_shift_right, 2047, A.bitwise_and)
-
-    es, en, ths, h0, de, dq, z, d0, e0, esa, th1, q1, w1, thb, hq, m2, h1, eq, du = (
-        small(n, 16) for n in ("es", "en", "ths", "h0", "de", "dq", "z", "d0", "e0", "esa", "th1", "q1", "w1", "thb", "hq", "m2", "h1",
-                               "eq", "du"))
-    ui, u7 = small("ui", 48, "smi"), small("u7", 48, "smi")
-    kn, ki, kk = small("kn", 1), small("ki", 1, "smi"), small("kk", 1, "smi")
-
-    def slack(t, j):
-        return view("al", (t * 2 + j) * 16, (t * 2 + j) * 16 + 16)
-
-    def second(t, h):
-        h8, q8, so = sub(h0, 8 * h, 8), sub(hq, 8 * h, 8), view("so", 8 * h, 8 * h + 8)
-        tt(h8, view("p3", 8 * h, 8 * h + 8), sub(ths, 8 * h, 8), A.is_le)
-        tt(q8, sub(inq, 8 * h, 8), h8, A.subtract)
-        ts(so, q8, float(NC), A.mult)
-        cp(lists(t, 2, h), ind(view("nw%d" % (t % 2), 0, 4 * NC), so))
-        send_list(t, 2, h)
+        def tag(w):
+            now["tag"] = "%d%s.%s" % (t, "AB"[x], w)
+        z, ud = "pz%d" % x, "ud%d" % x
+        tag("L0")
+        look(t, x, "L0")
+        tag("first")
+        u0 = view(ud, 3 * HC, 4 * HC)
+        product(x, 0, u0)
+        ts(names(x, 1), u0, 6, A.arith_shift_right, 2047, A.bitwise_and)
+        cp(lists(t, 1, x), names(x, 1))
+        send_list(t, 1, x)
+        ts(view(ud, 0, HC), u0, 77.0 * 64, A.add)
+        tag("L1")
+        look(t, x, "L1")
+        tag("second")
+        product(x, 1, view(ud, 2 * HC, 3 * HC))
+        grouped(view(z, 0, 80), slack(t, 0, x, 0, 80) + span("m", x, 0, -1, 0, 80) + span("m", x, 1, 1, 0, 80), 1)
+        r, so = sv("rb", 64, "smb"), sv("so", 8, "smu")
+        tt(r, view(z, 16, 80), thr, A.is_le)
+        ts(so, to_list(x, 0, r), 1.0 / 16, A.mult)
+        ts(names(x, 2), ind(view(ud, 0, 3 * HC), so), 6, A.arith_shift_right, 2047, A.bitwise_and)
+        cp(lists(t, 2, x), names(x, 2))
+        send_list(t, 2, x)
+        for kind in ("P0", "P1", "P2"):
+            tag(kind)
+            look(t, x, kind)
+        tag("answer")
+        for k, out, pairs in ((0, view("pq%d" % x, 0, 24), span("p", x, 0, 1, 8, 32) + span("p", x, 1, -1, 8, 32)),
+                              (1, view("pq%d" % x, 32, 40), span("p", x, 0, 1, 16, 24) + span("p", x, 2, -1, 16, 24))):
+            v = spans(t, k, x, "ro")
+            grouped(out, pairs, 1)
+            cp(sub(v, 8 * k, out[4]), out)
+            send(asker(t), v, "rin", "r%d%d%d" % (t, k, x))
+        tag("L2")
+        look(t, x, "L2")
+        tag("truth")
+        hh, dh, e, x12, w12, hd, m, sel = (sv(n, 16, "smb" if n == "e" else "sm") for n in ("hh", "dh", "e", "x12", "w12", "hd", "m", "sel"))
+        ts(hh, view(z, 32, 48), 0.0, A.is_le, 0.5, A.mult)
+        tt(view(z, 8, 32), view(z, 8, 32), spans(t, 0, x, "rin"), A.subtract)
+        ts(dh, view(z, 16, 32), 0.0, A.is_le, 0.5, A.mult)
+        tt(x12, view(z, 0, 16), hh, A.mult)
+        tt(e, hh, dh, A.is_equal)
+        tag("decide")
+        rz = view("pu%d" % x, 128, 144)
+        grouped(rz, slack(t, 1, x, 16, 32) + span("m", x, 0, -1, 16, 32) + span("m", x, 2, 1, 16, 32), 1)
+        tt(w12, rz, x12, A.subtract)
+        tt(hd, w12, spans(t, 1, x, "rin"), A.is_le)
+        tt(m, hd, e, A.mult)
+        tt(sub(sel, 0, 8), sub(m, 8, 8), sub(dh, 0, 8), A.max)
+        tt(r, ind(sub(sel, 0, 8), xo), mask, A.mult)
+        at = to_list(x, 8, r)
+        if t < R - 1:
+            ne = sv("ne", 8, "smb")
+            tt(ne, sub(m, 0, 8), sub(m, 8, 8), A.not_equal)
+            mms(view("pq0", 64 + 8 * x, 72 + 8 * x), [(view("cm64", 0, 128), sub(e, 0, 8)), (view("cp64", 0, 128), ne)])
+        tag("pick")
+        fo, no, fy = sv("fo", 8, "smu"), sv("no", 8, "smu"), view("fy%d" % x, 0, HC)
+        ts(fo, at, 15.0, A.add)
+        cp(fy, ind(view("mx%d" % x, 0, 3 * HN), fo))
+        mms(view("pl%d" % x, 16, 24), [(view("q7%d" % x, 15 - j, 143 - j), view(fy[1], j, HC, 16)) for j in range(16)])
+        ts(no, fo, 15.0, A.subtract, 1.0 / 16, A.mult)
+        picked = ind(view("nw%d" % x, 0, 3 * HC), no)
+        if t < R - 1:
+            cp(lists(t + 1, 0, x), picked)
+            send_list(t + 1, 0, x)
+            cp(names(x, 0), lists(t + 1, 0, x))
+        else:
+            y = view("ycf%d" % x, 0, HC)
+            cp(y, picked)
+            dma("y", "dyc%d" % x, [(T.yc[64 * x:64 * x + 64, h * HC:(h + 1) * HC], T[y[1]][64 * h:64 * h + 64, :]) for h in range(2)], [y], [])
+        tag("update")
+        ui, u7, tab = sv("ui", 8, "smi"), sv("u7", 8, "smi"), table(x)
+        cp(ui, view("pl%d" % x, 16, 24))
+        ts(u7, ui, 7, A.bitwise_and)
+        tb = T[tab[1]]
+        fresh = [tb[64 * h:64 * h + 64, 1024 * h:1024 * (h + 1)] for h in range(2)]
+        if MODE == "dual":
+            n = 2 if t < R - 1 else 1
+            ub, vo, old, xh = sv("ub", 8, "smb"), sub(sv("vo", 16, "smu"), 0, 8 * n), view(fy[1], HC, 2 * HC), view("xs%d" % x, 0, n * HC)
+            turn = [eye, view("swp", 0, 128)]
+            cp(ub, u7)
+            for h in range(n):
+                grouped(view("pl%d" % x, 32 + 8 * h, 40 + 8 * h), [(turn[h], ivb), (turn[h], ub)], 1)
+            cp(vo, view("pl%d" % x, 32, 32 + 8 * n))
+            cp(old, ind(tab, sub(vo, 0, 8)))
+            for h in range(n):
+                grouped(view(z, 128 + h * HC, 128 + (h + 1) * HC), [(turn[h], fy), (turn[h], old)], 1)
+            ts(xh, view(z, 128, 128 + n * HC), 0.5, A.mult, -0.25, A.add)
+        else:
+            vf, vo, xs, xh = sv("vf", 8), sv("vo", 8, "smu"), view("xs%d" % x, 0, HC), view("xs%d" % x, HC, 2 * HC)
+            tt(vf, u7, iv, A.add)
+            cp(vo, vf)
+            tt(xs, ind(tab, vo), fy, A.add)
+            ts(xh, xs, 1, A.arith_shift_right)
+        out = ind(tab, vo)
+        add("v", "op", lambda: g.vector.tensor_copy(out[0], xh[0]), [xh, vo], [tab], 50 + xh[4] * P["scatter"] * P["cycle"])
+        if t == R - 1:
+            dma("y", "dc%d" % x, [(T.yx[64 * x:64 * x + 64, 1024 * h:1024 * (h + 1)], fresh[h]) for h in range(2)], [tab], [])
+        elif MODE == "dma":
+            dma("y", "dc%d" % x, [(tb[64 * (1 - h):64 * (1 - h) + 64, 1024 * h:1024 * (h + 1)], fresh[h]) for h in range(2)], [], [tab])
 
     for t in range(R):
-        cur, new = "tab%d" % (t % 2), "tab%d" % ((t + 1) % 2)
-        gather("L00", t, lists(t, 0, 0), 2)
-        gather("L01", t, lists(t, 0, 1))
         if t:
-            cp(names(t, 0), lists(t, 0))
-            op("v", lambda: g.vector.tensor_reduce(kn[0], T.p7[:, 64:80], AxisListType.X, A.add), [view("p7", 64, 80)], [kn])
-            ts(ki, kn, -1.0, A.mult, float(8 * NC), A.add)
-            ts(kk, ki, 31, A.bitwise_and)
-            tt(c0, k613, kk, A.add)
-        ts(view("p2", 0, NC), names(t, 0), c0, A.add, 64.0, A.mult)
-        scan("L00", own(0, 0), False, [0])
-        scan("L00", own_min(0), True, [0])
-        scan("L00", own(0, 0), False, [1])
-        urep(0, 0)
-        scan("L00", own_min(0), True, [1])
-        proposal(t, 0, 0)
-        cp(lists(t, 1, 0), names(t, 1, 0))
-        send_list(t, 1, 0)
-        gather("P00", t, lists(t, 0, 0, "inl"))
-        gather("L10", t, lists(t, 1, 0))
-        scan("L01", own(0, 1), False)
-        urep(1, 0)
-        span_max("p4", 0, own(0), 2)
-        scan("L01", own_min(1), True)
-        span_min("p4", 0, own_min(), 2)
-        proposal(t, 1, 0)
-        cp(lists(t, 1, 1), names(t, 1, 1))
-        send_list(t, 1, 1)
-        if t == 0:
-            dma("y", "dx1", T[new][:], T.xt[:], [names(t, 1, 1)], [view(new, 0, 2048)])
-            cp(view("al", 0, 128), view("p7", 0, 128))
-        else:
-            dma("y", "dc%d" % (t - 1), T[new][:], T[cur][:], [view(cur, 0, 2048), names(t, 1, 1)], [view(new, 0, 2048)])
-        gather("L11", t, lists(t, 1, 1))
-        gather("P01", t, lists(t, 0, 1, "inl"))
-        nx = view("nx", 0, NC)
-        ts(nx, names(t, 1), 77.0, A.add)
-        ts(names(t, 3), nx, 2047, A.bitwise_and)
-        ts(view("p2", 0, NC), nx, c0, A.add, 64.0, A.mult)
-        pscan(0, 0, False)
-        pscan(0, 0, True)
-        cp(es, view("p4", 0, 16))
-        tt(ths, es, slack(t, 0), A.add)
-        low3(0)
-        for h in range(2):
-            k = "L1%d" % h
-            if h == 0:
-                scan(k, own(1, h), False)
-            urep(h, 1)
-            span_max("p3", 8 * h, own(1, h), 1)
-            scan(k, own_min(h), True)
-            span_min("p3", 8 * h, own_min(h), 1)
-            proposal(t, h, 1)
-            if h == 0:
-                scan("L11", own(1, 1), False)
-            else:
-                pscan(0, 1, False)
-            second(t, h)
-            gather("P1%d" % h, t, lists(t, 1, h, "inl"))
-        low3(1)
-        span_max("p6", 0, ptab(0, False), 2)
-        pscan(0, 1, True)
-        span_min("p6", 0, ptab(0, True), 2)
-        pscan(1, 0, False)
-        pscan(1, 0, True)
-        gather("P20", t, lists(t, 2, 0, "inl"))
-        gather("P21", t, lists(t, 2, 1, "inl"))
-        tt(de, view("p3", 0, 16), es, A.subtract)
-        tt(esa, es, slack(t, 1), A.add)
-        tt(q1, h0, de, A.mult)
-        tt(th1, esa, q1, A.add)
-        cp(sub(ui, 0, 32), view("p7", 0, 32))
-        ts(sub(u7, 0, 32), sub(ui, 0, 32), 7, A.bitwise_and)
-        tt(du, sub(u7, 16, 16), sub(u7, 0, 16), A.subtract)
-        if t == R - 1:
-            ts(sub(iv, 8, 8), sub(iv, 8, 8), -1024.0, A.add)
-        tt(sub(ib, 32, 16), iv, sub(u7, 0, 16), A.add)
-        ts(sub(cb, 0, 16), hq, float(NC), A.mult)
-        pscan(1, 1, False)
-        span_max("p6", 16, ptab(1, False), 2)
-        pscan(1, 1, True)
-        span_min("p6", 16, ptab(1, True), 2)
-        gather("L20", t, lists(t, 2, 0), 2)
-        gather("L21", t, lists(t, 2, 1), 2)
-        pscan(2, 0, False)
-        cp(view("ro", t * 48, t * 48 + 32), view("p6", 0, 32))
-        send_spans(t, 0)
-        pscan(2, 0, True)
-        pscan(2, 1, False)
-        span_max("p6", 32, ptab(2, False), 2)
-        pscan(2, 1, True)
-        span_min("p6", 32, ptab(2, True), 2)
-        scan("L20", own(2, 0), False)
-        span_max("p5", 0, own(2, 0), 1)
-        cp(view("ro", t * 48 + 32, t * 48 + 48), view("p6", 32, 48))
-        send_spans(t, 1)
-        scan("L20", own_min(0), True)
-        span_min("p5", 0, own_min(0), 1)
-        scan("L21", own(2, 1), False)
-        low3(2)
-        scan("L21", own(3), True)
-        tolist("p5", 8, "qo", own(2, 1), 2, True, True)
-        qs, qn, qx = (view("rin", t * 48 + 16 * k, t * 48 + 16 * k + 16) for k in range(3))
-        tt(dq, qn, qs, A.subtract)
-        tt(z, de, dq, A.add)
-        tt(d0, z, slack(t, 0), A.is_le)
-        tt(w1, esa, qs, A.add)
-        tt(q1, h0, z, A.mult)
-        tt(e0, h0, d0, A.is_equal)
-        ts(sub(tmp, 0, 16), d0, float(NC), A.mult)
-        ts(sub(tmp, 16, 16), d0, float(2 * HN), A.mult)
-        tt(sub(tmp, 32, 16), d0, du, A.mult)
-        tt(w1, w1, q1, A.add)
-        ts(thb, e0, 65536.0, A.mult, -65536.0, A.add)
-        tt(base, tmp, ib, A.add)
-        tt(w1, w1, thb, A.add)
-        tt(sub(d2, 0, 32), sub(cb, 0, 32), sub(base, 0, 32), A.subtract)
-        cp(sub(ui, 32, 16), view("p7", 32, 48))
-        ts(sub(u7, 32, 16), sub(ui, 32, 16), 7, A.bitwise_and)
-        tt(sub(cb, 32, 16), iv, sub(u7, 32, 16), A.add)
-        tt(sub(d2, 32, 16), sub(cb, 32, 16), sub(base, 32, 16), A.subtract)
-        tt(thb, w1, qx, A.subtract)
-        tt(sub(m2, 0, 8), view("p5", 0, 8), sub(thb, 0, 8), A.is_le)
-        tt(sub(z, 0, 8), view("p5", 8, 16), sub(thb, 8, 8), A.subtract)
-        tt(sub(m2, 8, 8), view("p5", 16, 24), sub(z, 0, 8), A.is_ge)
-        for k in range(3):
-            tt(sub(tmp, 16 * k, 16), m2, sub(d2, 16 * k, 16), A.mult)
-        tt(fl, tmp, base, A.add)
-        cp(view("fo", 0, 48), fl)
-        fy, xs, xh = view("fy", 0, NC), view("xs", 0, NC), view("xh", 0, NC)
-        src = ind(view("mxw", 0, 6 * HN), view("fo", 16, 32))
-        op("s", lambda: g.scalar.activation(fy[0], src[0], F.Copy), [src], [fy])
-        picked = ind(view("nw%d" % (t % 2), 0, 4 * NC), view("fo", 0, 16))
-        vo = view("fo", 32, 48)
-        if t < R - 1:
-            cp(lists(t + 1, 0), picked)
-            send_list(t + 1, 0)
-        else:
-            cp(view("ycf", 0, NC), picked)
-            dma("y", "dyc", T.yc[:], T.ycf[:], [view("ycf", 0, NC)], [])
-        parts = [(0, 1)] if t < R - 1 else [(0, 2), (1, 2)]
-        for i, n in parts:
-            w = NC // n
-            xi, hi, oi = sub(xs, i * w, w), sub(xh, i * w, w), sub(vo, i * w // 16, w // 16)
-            tt(xi, ind(view(cur, i * 8 * w, (i + 1) * 8 * w), oi), sub(fy, i * w, w), A.add)
-            ts(hi, xi, 1, A.arith_shift_right)
-            col = view(new, i * 8 * w, (i + 1) * 8 * w)
-            out = ind(col, oi)
-            op("v", lambda: g.vector.tensor_copy(out[0], hi[0]), [hi, oi], [col])
-            if n == 2:
-                dma("ys"[i], "dyx%d" % i, T.yx[:, col[2]:col[3]], col[0], [col], [])
-        if t < R - 1:
-            tt(sub(h1, 0, 8), view("p5", 0, 8), sub(th1, 0, 8), A.is_le)
-            tt(sub(z, 8, 8), view("p5", 8, 16), sub(th1, 8, 8), A.subtract)
-            tt(sub(h1, 8, 8), view("p5", 16, 24), sub(z, 8, 8), A.is_ge)
-            tt(eq, h1, m2, A.is_equal)
-            tt(view("rt", 0, 16), eq, e0, A.mult)
-            mms(view("p7", 64, 80), [(view("ones", 0, 128), view("rt", 0, 16))], True, True)
+            now["x"], now["tag"] = 0, "%dkappa" % t
+            kappa()
+        for x in range(2):
+            now["x"] = x
+            stream(t, x)
 
-    for q in "vstg":
+    issue(g, T, topo, core, eng, plan(prog), {"inl": asker, "rin": partner})
+
+
+def plan(prog):
+    P, n = PLAN, len(prog)
+    pred, acc, last = [set() for _ in prog], {}, {}
+    for i, o in enumerate(prog):
+        for vs, w in ((o["reads"], False), (o["writes"], True)):
+            for v in vs:
+                for lo, hi, aw, j in acc.get(v[1], ()):
+                    if lo < v[3] and v[2] < hi and (w or aw) and j != i:
+                        pred[i].add(j)
+        for vs, w in ((o["reads"], False), (o["writes"], True)):
+            for v in vs:
+                lst = acc.setdefault(v[1], [])
+                if w:
+                    lst[:] = [a for a in lst if not (v[2] <= a[0] and a[1] <= v[3])]
+                lst.append((v[2], v[3], w, i))
+        if o["q"] == "t":
+            bank = o["writes"][0][1]
+            if bank in last:
+                pred[i].add(last[bank])
+            last[bank] = i
+    succ = [[] for _ in prog]
+    for i in range(n):
+        for j in pred[i]:
+            succ[j].append(i)
+    rank = [0.0] * n
+    for i in range(n - 1, -1, -1):
+        rank[i] = prog[i]["ns"] + prog[i]["lag"] + max([P["wake"] + rank[j] for j in succ[i]], default=0.0)
+
+    def place(turn, first, back):
+        at, gaps = [0.0] * n, {q: [[0.0, 1e12]] for q in "vstgy"}
+        for i in turn:
+            o = prog[i]
+            t = max([at[j] + prog[j]["ns"] + P["wake"] + (0 if back else prog[j]["lag"]) for j in first[i]], default=0.0)
+            t += o["lag"] if back else 0
+            gs = gaps[o["q"]]
+            k = len(gs) - 1
+            while k > 0 and gs[k - 1][1] > t:
+                k -= 1
+            while gs[k][1] - max(gs[k][0], t) < o["ns"]:
+                k += 1
+            lo, hi = gs[k]
+            at[i] = max(lo, t)
+            gs[k:k + 1] = [x for x in ([lo, at[i]], [at[i] + o["ns"], hi]) if x[1] - x[0] > 40]
+        return at
+
+    if not TURN:
+        lead = [rank[i] + P["lead"] * (prog[i]["x"] == 0) for i in range(n)]
+        for i in range(n - 1, -1, -1):
+            lead[i] = max([lead[i]] + [lead[j] + 1 for j in succ[i]])
+        turn, best = sorted(range(n), key=lambda i: -lead[i]), None
+        for _ in range(P["passes"]):
+            at = place(turn, pred, False)
+            end = max(at[i] + prog[i]["ns"] + prog[i]["lag"] for i in range(n))
+            if best is None or end < best:
+                best = end
+                TURN[:] = [at, end]
+            late = place(sorted(range(n), key=lambda i: -(at[i] + prog[i]["ns"] + prog[i]["lag"])), succ, True)
+            turn = sorted(range(n), key=lambda i: -(late[i] + prog[i]["ns"]))
+    start = TURN[0]
+    order = sorted((start[i], i) for i in range(n))
+    done = [start[i] + prog[i]["ns"] + prog[i]["lag"] for i in range(n)]
+    ready = [max([done[j] + P["wake"] for j in pred[i]], default=0.0) for i in range(n)]
+    out, tail = [], {}
+    for at, i in order:
+        o, t = prog[i], tail.get(prog[i]["q"])
+        if t and o["join"] and t["join"] and t["join"][0] is o["join"][0] and sum(t["join"][1:]) == o["join"][1] and ready[i] <= t["at"] \
+                and all(start[j] >= done[i] for k in t["parts"] for j in succ[k]):
+            make, lo, m = t["join"][0], t["join"][1], t["join"][2] + o["join"][2]
+            call, reads, writes, _ = make(lo, m)
+            t.update(call=call, join=(make, lo, m), parts=t["parts"] + [i], reads=t["reads"] + o["reads"], writes=t["writes"] + o["writes"])
+        else:
+            t = dict(o, at=at, parts=[i])
+            tail[o["q"]] = t
+            out.append(t)
+    return out
+
+
+def issue(g, T, topo, core, eng, calls, sender):
+    count = {"v": 0, "s": 0, "t": 0, "g": 0}
+    clock = {q: {} for q in eng}
+    acc = {}
+    total = {s: 0 for s in DMAS + ["loc"]}
+
+    def engines(src, dst):
+        return topo.engines(src, dst)[:8]
+
+    def region(v):
+        if SCRATCH[v[1]][0] == "psum":
+            return v[1], 0, 512, True
+        return v[1], v[2], v[3], False
+
+    def before(q, reads, writes):
+        need, cks = {}, []
+        for vs, w in ((reads, False), (writes, True)):
+            for v in vs:
+                ps = region(v)[3]
+                for a in acc.get(v[1], ()):
+                    if ps and a[3] != q or (a[0] < v[3] and v[2] < a[1] and (w or a[2]) and not (ps and q == "t")):
+                        need[a[4]] = max(need.get(a[4], 0), a[5])
+                        cks.append((a[4], a[6]))
+        for s in sorted(need):
+            if clock[q].get(s, 0) < need[s] and not any(o != s and ck.get(s, 0) >= need[s] for o, ck in cks):
+                eng[q].wait_ge(T.sem[s], need[s])
+                clock[q][s] = need[s]
+        for _, ck in cks:
+            for s, v in ck.items():
+                clock[q][s] = max(clock[q].get(s, 0), v)
+
+    def after(q, reads, writes, sem, val):
+        ck = dict(clock[q])
+        ck[sem] = val
+        for vs, w in ((reads, False), (writes, True)):
+            for v in vs:
+                lst = acc.setdefault(v[1], [])
+                if region(v)[3]:
+                    lst[:] = [a for a in lst if a[3] == q]
+                if w:
+                    lst[:] = [a for a in lst if not (v[2] <= a[0] and a[1] <= v[3])]
+                lst.append((v[2], v[3], w, q, sem, val, ck))
+
+    for o in calls:
+        if o["kind"] == "send":
+            _, src, land, sem = o["call"]
+            n = len(engines(T.cores[sender[land](int(sem[1]))], core))
+            acc.setdefault(land, []).append((src[2], src[3], True, "x", sem, n, {sem: n}))
+    for o in calls:
+        q = o["q"]
+        if TAG[0]:
+            TAG[0][0] = o["tag"]
+        if o["kind"] == "send":
+            dst, src, land, sem = o["call"]
+            before(q, [src], [])
+            es = engines(core, T.cores[dst])
+            rid, pid = topo.addr(T.cores[dst], core)
+            g.remote_dma(T[land][:, src[2]:src[3]], src[0], T.sem[sem], T.sem.loc, pid, rid, sum(1 << e for e in es))
+            total["loc"] += len(es)
+            continue
+        before(q, o["reads"], o["writes"])
+        if o["kind"] == "dma":
+            sem, pairs = o["call"]
+            for out, in_ in pairs:
+                eng[q].dma_start(out, in_).then_inc(T.sem[sem], 16)
+            total[sem] += 16 * len(pairs)
+            after(q, o["reads"], o["writes"], sem, total[sem])
+        else:
+            count[q] += 1
+            o["call"]().then_inc(T.sem["q" + q], 1)
+            after(q, o["reads"], o["writes"], "q" + q, count[q])
+    for q in count:
         g.wait_ge(T.sem["q" + q], count[q])
-    for s in DMAS:
-        g.wait_ge(T.sem[s], 16)
-    g.wait_ge(T.sem.loc, nloc[0])
+    for s in total:
+        if total[s]:
+            g.wait_ge(T.sem[s], total[s])

@@ -2,38 +2,37 @@ from concourse.mybir import AluOpType, ActivationFunctionType
 
 R, HC = 4, 128
 HN = 16 * HC
+MK = 1024
 BIG = 65536.0
-MODE = "dual"
 KINDS = ("L0", "P0", "L1", "P1", "L2", "P2")
 
 SCRATCH = {
-    "mkx": ("sbuf", [128, HN], "bfloat16"), "mkn": ("sbuf", [128, HN], "bfloat16"),
+    "mkx": ("sbuf", [128, MK], "bfloat16"), "mkn": ("sbuf", [128, MK], "bfloat16"),
     "outl": ("sbuf", [128, R * 6 * HC], "uint16"), "inl": ("sbuf", [128, R * 6 * HC], "uint16"),
-    "ro": ("sbuf", [128, R * 80], "float32"), "rin": ("sbuf", [128, R * 80], "float32"),
+    "ro": ("sbuf", [128, R * 128], "float32"), "rin": ("sbuf", [128, R * 128], "float32"),
     "wti": ("sbuf", [128, 2], "int32"), "sli": ("sbuf", [128, 128], "int32"),
     "slc": ("sbuf", [128, 128], "bfloat16"), "slb": ("sbuf", [128, 2048], "bfloat16"),
-    "ones": ("sbuf", [128, 144], "bfloat16"), "blk0": ("sbuf", [128, 144], "bfloat16"), "blk": ("sbuf", [128, 144], "bfloat16"),
-    "qo": ("sbuf", [128, 144], "bfloat16"), "eye": ("sbuf", [128, 128], "bfloat16"), "swp": ("sbuf", [128, 128], "bfloat16"),
-    "shf": ("sbuf", [128, 240], "bfloat16"),
-    "c13": ("sbuf", [128, 128], "bfloat16"), "cp64": ("sbuf", [128, 128], "bfloat16"), "cm64": ("sbuf", [128, 128], "bfloat16"),
-    "ip": ("sbuf", [128, 80], "bfloat16"), "im": ("sbuf", [128, 80], "bfloat16"), "esl": ("sbuf", [128, 320], "bfloat16"),
-    "sm": ("sbuf", [128, 640], "float32"), "smi": ("sbuf", [128, 512], "int32"), "smb": ("sbuf", [128, 384], "bfloat16"),
-    "smu": ("sbuf", [128, 128], "uint16"),
+    "sm": ("sbuf", [128, 640], "float32"), "smi": ("sbuf", [128, 512], "int32"), "smb": ("sbuf", [128, 1280], "bfloat16"),
+    "smu": ("sbuf", [128, 128], "uint16"), "esl": ("sbuf", [128, 448], "bfloat16"), "shf": ("sbuf", [128, 48], "bfloat16"),
 }
+for _k in ("ones", "blk", "eye", "c13", "chalf", "cp64", "zb", "beye", "ip", "im", "swp", "old0", "old1"):
+    SCRATCH[_k] = ("sbuf", [128, 128], "bfloat16")
+for _k in ("eyeh", "hi0", "hi1"):
+    SCRATCH[_k] = ("sbuf", [128, 128], "float16")
+for _k in ("zf", "eyef", "em2"):
+    SCRATCH[_k] = ("sbuf", [128, 128], "float32")
 for _x in "01":
     SCRATCH["tab" + _x] = ("sbuf", [128, 2048], "bfloat16")
     for _k in ("mx", "mn", "px", "pn"):
         SCRATCH[_k + _x] = ("sbuf", [128, 3 * HN], "bfloat16")
     SCRATCH["gb" + _x] = ("sbuf", [128, 6 * HN], "bfloat16")
     SCRATCH["nw" + _x] = ("sbuf", [128, 3 * HC], "int32")
-    SCRATCH["ud" + _x] = ("sbuf", [128, 4 * HC], "int32")
-    SCRATCH["uc" + _x] = ("sbuf", [128, HC], "float32")
-    SCRATCH["fy" + _x] = ("sbuf", [128, 2 * HC], "bfloat16")
+    SCRATCH["ud" + _x] = ("sbuf", [128, HC], "int32")
+    SCRATCH["uc" + _x] = ("sbuf", [128, 2 * HC], "float32")
+    SCRATCH["fy" + _x] = ("sbuf", [128, HC], "bfloat16")
     SCRATCH["xs" + _x] = ("sbuf", [128, 2 * HC], "int32")
-    SCRATCH["ycf" + _x] = ("sbuf", [128, HC], "float32")
     SCRATCH["wh" + _x] = ("sbuf", [128, 128], "bfloat16")
     SCRATCH["wl" + _x] = ("sbuf", [128, 128], "bfloat16")
-    SCRATCH["q7" + _x] = ("sbuf", [128, 144], "bfloat16")
     for _k in "uzql":
         SCRATCH["p" + _k + _x] = ("psum", [128, 512], "float32")
 
@@ -42,8 +41,13 @@ SEMAPHORES = ["qv", "qs", "qt", "qg", "loc"] + DMAS
 SEMAPHORES += ["l%d%d%d" % (t, k, x) for t in range(R) for k in range(3) for x in range(2)]
 SEMAPHORES += ["r%d%d%d" % (t, k, x) for t in range(R) for k in range(2) for x in range(2)]
 
-PLAN = dict(cycle=0.83, gather=1.4, scatter=3.8, call=15, wake=130, message=3500, dma=3000, lead=10000, passes=4,
-            spiece=256, gpiece=1024)
+PLAN = dict(cycle=0.83, gather=1.5, scatter=3.8, call=10, wake=170, message=3500, first=3500, dma=3000, lead=3500, passes=2,
+            spiece=256, gpiece=1024, early=(1,))
+BIAS = {"A.L0 s": 15000, "A.L0 v": -5500, "A.second v": 3000, "A.answer v": 3500, "A.pick v": 5500, "A.names v": 6500,
+        "B.first v": 11000, "B.L1 s": 5000, "B.L1help v": 5500, "B.second v": 3000, "B.P0 s": 10000, "B.answer v": 7000,
+        "B.truth v": 9000, "B.pick v": 2500}
+HELP = {(t, 1, "L1"): 192 for t in range(R)}
+HELP.update({(0, 0, "L0"): 1024, (0, 0, "L1"): 512, (R - 1, 1, "P2"): 512})
 TURN = []
 TAG = [None]
 
@@ -55,13 +59,22 @@ def rank_program(g, core, T, topo):
     A, F, P = AluOpType, ActivationFunctionType, PLAN
     N = len(T.cores)
     eng = {"v": g.vector, "s": g.scalar, "t": g.tensor, "g": g, "y": g.sync}
-    prog, now = [], {"x": 1, "tag": ""}
+    prog, now = [], {"x": 1, "tag": "", "sent": 0}
 
-    def view(name, lo, hi, step=1, parts=128):
-        return (T[name][0:parts, lo:hi:step], name, lo, hi, (hi - lo + step - 1) // step)
+    def view(name, lo, hi, step=1, parts=128, first=0):
+        return (T[name][first:first + parts, lo:hi:step], name, lo, hi, (hi - lo + step - 1) // step, step, parts)
 
     def sub(v, lo, n):
         return view(v[1], v[2] + lo, v[2] + lo + n)
+
+    def half(v, h):
+        if h is None:
+            return v
+        lo = v[2] + v[4] // 2 * v[5] * h
+        return view(v[1], lo, lo + (v[4] // 2 - 1) * v[5] + 1, v[5], v[6])
+
+    def part(v, h):
+        return view(v[1], v[2], v[3], 1, 64, 64 * h)
 
     def ind(win, off):
         return (win[0].indirect(off[0]), win, off)
@@ -105,19 +118,28 @@ def rank_program(g, core, T, topo):
     def fill(out, c):
         add("v", "op", lambda: g.vector.memset(out[0], c), [], [out], P["call"] + max(64, out[4] / 2) * P["cycle"])
 
+    def act(out, in_, scale, bias=0.0, token=()):
+        add("s", "op", lambda: g.scalar.activation(out[0], in_[0], F.Identity, bias, scale), [in_], list(token) or [out],
+            60 + max(64, out[4]) * P["cycle"])
+
     def iota(out, pattern, base, mul):
         add("g", "op", lambda: g.iota(out[0], pattern, base, mul), [], [out], 130 + 2 * out[4] * P["cycle"])
 
-    def select(out, in_, pattern, o, base, mul):
-        add("g", "op", lambda: g.affine_select(out[0], in_[0], pattern, o, 0.0, base, mul), [in_], [out], 170 + 2 * out[4] * P["cycle"])
+    def select(out, in_, pattern, o, base, mul, rest=0.0):
+        add("g", "op", lambda: g.affine_select(out[0], in_[0], pattern, o, rest, base, mul), [in_], [out], 170 + 2 * out[4] * P["cycle"])
+
+    def band(out, in_, pattern, rest=0.0):
+        select(out, in_, [[-s, n] for s, n in pattern], A.is_ge, 0, 1, rest)
+        select(out, out, pattern, A.is_ge, 15, -1, rest)
 
     def mms(out, pairs, start=True, stop=True):
         def call():
             ins = None
-            for k, (l, r) in enumerate(pairs):
-                ins = g.tensor.matmul(out[0], l[0], r[0], start and k == 0, stop and k == len(pairs) - 1)
+            for k, p in enumerate(pairs):
+                ins = g.tensor.matmul((p + (out,))[2][0], p[0][0], p[1][0], start and k == 0, stop and k == len(pairs) - 1)
             return ins
-        add("t", "op", call, [l for l, _ in pairs] + [r for _, r in pairs], [out], len(pairs) * max(64, out[4]) * P["cycle"])
+        ns = sum(max(min(64, p[0][4]), out[4]) * (4 if SCRATCH[p[0][1]][2] == "float32" else 1) for p in pairs) * P["cycle"]
+        add("t", "op", call, [p[0] for p in pairs] + [p[1] for p in pairs], [out], ns)
 
     def grouped(out, pairs, last):
         mms(out, pairs[:-last], True, False)
@@ -126,8 +148,10 @@ def rank_program(g, core, T, topo):
     def dma(q, sem, pairs, reads, writes):
         add(q, "dma", (sem, pairs), reads, writes, 60 * len(pairs), P["dma"])
 
-    def send(dst, src, land, sem):
-        add("g", "send", (dst, src, land, sem), [src], [view(land, src[2], src[3])], 300, P["message"])
+    def send(dst, src, land, sem, more=()):
+        add("g", "send", (dst, src, land, sem), [src] + list(more), [view(land, src[2], src[3])], 300 if now["sent"] else P["first"],
+            P["message"])
+        now["sent"] = 1
 
     cols, nxt = {}, {}
 
@@ -148,12 +172,12 @@ def rank_program(g, core, T, topo):
         lo = ((t * 3 + k) * 2 + x) * HC
         return view(buf, lo, lo + HC)
 
-    def spans(t, k, x, buf):
-        lo = (t * 2 + x) * 40
-        return view(buf, lo, lo + 24) if k == 0 else view(buf, lo + 24, lo + 40)
+    def spans(t, k, x, buf, zeros):
+        lo, n = (t * 2 + x) * 64 + 48 * k, 24 - 16 * k
+        return view(buf, lo + (0 if zeros else n), lo + 2 * n)
 
-    def send_list(t, k, x):
-        send(partner(t), lists(t, k, x), "inl", "l%d%d%d" % (t, k, x))
+    def send_list(t, k, x, more=()):
+        send(partner(t), lists(t, k, x), "inl", "l%d%d%d" % (t, k, x), more)
 
     def names(x, slot):
         return view("nw%d" % x, slot * HC, (slot + 1) * HC)
@@ -161,88 +185,105 @@ def rank_program(g, core, T, topo):
     def table(x):
         return view("tab%d" % x, 0, 2048)
 
+    def whole(name):
+        return view(name, 0, SCRATCH[name][1][1])
+
+    zeroed = small("zeroed", 8)
+    for v, c in ((whole("ones"), 1.0), (whole("mkx"), 1.0), (view("mkx", 0, MK, 16), 0.0)):
+        fill(v, c)
+    act(whole("rin"), view("mkx", 0, R * 128), 0.0, 0.0, [zeroed])
     for x in range(2):
-        now["x"] = x
+        now["x"], now["tag"] = x, "0%s.start" % "AB"[x]
         dma("y", "dch%d" % x, [(T["nw%d" % x][64 * h:64 * h + 64, 0:HC], T.ch[64 * x:64 * x + 64, h * HC:(h + 1) * HC]) for h in range(2)],
             [], [names(x, 0)])
         dma("sy"[x], "dx%d" % x, [(T["tab%d" % x][64 * h:64 * h + 64, :], T.xt[64 * x:64 * x + 64, :]) for h in range(2)], [], [table(x)])
         cp(lists(0, 0, x), names(x, 0))
-        send_list(0, 0, x)
-    now["x"] = 0
+        send_list(0, 0, x, [zeroed])
+    now["x"], now["tag"] = 0, ""
     dma("y", "dwt", [(T.wti[64 * h:64 * h + 64, z:z + 1], T.wt[64 * z:64 * z + 64, :]) for z in range(2) for h in range(2)],
         [], [view("wti", 0, 2)])
     dma("s", "dsl", [(T.sli[:], T.sl[:])], [], [view("sli", 0, 128)])
     cp(view("slc", 0, 128), view("sli", 0, 128))
     dma("y", "dsb", [(T.slb[0:8, :], T.slc[:])], [view("slc", 0, 128)], [view("slb", 0, 2048)])
 
-    ones, blk, qo, eye = view("ones", 0, 144), view("blk", 0, 144), view("qo", 0, 144), view("eye", 0, 128)
-    mkx, mkn = view("mkx", 0, HN), view("mkn", 0, HN)
-    fill(ones, 1.0)
-    fill(mkx, 1.0)
-    fill(view("mkx", 0, HN, 16), 0.0)
-    add("s", "op", lambda: g.scalar.activation(mkn[0], mkx[0], F.Identity, 512.0, -512.0), [mkx], [mkn], HN * P["cycle"])
-    for name, n, c in (("c13", 128, 2.0 ** -13), ("cp64", 128, 64.0), ("cm64", 128, -64.0), ("shf", 240, 0.0), ("esl", 320, 0.0),
-                       ("ro", R * 80, 0.0)):
-        fill(view(name, 0, n), c)
-    pidx, i16, ib, ic, ie = (small(n, w, "smi") for n, w in (("pidx", 8), ("i16", 16), ("ib", 80), ("ic", 64), ("ie", 64)))
+    ones, blk, eye, zb, zf = (whole(n) for n in ("ones", "blk", "eye", "zb", "zf"))
+    ip, im, sgn = view("ip", 0, 88), view("im", 0, 88), small("sgn", 112, "smb")
+    c716, c35, last = small("c716", 64, "smb"), small("c35", 16, "smb"), small("last", 16, "smb")
+    for v, c in ((zb, 0.0), (c716, -7.0 / 16), (c35, 3.5), (sub(last, 0, 8), 15.0), (sub(last, 8, 8), 0.0),
+                 (sgn, -1.0), (sub(sgn, 16, 16), 0.0), (sub(sgn, 96, 8), 1.0)):
+        fill(v, c)
+    act(whole("mkn"), whole("mkx"), -512.0, 512.0)
+    for v, c in ((whole("c13"), 2.0 ** -13), (whole("cp64"), 64.0), (zf, 0.0)):
+        act(v, sub(ones, 0, 128), c)
+    act(whole("shf"), sub(ones, 0, 48), 0.0)
+    for h, c in enumerate((-2.0 ** -7, 2.0 ** -19)):
+        add("v", "op", lambda h=h, c=c: g.vector.memset(T.chalf[64 * h:64 * h + 64, :], c), [], [whole("chalf")], P["call"] + 64 * P["cycle"])
+    pidx, i16, i8, i77 = (small(n, w, "smi") for n, w in (("pidx", 8), ("i16", 16), ("i8", 8), ("i77", 2)))
+    mask2, thr = small("mask", 128, "smb"), small("thr", 64, "smb")
+    mask = sub(mask2, 0, 64)
     iota(pidx, [[0, 8]], 0, 1)
-    select(view("blk0", 0, 144), ones, [[-16, 9], [0, 16]], A.is_ge, 0, 1)
-    select(blk, view("blk0", 0, 144), [[16, 9], [0, 16]], A.is_ge, 15, -1)
-    iota(ib, [[0, 10], [-16, 8]], 0, 1)
+    iota(i77, [[77, 2]], 0, 0)
+    band(blk, ones, [[16, 8], [0, 16]])
     iota(i16, [[1, 16]], 0, 0)
-    iota(ic, [[-16, 8], [0, 8]], 0, 1)
-    iota(ie, [[0, 8], [-100, 2], [-1, 4]], 0, 1)
+    iota(i8, [[16, 8]], 0, 0)
     select(eye, sub(ones, 0, 128), [[-1, 128]], A.is_equal, 0, 1)
-    select(qo, blk, [[0, 9], [1, 16]], A.is_equal, -15, 0)
+    ts(whole("eyeh"), eye, -1.0, A.mult)
+    band(ip, sub(ones, 0, 88), [[0, 11], [16, 8]])
+    ts(im, ip, -1.0, A.mult)
+    for a, b in ((ip, im), (im, ip)):
+        select(sub(a, 16, 8), sub(b, 24, 8), [[0, 8]], A.is_ge, 0, 0)
+    band(thr, sub(zb, 0, 64), [[16, 8], [0, 8]], -BIG)
+    band(mask, sub(ones, 0, 64), [[16, 8], [0, 8]])
+    for x in range(2):
+        for h in range(2):
+            select(view("esl", (2 * x + h) * 112, (2 * x + h + 1) * 112), sgn, [[0, 14], [-100, 2], [-1, 4]], A.is_equal, 100 * h - 4 * x, 1)
+    for name, zero, c in (("eyef", zf, 1.0), ("em2", zf, -2.0), ("beye", zb, BIG)):
+        select(whole(name), zero, [[-1, 128]], A.not_equal, 0, 1, c)
+    select(whole("swp"), zb, [[-1, 128]], A.not_equal, -64, 1, 1.0)
+    select(whole("swp"), whole("swp"), [[-1, 128]], A.not_equal, 64, 1, 1.0)
 
-    wti = view("wti", 0, 2)
-    wa, wb, wc, wd = (small(n, 2, "smi") for n in ("wa", "wb", "wc", "wd"))
-    fa, fb, fd = (small(n, 2) for n in ("fa", "fb", "fd"))
-    pm, k6, k7, p8 = small("pm", 8, "smi"), small("k6", 1, "smi"), small("k7", 1, "smi"), small("p8", 4, "smi")
-    kc, c01, pf, ph, il = small("kc", 2), small("c01", 2), small("pf", 1), small("ph", 1), small("il", 8)
-    mask, thr, iv = small("mask", 64), small("thr", 64), small("iv", 8)
-    at16, ivb, xo = small("at16", 8, "smb"), small("ivb", 8, "smb"), small("xo", 4, "smu")
+    wti, wi, wf, wb = view("wti", 0, 2), small("wi", 10, "smi"), small("wf", 10), small("wb", 4)
+    pm, p8 = small("pm", 8, "smi"), small("p8", 8, "smi")
+    kc, c01, pf, pk, ph = small("kc", 2), small("c01", 2), small("pf", 1), small("pk", 1), small("ph", 2)
+    bases, mask9, xo, xo2 = small("bases", 24, "smb"), small("mask9", 64, "smb"), small("xo", 8, "smu"), small("xo2", 8, "smu")
+    at16 = sub(bases, 0, 8)
     ts(pm, pidx, 15, A.bitwise_and)
-    ts(p8, sub(pidx, 0, 4), 7, A.bitwise_and)
-    ts(ph, sub(pidx, 0, 1), 64.0, A.is_ge, 1024.0, A.mult)
-    ts(k6, sub(pm, 0, 1), 613.0, A.mult)
+    ts(p8, pidx, 7, A.bitwise_and)
+    for h, o in enumerate((A.is_ge, A.is_lt)):
+        ts(sub(ph, h, 1), sub(pidx, 0, 1), 64.0, o, 1024.0, A.mult)
+    ts(pk, sub(pm, 0, 1), 613.0, A.mult)
     cp(pf, sub(pm, 0, 1))
     cp(xo, p8)
-    ts(k7, k6, 2047, A.bitwise_and)
-    for j in range(2):
-        ts(sub(c01, j, 1), k7, 77.0 * j, A.add, 64.0, A.mult)
+    ts(c01, i77, pk, A.add, 64.0, A.mult)
     ts(kc, c01, 992.0, A.add)
-    for o, m in ((wb, 1984), (wc, 2048), (wa, 63), (wd, 7)):
-        ts(o, wti, m, A.bitwise_and)
-    tt(fb, wb, wc, A.subtract)
-    cp(fa, wa)
-    cp(fd, wd)
-    ts(ib, ib, 4, A.arith_shift_right)
-    ts(ic, ic, 4, A.arith_shift_right)
-    ts(il, sub(i16, 0, 8), 16.0, A.mult, pf, A.add)
-    ts(view("shf", 112, 128), i16, pf, A.is_equal, 4096.0, A.mult)
-    for name, s in (("ip", 1.0), ("im", -1.0)):
-        ts(view(name, 0, 16), sub(ib, 0, 16), 0.0, A.is_equal, 2.0 * s, A.mult)
-        ts(view(name, 16, 80), sub(ib, 16, 64), 0.0, A.is_equal, s, A.mult)
-    ts(mask, ic, 0.0, A.is_equal)
-    ts(thr, ic, 0.0, A.not_equal, -BIG, A.mult)
-    ts(at16, il, 16.0, A.mult)
-    ts(iv if MODE == "dma" else ivb, il, 8.0, A.mult, ph, A.add)
+    for k, m in enumerate((1984, 3, 2048, 4, 63)):
+        ts(sub(wi, 2 * k, 2), wti, m, A.bitwise_and)
+    ts(wf, wi, 2.0 ** -12, A.mult)
+    tt(wb, sub(wf, 0, 4), sub(wf, 4, 4), A.subtract)
+    ts(view("shf", 16, 32), i16, pf, A.is_equal, 4096.0, A.mult)
+    ts(at16, i8, pf, A.add, 16.0, A.mult)
+    for h in range(2):
+        ts(sub(bases, 8 + 8 * h, 8), at16, 0.5, A.mult, sub(ph, h, 1), A.add)
     for x in range(2):
-        ts(view("wh%d" % x, 0, 128), sub(blk, 0, 128), sub(fb, x, 1), A.mult, 2.0 ** -12, A.mult)
-        ts(view("wl%d" % x, 0, 128), sub(blk, 0, 128), sub(fa, x, 1), A.mult, 2.0 ** -12, A.mult)
-        ts(view("q7%d" % x, 0, 144), qo, sub(fd, x, 1), A.mult)
-        cp(view("swp", 64 * x, 64 * x + 64), sub(eye, 64 - 64 * x, 64))
-        for h in range(2):
-            ts(view("esl", (2 * x + h) * 80 + 16, (2 * x + h) * 80 + 80), ie, 4.0 * x - 100.0 * h, A.is_equal, -1.0, A.mult)
+        ts(whole("wh%d" % x), blk, sub(wb, x, 1), A.mult)
+        ts(whole("wl%d" % x), blk, sub(wf, 8 + x, 1), A.mult)
+        ts(small("w8%d" % x, 64, "smb"), sub(ip, 24, 64), sub(wb, 2 + x, 1), A.mult, 512.0, A.mult)
+    ts(mask9, mask, 2.0 ** -9, A.mult)
+    ts(sub(mask2, 64, 64), mask, 2.0 ** -12, A.mult)
+    cp(sub(xo2, 0, 4), sub(p8, 0, 4))
+    ts(sub(xo2, 4, 4), sub(p8, 0, 4), 8.0, A.add)
 
     def look(t, x, kind):
         k, own = int(kind[1]), kind[0] == "L"
         at, off = KINDS.index(kind) * HN, lists(t, k, x, "outl" if own else "inl")
 
-        def gather(lo, n):
-            src, dst = ind(table(x), sub(off, lo // 16, n // 16)), view("gb%d" % x, at + lo, at + lo + n)
-            return lambda: g.scalar.activation(dst[0], src[0], F.Copy), [src], [dst], 65 + n * P["gather"] * P["cycle"]
+        def gather(q):
+            def make(lo, n):
+                src, dst = ind(table(x), sub(off, lo // 16, n // 16)), view("gb%d" % x, at + lo, at + lo + n)
+                if q == "v":
+                    return lambda: g.vector.tensor_copy(dst[0], src[0]), [src], [dst], 50 + n * P["gather"] * P["cycle"]
+                return lambda: g.scalar.activation(dst[0], src[0], F.Copy), [src], [dst], 65 + n * P["gather"] * P["cycle"]
+            return make
 
         def scan(least):
             o0, o1 = (A.max, A.min) if least else (A.mult, A.max)
@@ -252,38 +293,56 @@ def rank_program(g, core, T, topo):
                 o = view(("m" if own else "p") + ("n%d" if least else "x%d") % x, k * HN + lo, k * HN + lo + n)
                 return lambda: g.vector.tensor_tensor_scan(o[0], d0[0], d1[0], 0.0, o0, o1), [d0, d1], [o], P["call"] + n / 2 * P["cycle"]
             return make
-        for q, make, n in (("s", gather, P["gpiece"]), ("v", scan(False), P["spiece"]), ("v", scan(True), P["spiece"])):
-            for lo in range(0, HN, n):
-                add(q, "op", *make(lo, n), join=(make, lo, n))
+        cut = HN - HELP.get((t, x, kind), 0)
+        step = now["tag"]
+        for q, make, a, b, n, most, what in (("s", gather("s"), 0, cut, P["gpiece"], HN, ""), ("v", gather("v"), cut, HN, P["spiece"], HN, "help"),
+                                             ("v", scan(False), 0, HN, P["spiece"], MK, ""), ("v", scan(True), 0, HN, P["spiece"], MK, "min")):
+            now["tag"] = step + what
+            for lo in range(a, b, n):
+                add(q, "op", *make(lo, min(n, b - lo)), join=(make, lo, min(n, b - lo), most))
 
     def res(buf, x, k):
         return view("%s%d" % (buf, x), k * HN + 15, (k + 1) * HN, 16)
 
-    def span(side, x, k, sign, lo, hi):
-        p, m = view("ip", lo, hi), view("im", lo, hi)
+    def span(side, x, k, sign, lo, n):
+        p, m = sub(ip, lo, n), sub(im, lo, n)
         return [(res(side + "x", x, k), p if sign > 0 else m), (res(side + "n", x, k), m if sign > 0 else p)]
 
-    def slack(t, j, x, lo, hi):
+    def slack(t, j, x, lo, n):
         o = (t * 2 + j) * 2 * HC
-        return [(view("slb", o + h * HC, o + (h + 1) * HC, 1, 8), view("esl", (2 * x + h) * 80 + lo, (2 * x + h) * 80 + hi, 1, 8))
+        return [(view("slb", o + h * HC, o + (h + 1) * HC, 1, 8), view("esl", (2 * x + h) * 112 + lo, (2 * x + h) * 112 + lo + n, 1, 8))
                 for h in range(2)]
 
-    def to_list(x, col, r):
-        out = view("pl%d" % x, col, col + 8)
-        grouped(out, [(eye, at16)] + [(view("shf", 112 - 16 * b, 240 - 16 * b), view(r[1], r[2] + b, r[3], 8)) for b in range(8)], 8)
-        return out
+    def shifted(out, r, turn=0):
+        return [(view("shf", 16 - 16 * (b % 2), 48 - 16 * (b % 2)), view(r[1], r[2] + (b + 4 * turn) % 8, r[3], 8),
+                 view(out[1], out[2], out[3], 1, 32, 32 * (b // 2))) for b in range(8)]
 
-    def product(x, k, out):
-        y, v, hi, uc = res("mx", x, k), view("pu%d" % x, 0, HC), view("ud%d" % x, HC, 2 * HC), view("uc%d" % x, 0, HC)
-        grouped(v, [(view("c13", 0, 128), sub(ones, 0, HC)), (view("wh%d" % x, 0, 128), y), (view("wl%d" % x, 0, 128), y)], 2)
-        ts(hi, v, 2.0 ** -13 - 0.5 - 1.0 / 64, A.add)
-        tt(v, v, hi, A.subtract)
-        tt(uc, v, names(x, k), A.mult)
-        ts(out, uc, 4096.0, A.mult, sub(c01, k, 1), A.add)
+    def product(x, k, h):
+        lo, n = (0, HC) if h is None else (64 * h, 64)
+        y = half(res("mx", x, k), h)
+        hi, uc = view("hi%d" % x, lo, lo + n), view("uc%d" % x, HC * k + lo, HC * k + lo + n)
+        low, v = view("pu%d" % x, lo, lo + n), view("pq%d" % x, HC + lo, HC + lo + n)
+        weigh = [(whole("wh%d" % x), y), (whole("wl%d" % x), y)]
+        grouped(low, [(whole("chalf"), sub(ones, 0, n))] + weigh, 2)
+        mms(v, [(whole("c13"), sub(ones, 0, n))] + weigh, True, False)
+        ts(hi, low, 1.5 * 2.0 ** 23, A.add, -1.5 * 2.0 ** 23, A.add)
+        mms(v, [(whole("eyeh"), hi)], False, True)
+        tt(uc, v, sub(names(x, k), lo, n), A.mult)
+        return uc
+
+    def propose(t, x, j, uc, h):
+        raw, new = half(whole("ud%d" % x), h), half(names(x, j + 1), h)
+        ts(raw, uc, 4096.0, A.mult, sub(c01, j, 1), A.add)
+        ts(new, raw, 6, A.arith_shift_right, 2047, A.bitwise_and)
+        cp(half(lists(t, j + 1, x), h), new)
+
+    both = small("both", 32)
 
     def kappa():
-        kv, kr = small("kv", 16), small("kr", 1)
+        kv, kr, ne = small("kv", 16), small("kr", 1), small("ne", 16, "smb")
+        tt(ne, sub(both, 0, 16), sub(both, 16, 16), A.is_equal)
         d0, d1 = sub(ones, 0, 16), view("pq0", 64, 80)
+        mms(d1, [(whole("cp64"), ne)])
         vec(lambda: g.vector.tensor_tensor_scan(kv[0], d0[0], d1[0], -992.0, A.mult, A.add), kv, [d0, d1])
         ts(kr, sub(kv, 15, 1), 1.5 * 2.0 ** 34, A.add, -1.5 * 2.0 ** 34, A.add)
         ts(c01, kc, sub(kv, 15, 1), A.add, kr, A.subtract)
@@ -294,64 +353,85 @@ def rank_program(g, core, T, topo):
 
         def tag(w):
             now["tag"] = "%d%s.%s" % (t, "AB"[x], w)
-        z, ud = "pz%d" % x, "ud%d" % x
+        z = "pz%d" % x
+        rise = span("m", x, 0, -1, 0, 88), span("m", x, 1, 1, 0, 88), span("m", x, 2, 1, 0, 88)
+
+        def cut(pairs, lo, n):
+            return [(l, sub(r, lo, n)) for l, r in pairs]
         tag("L0")
         look(t, x, "L0")
         tag("first")
-        u0 = view(ud, 3 * HC, 4 * HC)
-        product(x, 0, u0)
-        ts(names(x, 1), u0, 6, A.arith_shift_right, 2047, A.bitwise_and)
-        cp(lists(t, 1, x), names(x, 1))
+        for h in range(2):
+            propose(t, x, 0, product(x, 0, h), h)
         send_list(t, 1, x)
-        ts(view(ud, 0, HC), u0, 77.0 * 64, A.add)
         tag("L1")
         look(t, x, "L1")
         tag("second")
-        product(x, 1, view(ud, 2 * HC, 3 * HC))
-        grouped(view(z, 0, 80), slack(t, 0, x, 0, 80) + span("m", x, 0, -1, 0, 80) + span("m", x, 1, 1, 0, 80), 1)
         r, so = sv("rb", 64, "smb"), sv("so", 8, "smu")
-        tt(r, view(z, 16, 80), thr, A.is_le)
-        ts(so, to_list(x, 0, r), 1.0 / 16, A.mult)
-        ts(names(x, 2), ind(view(ud, 0, 3 * HC), so), 6, A.arith_shift_right, 2047, A.bitwise_and)
-        cp(lists(t, 2, x), names(x, 2))
+        product(x, 1, None)
+        at = view("pl%d" % x, 0, 8)
+        grouped(view(z, 0, 64), slack(t, 0, x, 32, 64) + cut(rise[0] + rise[1], 24, 64), 1)
+        tt(r, view(z, 0, 64), thr, A.is_le)
+        grouped(at, [(eye, at16)] + shifted(at, r) + [(eye, at16)], 9)
+        ts(so, at, 1.0 / 32, A.mult)
+        propose(t, x, 1, ind(whole("uc%d" % x), so), None)
         send_list(t, 2, x)
         for kind in ("P0", "P1", "P2"):
             tag(kind)
             look(t, x, kind)
         tag("answer")
-        for k, out, pairs in ((0, view("pq%d" % x, 0, 24), span("p", x, 0, 1, 8, 32) + span("p", x, 1, -1, 8, 32)),
-                              (1, view("pq%d" % x, 32, 40), span("p", x, 0, 1, 16, 24) + span("p", x, 2, -1, 16, 24))):
-            v = spans(t, k, x, "ro")
+        for k, out, pairs in ((0, view("pq%d" % x, 0, 24), span("p", x, 0, -1, 24, 24) + span("p", x, 1, 1, 24, 24)),
+                              (1, view("pq%d" % x, 32, 40), span("p", x, 0, 1, 24, 8) + span("p", x, 2, -1, 24, 8))):
+            v = spans(t, k, x, "ro", False)
             grouped(out, pairs, 1)
-            cp(sub(v, 8 * k, out[4]), out)
+            ts(v, out, float(k), A.add)
             send(asker(t), v, "rin", "r%d%d%d" % (t, k, x))
         tag("L2")
         look(t, x, "L2")
         tag("truth")
-        hh, dh, e, x12, w12, hd, m, sel = (sv(n, 16, "smb" if n == "e" else "sm") for n in ("hh", "dh", "e", "x12", "w12", "hd", "m", "sel"))
-        ts(hh, view(z, 32, 48), 0.0, A.is_le, 0.5, A.mult)
-        tt(view(z, 8, 32), view(z, 8, 32), spans(t, 0, x, "rin"), A.subtract)
-        ts(dh, view(z, 16, 32), 0.0, A.is_le, 0.5, A.mult)
-        tt(x12, view(z, 0, 16), hh, A.mult)
-        tt(e, hh, dh, A.is_equal)
+        z2, hd, x12, sel, ne0 = view(z, 64, 112), sv("hd", 48), sv("x12", 16), sv("sel", 8), sv("ne0", 16, "smb")
+        grouped(z2, slack(t, 0, x, 0, 48) + cut(rise[0] + rise[1], 0, 48) + [(whole("eyef"), spans(t, 0, x, "rin", True))], 1)
+        ts(hd, z2, 0.0, A.is_le, 0.5, A.mult)
+        tt(x12, sub(z2, 16, 16), sub(hd, 0, 16), A.mult)
+        tt(ne0, sub(hd, 0, 16), sub(hd, 32, 16), A.not_equal)
         tag("decide")
-        rz = view("pu%d" % x, 128, 144)
-        grouped(rz, slack(t, 1, x, 16, 32) + span("m", x, 0, -1, 16, 32) + span("m", x, 2, 1, 16, 32), 1)
-        tt(w12, rz, x12, A.subtract)
-        tt(hd, w12, spans(t, 1, x, "rin"), A.is_le)
-        tt(m, hd, e, A.mult)
-        tt(sub(sel, 0, 8), sub(m, 8, 8), sub(dh, 0, 8), A.max)
-        tt(r, ind(sub(sel, 0, 8), xo), mask, A.mult)
-        at = to_list(x, 8, r)
-        if t < R - 1:
-            ne = sv("ne", 8, "smb")
-            tt(ne, sub(m, 0, 8), sub(m, 8, 8), A.not_equal)
-            mms(view("pq0", 64 + 8 * x, 72 + 8 * x), [(view("cm64", 0, 128), sub(e, 0, 8)), (view("cp64", 0, 128), ne)])
-        tag("pick")
-        fo, no, fy = sv("fo", 8, "smu"), sv("no", 8, "smu"), view("fy%d" % x, 0, HC)
-        ts(fo, at, 15.0, A.add)
+        w2 = view("pu%d" % x, 128, 144)
+        grouped(w2, slack(t, 1, x, 96, 16) + cut(rise[0], 16, 16) + [(whole("em2"), x12), (whole("beye"), ne0)] + cut(rise[2], 16, 16), 2)
+        fv, no, fy = sv("fv", 24, "smu"), sv("no", 8, "smu"), view("fy%d" % x, 0, HC)
+        fo, vo, d0 = sub(fv, 0, 8), sub(fv, 8, 8), sub(hd, 32, 8)
+        early = t == R - 1 and x in P["early"]
+        if early:
+            u3, ui, xa, xb, d1 = view("pl%d" % x, 16, 40), small("ui", 24, "smi"), small("xa", 16), small("xb", 16), small("d1", 16)
+            ra, rb, rc = (small(n, 128, "smb") for n in ("ra", "rb", "rc"))
+            for k in range(3):
+                mms(sub(u3, 8 * k, 8), [(res("mx", x, k), sv("w8", 8, "smb"))])
+            ts(ui, u3, 8.0, A.mult)
+            ts(ui, ui, 7, A.bitwise_and)
+            cp(sub(xa, 0, 8), d0)
+            ts(sub(xb, 0, 8), d0, 2.0, A.mult)
+            tt(sub(xb, 8, 8), sub(ui, 8, 8), sub(ui, 0, 8), A.subtract)
+            tt(sub(xb, 8, 8), sub(xb, 8, 8), sub(xb, 0, 8), A.mult)
+            tt(sub(xa, 8, 8), sub(xb, 8, 8), sub(ui, 0, 8), A.add)
+            tt(sub(xb, 8, 8), sub(ui, 16, 8), sub(xa, 8, 8), A.subtract)
+            ts(sub(xb, 0, 8), d0, -1.0, A.mult, 1.0, A.add)
+            tt(ra, ind(xa, xo2), mask2, A.mult)
+            tt(rb, ind(xb, xo2), mask2, A.mult)
+            tt(d1, w2, spans(t, 1, x, "rin", True), A.is_lt)
+            tt(rc, ind(sub(d1, 8, 8), xo), rb, A.mult)
+            at = view("pl%d" % x, 40, 56)
+            grouped(at, [(eye, sub(bases, 0, 16))] + shifted(at, ra) + shifted(at, rc) + [(eye, last)], 9)
+            tag("pick")
+            cp(sub(fv, 0, 16), at)
+        else:
+            tt(view(both[1], both[2] + x, both[3], 2), w2, spans(t, 1, x, "rin", True), A.is_lt)
+            tt(sel, view(both[1], both[2] + 16 + x, both[3], 2), d0, A.max)
+            tt(r, ind(sel, sub(xo, 0, 4)), mask, A.mult)
+            at = view("pl%d" % x, 8, 16)
+            grouped(at, [(eye, at16)] + shifted(at, r) + [(eye, sub(last, 0, 8))], 9)
+            tag("pick")
+            cp(fo, at)
         cp(fy, ind(view("mx%d" % x, 0, 3 * HN), fo))
-        mms(view("pl%d" % x, 16, 24), [(view("q7%d" % x, 15 - j, 143 - j), view(fy[1], j, HC, 16)) for j in range(16)])
+        tag("names")
         ts(no, fo, 15.0, A.subtract, 1.0 / 16, A.mult)
         picked = ind(view("nw%d" % x, 0, 3 * HC), no)
         if t < R - 1:
@@ -359,39 +439,36 @@ def rank_program(g, core, T, topo):
             send_list(t + 1, 0, x)
             cp(names(x, 0), lists(t + 1, 0, x))
         else:
-            y = view("ycf%d" % x, 0, HC)
+            y = view("uc%d" % x, 0, HC)
             cp(y, picked)
-            dma("y", "dyc%d" % x, [(T.yc[64 * x:64 * x + 64, h * HC:(h + 1) * HC], T[y[1]][64 * h:64 * h + 64, :]) for h in range(2)], [y], [])
+            dma("y", "dyc%d" % x, [(T.yc[64 * x:64 * x + 64, h * HC:(h + 1) * HC], part(y, h)[0]) for h in range(2)], [y], [])
         tag("update")
-        ui, u7, tab = sv("ui", 8, "smi"), sv("u7", 8, "smi"), table(x)
-        cp(ui, view("pl%d" % x, 16, 24))
-        ts(u7, ui, 7, A.bitwise_and)
-        tb = T[tab[1]]
-        fresh = [tb[64 * h:64 * h + 64, 1024 * h:1024 * (h + 1)] for h in range(2)]
-        if MODE == "dual":
+        tab, xs, xh = table(x), view("xs%d" % x, 0, HC), view("xs%d" % x, HC, 2 * HC)
+        if not early:
+            u8, rest, q8, at = view("pu%d" % x, 192, 256), view(z, 128, 192), view("hi%d" % x, 0, 64), view("pl%d" % x, 16, 24)
+            grouped(u8, [(eye, c716), (fy, sv("w8", 64, "smb"))], 1)
+            mms(rest, [(eye, c716), (fy, sv("w8", 64, "smb"))], True, False)
+            ts(q8, u8, 1.5 * 2.0 ** 23, A.add, -1.5 * 2.0 ** 23, A.add)
+            mms(rest, [(whole("eyeh"), q8)], False, True)
+            tt(r, rest, mask9, A.mult)
             n = 2 if t < R - 1 else 1
-            ub, vo, old, xh = sv("ub", 8, "smb"), sub(sv("vo", 16, "smu"), 0, 8 * n), view(fy[1], HC, 2 * HC), view("xs%d" % x, 0, n * HC)
-            turn = [eye, view("swp", 0, 128)]
-            cp(ub, u7)
-            for h in range(n):
-                grouped(view("pl%d" % x, 32 + 8 * h, 40 + 8 * h), [(turn[h], ivb), (turn[h], ub)], 1)
-            cp(vo, view("pl%d" % x, 32, 32 + 8 * n))
+            at, vo = view("pl%d" % x, 16, 16 + 8 * n), sub(fv, 8, 8 * n)
+            moves = [m for h in range(n) for m in shifted(sub(at, 8 * h, 8), r, h)]
+            grouped(at, [(eye, sub(bases, 8, 8 * n))] + moves + [(eye, sub(c35, 0, 8 * n))], 8 * n + 1)
+            cp(vo, at)
+        if t < R - 1:
+            old, xh = view("old%d" % x, 0, HC), whole("xs%d" % x)
             cp(old, ind(tab, sub(vo, 0, 8)))
-            for h in range(n):
-                grouped(view(z, 128 + h * HC, 128 + (h + 1) * HC), [(turn[h], fy), (turn[h], old)], 1)
-            ts(xh, view(z, 128, 128 + n * HC), 0.5, A.mult, -0.25, A.add)
+            for h, turn in enumerate((eye, whole("swp"))):
+                grouped(view(z, (2 + h) * HC, (3 + h) * HC), [(turn, fy), (turn, old)], 1)
+            ts(xh, view(z, 2 * HC, 4 * HC), 0.5, A.mult, -0.25, A.add)
         else:
-            vf, vo, xs, xh = sv("vf", 8), sv("vo", 8, "smu"), view("xs%d" % x, 0, HC), view("xs%d" % x, HC, 2 * HC)
-            tt(vf, u7, iv, A.add)
-            cp(vo, vf)
             tt(xs, ind(tab, vo), fy, A.add)
             ts(xh, xs, 1, A.arith_shift_right)
         out = ind(tab, vo)
         add("v", "op", lambda: g.vector.tensor_copy(out[0], xh[0]), [xh, vo], [tab], 50 + xh[4] * P["scatter"] * P["cycle"])
         if t == R - 1:
-            dma("y", "dc%d" % x, [(T.yx[64 * x:64 * x + 64, 1024 * h:1024 * (h + 1)], fresh[h]) for h in range(2)], [tab], [])
-        elif MODE == "dma":
-            dma("y", "dc%d" % x, [(tb[64 * (1 - h):64 * (1 - h) + 64, 1024 * h:1024 * (h + 1)], fresh[h]) for h in range(2)], [], [tab])
+            dma("y", "dc%d" % x, [(T.yx[64 * x:64 * x + 64, 1024 * h:1024 * (h + 1)], part(half(tab, h), h)[0]) for h in range(2)], [tab], [])
 
     for t in range(R):
         if t:
@@ -450,7 +527,8 @@ def plan(prog):
         return at
 
     if not TURN:
-        lead = [rank[i] + P["lead"] * (prog[i]["x"] == 0) for i in range(n)]
+        lead = [rank[i] + P["lead"] * (o["x"] == 0) + BIAS.get(o["tag"][1:] + " " + o["q"], 0)
+                for i, o in enumerate(prog)]
         for i in range(n - 1, -1, -1):
             lead[i] = max([lead[i]] + [lead[j] + 1 for j in succ[i]])
         turn, best = sorted(range(n), key=lambda i: -lead[i]), None
@@ -469,8 +547,8 @@ def plan(prog):
     out, tail = [], {}
     for at, i in order:
         o, t = prog[i], tail.get(prog[i]["q"])
-        if t and o["join"] and t["join"] and t["join"][0] is o["join"][0] and sum(t["join"][1:]) == o["join"][1] and ready[i] <= t["at"] \
-                and all(start[j] >= done[i] for k in t["parts"] for j in succ[k]):
+        if t and o["join"] and t["join"] and t["join"][0] is o["join"][0] and sum(t["join"][1:3]) == o["join"][1] and ready[i] <= t["at"] \
+                and t["join"][2] + o["join"][2] <= o["join"][3] and all(start[j] >= done[i] for k in t["parts"] for j in succ[k]):
             make, lo, m = t["join"][0], t["join"][1], t["join"][2] + o["join"][2]
             call, reads, writes, _ = make(lo, m)
             t.update(call=call, join=(make, lo, m), parts=t["parts"] + [i], reads=t["reads"] + o["reads"], writes=t["writes"] + o["writes"])
@@ -535,7 +613,7 @@ def issue(g, T, topo, core, eng, calls, sender):
             TAG[0][0] = o["tag"]
         if o["kind"] == "send":
             dst, src, land, sem = o["call"]
-            before(q, [src], [])
+            before(q, o["reads"], [])
             es = engines(core, T.cores[dst])
             rid, pid = topo.addr(T.cores[dst], core)
             g.remote_dma(T[land][:, src[2]:src[3]], src[0], T.sem[sem], T.sem.loc, pid, rid, sum(1 << e for e in es))

@@ -1,3 +1,4 @@
+import numpy as np
 from concourse.mybir import AluOpType, ActivationFunctionType
 
 R, HC = 4, 128
@@ -12,13 +13,11 @@ SCRATCH = {
     "ro": ("sbuf", [128, R * 128], "float32"), "rin": ("sbuf", [128, R * 128], "float32"),
     "wti": ("sbuf", [128, 2], "int32"), "sli": ("sbuf", [128, 128], "int32"),
     "slc": ("sbuf", [128, 128], "bfloat16"), "slb": ("sbuf", [128, 2048], "bfloat16"),
-    "sm": ("sbuf", [128, 640], "float32"), "smi": ("sbuf", [128, 512], "int32"), "smb": ("sbuf", [128, 1280], "bfloat16"),
-    "smu": ("sbuf", [128, 128], "uint16"), "esl": ("sbuf", [128, 448], "bfloat16"), "shf": ("sbuf", [128, 48], "bfloat16"),
+    "sm": ("sbuf", [128, 640], "float32"), "smi": ("sbuf", [128, 512], "int32"), "smb": ("sbuf", [128, 1536], "bfloat16"),
+    "smu": ("sbuf", [128, 128], "uint16"), "esl": ("sbuf", [128, 448], "bfloat16"), "shf": ("sbuf", [128, 96], "bfloat16"),
 }
-for _k in ("ones", "blk", "eye", "c13", "chalf", "cp64", "zb", "beye", "ip", "im", "swp", "old0", "old1"):
+for _k in ("ones", "blk", "eye", "c13", "chalf", "cp64", "zb", "beye", "ip", "im", "swp", "old0", "old1", "up", "down"):
     SCRATCH[_k] = ("sbuf", [128, 128], "bfloat16")
-for _k in ("eyeh", "hi0", "hi1"):
-    SCRATCH[_k] = ("sbuf", [128, 128], "float16")
 for _k in ("zf", "eyef", "em2"):
     SCRATCH[_k] = ("sbuf", [128, 128], "float32")
 for _x in "01":
@@ -31,8 +30,8 @@ for _x in "01":
     SCRATCH["uc" + _x] = ("sbuf", [128, 2 * HC], "float32")
     SCRATCH["fy" + _x] = ("sbuf", [128, HC], "bfloat16")
     SCRATCH["xs" + _x] = ("sbuf", [128, 2 * HC], "int32")
-    SCRATCH["wh" + _x] = ("sbuf", [128, 128], "bfloat16")
-    SCRATCH["wl" + _x] = ("sbuf", [128, 128], "bfloat16")
+    SCRATCH["wp" + _x] = ("sbuf", [128, 128], "float16")
+    SCRATCH["wm" + _x] = ("sbuf", [128, 128], "float16")
     for _k in "uzql":
         SCRATCH["p" + _k + _x] = ("psum", [128, 512], "float32")
 
@@ -41,13 +40,32 @@ SEMAPHORES = ["qv", "qs", "qt", "qg", "loc"] + DMAS
 SEMAPHORES += ["l%d%d%d" % (t, k, x) for t in range(R) for k in range(3) for x in range(2)]
 SEMAPHORES += ["r%d%d%d" % (t, k, x) for t in range(R) for k in range(2) for x in range(2)]
 
-PLAN = dict(cycle=0.83, gather=1.5, scatter=3.8, call=10, wake=170, message=3500, first=3500, dma=3000, lead=3500, passes=2,
-            spiece=256, gpiece=1024, early=(1,))
-BIAS = {"A.L0 s": 15000, "A.L0 v": -5500, "A.second v": 3000, "A.answer v": 3500, "A.pick v": 5500, "A.names v": 6500,
-        "B.first v": 11000, "B.L1 s": 5000, "B.L1help v": 5500, "B.second v": 3000, "B.P0 s": 10000, "B.answer v": 7000,
-        "B.truth v": 9000, "B.pick v": 2500}
+CASES = dict(cycle=(0.83, 0.83, 0.86, 0.89, 1.04, 1.13, 1.16, 1.19, 0.83),
+             gather=(1.29, 1.29, 1.05, 1.54, 0.99, 1.23, 0.86, 1.66, 1.7),
+             scatter=(3.2, 3.7, 3.4, 3.9, 3.9, 3, 4.5, 1.5, 3.2),
+             call=(10, 1, 0, 14, 8, 13, 0, 7, 10),
+             wake=(170, 150, 150, 100, 270, 110, 170, 130, 170),
+             far=(170, 270, 450, 300, 260, 100, 420, 190, 170),
+             message=(2000, 3400, 1600, 2400, 2600, 1900, 2300, 1900, 2000),
+             first=(3000, 4500, 4600, 3000, 4900, 4800, 4200, 2700, 3000),
+             send=(300, 390, 460, 200, 150, 310, 390, 270, 300),
+             dma=(1500, 1700, 1500, 2200, 1600, 2400, 1900, 2000, 1500),
+             local=(3.4, 3.7, 2.7, 4.5, 4.1, 3.8, 3.2, 2.8, 3.4),
+             remote=(17, 11, 13, 23, 16, 19, 14, 31, 17),
+             goal=(148000, 150000, 136000, 172000, 182000, 171000, 171000, 181000, 184000))
+KB = dict(dch=64, dx0=512, dx1=512, dwt=1, dsl=64, dsb=32, dyc=64, dc0=256, dc1=256)
+PLAN = dict(lead=0, passes=2, spare=1000, moves=((0, False, 0), (8000, True, 0), (6000, True, 0.85), (4000, False, 0)), seed=3, heat=0.0001,
+            power=40, spiece=256, early=(), halves=[(t, x) for t in range(R) for x in range(2)], spick=[(3, 0), (3, 1)], snames=[0, 1],
+            swap=[0, 1])
 HELP = {(t, 1, "L1"): 192 for t in range(R)}
+HELP.update({(t, 0, "L0"): 256 for t in range(1, R)})
 HELP.update({(0, 0, "L0"): 1024, (0, 0, "L1"): 512, (R - 1, 1, "P2"): 512})
+ORDER = ["A.L0 B.L0 A.L1 B.L1 A.P0 A.P1 B.P0 A.P2 A.L2 B.P1 B.P2 B.L2",
+         "A.L0 A.P0 A.L1 B.L0 A.P1 B.L1 A.P2 A.L2 B.P0 B.P1 B.P2 B.L2",
+         "A.L0 A.P0 A.L1 B.L0 A.P1 B.L1 A.P2 A.L2 B.P0 B.P1 B.P2 B.L2",
+         "A.L0 A.P0 A.L1 B.L0 A.P1 B.L1 A.P2 B.P0 B.P1 B.P2 A.L2 B.L2"]
+CUTS = {"3B.L2": (1024, 1536, 1792), "3A.L2": (1024, 1536), "3B.P2": (1024, 1536), "3A.P2": (1024, 1536)}
+NOTE = []
 TURN = []
 TAG = [None]
 
@@ -56,7 +74,7 @@ def rank_program(g, core, T, topo):
     rank = T.rank_of(core)
     if rank is None:
         return
-    A, F, P = AluOpType, ActivationFunctionType, PLAN
+    A, F, P = AluOpType, ActivationFunctionType, dict(PLAN, **{k: np.array(v, float) for k, v in CASES.items()})
     N = len(T.cores)
     eng = {"v": g.vector, "s": g.scalar, "t": g.tensor, "g": g, "y": g.sync}
     prog, now = [], {"x": 1, "tag": "", "sent": 0}
@@ -88,13 +106,13 @@ def rank_program(g, core, T, topo):
     def psum(v):
         return SCRATCH[v[1]][0] == "psum"
 
-    def add(q, kind, call, reads, writes, ns, lag=0.0, join=None):
-        prog.append(dict(q=q, kind=kind, call=call, reads=flat(reads), writes=flat(writes), ns=ns, lag=lag, join=join, x=now["x"],
-                         tag=now["tag"]))
+    def add(q, kind, call, reads, writes, ns, lag=None, join=None):
+        prog.append(dict(q=q, kind=kind, call=call, reads=flat(reads), writes=flat(writes), ns=ns + 0 * P["cycle"], lag=lag, join=join,
+                         x=now["x"], tag=now["tag"]))
 
     def vec(call, out, ins, more=(), rate=None):
         if len(ins[0]) == 3:
-            ns = 50 + out[4] * P["gather"] * P["cycle"]
+            ns = 50 + out[4] * P["gather"]
         else:
             if rate is None:
                 rate = 0.5 if all(SCRATCH[v[1]][2] in ("bfloat16", "uint16") for v in [out] + ins) else 1
@@ -122,6 +140,9 @@ def rank_program(g, core, T, topo):
         add("s", "op", lambda: g.scalar.activation(out[0], in_[0], F.Identity, bias, scale), [in_], list(token) or [out],
             60 + max(64, out[4]) * P["cycle"])
 
+    def take(out, in_):
+        add("s", "op", lambda: g.scalar.activation(out[0], in_[0], F.Copy), [in_], [out], 65 + out[4] * P["gather"])
+
     def iota(out, pattern, base, mul):
         add("g", "op", lambda: g.iota(out[0], pattern, base, mul), [], [out], 130 + 2 * out[4] * P["cycle"])
 
@@ -146,11 +167,12 @@ def rank_program(g, core, T, topo):
         mms(out, pairs[-last:], False, True)
 
     def dma(q, sem, pairs, reads, writes):
-        add(q, "dma", (sem, pairs), reads, writes, 60 * len(pairs), P["dma"])
+        add(q, "dma", (sem, pairs), reads, writes, 60 * len(pairs), (P["dma"], KB[sem[:3]] * P["local"]))
 
     def send(dst, src, land, sem, more=()):
-        add("g", "send", (dst, src, land, sem), [src] + list(more), [view(land, src[2], src[3])], 300 if now["sent"] else P["first"],
-            P["message"])
+        kb = src[4] / (4 if land == "inl" else 2)
+        add("g", "send", (dst, src, land, sem), [src] + list(more), [view(land, src[2], src[3])], P["send"] + (0 if now["sent"] else P["first"]),
+            (P["message"], kb * P["remote"]))
         now["sent"] = 1
 
     cols, nxt = {}, {}
@@ -208,15 +230,15 @@ def rank_program(g, core, T, topo):
 
     ones, blk, eye, zb, zf = (whole(n) for n in ("ones", "blk", "eye", "zb", "zf"))
     ip, im, sgn = view("ip", 0, 88), view("im", 0, 88), small("sgn", 112, "smb")
-    c716, c35, last = small("c716", 64, "smb"), small("c35", 16, "smb"), small("last", 16, "smb")
-    for v, c in ((zb, 0.0), (c716, -7.0 / 16), (c35, 3.5), (sub(last, 0, 8), 15.0), (sub(last, 8, 8), 0.0),
+    c716, last = small("c716", 64, "smb"), small("last", 24, "smb")
+    for v, c in ((zb, 0.0), (c716, 7.0 / 16), (last, 0.0), (sub(last, 8, 8), 15.0),
                  (sgn, -1.0), (sub(sgn, 16, 16), 0.0), (sub(sgn, 96, 8), 1.0)):
         fill(v, c)
     act(whole("mkn"), whole("mkx"), -512.0, 512.0)
-    for v, c in ((whole("c13"), 2.0 ** -13), (whole("cp64"), 64.0), (zf, 0.0)):
+    for v, c in ((whole("up"), 1.5 * 2.0 ** 16), (whole("down"), -1.5 * 2.0 ** 16), (whole("c13"), 2.0 ** -13), (whole("cp64"), 64.0), (zf, 0.0)):
         act(v, sub(ones, 0, 128), c)
-    act(whole("shf"), sub(ones, 0, 48), 0.0)
-    for h, c in enumerate((-2.0 ** -7, 2.0 ** -19)):
+    act(whole("shf"), sub(ones, 0, 96), 0.0)
+    for h, c in enumerate((2.0 ** -7, -2.0 ** -19)):
         add("v", "op", lambda h=h, c=c: g.vector.memset(T.chalf[64 * h:64 * h + 64, :], c), [], [whole("chalf")], P["call"] + 64 * P["cycle"])
     pidx, i16, i8, i77 = (small(n, w, "smi") for n, w in (("pidx", 8), ("i16", 16), ("i8", 8), ("i77", 2)))
     mask2, thr = small("mask", 128, "smb"), small("thr", 64, "smb")
@@ -227,7 +249,6 @@ def rank_program(g, core, T, topo):
     iota(i16, [[1, 16]], 0, 0)
     iota(i8, [[16, 8]], 0, 0)
     select(eye, sub(ones, 0, 128), [[-1, 128]], A.is_equal, 0, 1)
-    ts(whole("eyeh"), eye, -1.0, A.mult)
     band(ip, sub(ones, 0, 88), [[0, 11], [16, 8]])
     ts(im, ip, -1.0, A.mult)
     for a, b in ((ip, im), (im, ip)):
@@ -242,11 +263,11 @@ def rank_program(g, core, T, topo):
     select(whole("swp"), zb, [[-1, 128]], A.not_equal, -64, 1, 1.0)
     select(whole("swp"), whole("swp"), [[-1, 128]], A.not_equal, 64, 1, 1.0)
 
-    wti, wi, wf, wb = view("wti", 0, 2), small("wi", 10, "smi"), small("wf", 10), small("wb", 4)
+    wti, wi, wb = view("wti", 0, 2), small("wi", 8, "smi"), small("wb", 4)
     pm, p8 = small("pm", 8, "smi"), small("p8", 8, "smi")
     kc, c01, pf, pk, ph = small("kc", 2), small("c01", 2), small("pf", 1), small("pk", 1), small("ph", 2)
-    bases, mask9, xo, xo2 = small("bases", 24, "smb"), small("mask9", 64, "smb"), small("xo", 8, "smu"), small("xo2", 8, "smu")
-    at16 = sub(bases, 0, 8)
+    bases, mask9, xo, xo2 = small("bases", 32, "smb"), small("mask9", 64, "smb"), small("xo", 8, "smu"), small("xo2", 8, "smu")
+    at16 = sub(bases, 8, 8)
     ts(pm, pidx, 15, A.bitwise_and)
     ts(p8, pidx, 7, A.bitwise_and)
     for h, o in enumerate((A.is_ge, A.is_lt)):
@@ -256,18 +277,19 @@ def rank_program(g, core, T, topo):
     cp(xo, p8)
     ts(c01, i77, pk, A.add, 64.0, A.mult)
     ts(kc, c01, 992.0, A.add)
-    for k, m in enumerate((1984, 3, 2048, 4, 63)):
+    for k, m in enumerate((2047, 3, 2048, 4)):
         ts(sub(wi, 2 * k, 2), wti, m, A.bitwise_and)
-    ts(wf, wi, 2.0 ** -12, A.mult)
-    tt(wb, sub(wf, 0, 4), sub(wf, 4, 4), A.subtract)
-    ts(view("shf", 16, 32), i16, pf, A.is_equal, 4096.0, A.mult)
+    tt(wb, sub(wi, 0, 4), sub(wi, 4, 4), A.subtract)
+    for o, c in ((16, 4096.0), (64, 256.0)):
+        ts(view("shf", o, o + 16), i16, pf, A.is_equal, c, A.mult)
     ts(at16, i8, pf, A.add, 16.0, A.mult)
+    ts(sub(bases, 0, 8), i8, pf, A.add)
     for h in range(2):
-        ts(sub(bases, 8 + 8 * h, 8), at16, 0.5, A.mult, sub(ph, h, 1), A.add)
+        ts(sub(bases, 16 + 8 * h, 8), at16, 0.5, A.mult, sub(ph, h, 1), A.add)
     for x in range(2):
-        ts(whole("wh%d" % x), blk, sub(wb, x, 1), A.mult)
-        ts(whole("wl%d" % x), blk, sub(wf, 8 + x, 1), A.mult)
-        ts(small("w8%d" % x, 64, "smb"), sub(ip, 24, 64), sub(wb, 2 + x, 1), A.mult, 512.0, A.mult)
+        for sign, c in (("p", 1.0), ("m", -1.0)):
+            ts(whole("w%s%d" % (sign, x)), blk, sub(wb, x, 1), A.mult, c / 4096, A.mult)
+            ts(small("w8%s%d" % (sign, x), 64, "smb"), sub(ip, 24, 64), sub(wb, 2 + x, 1), A.mult, c / 8, A.mult)
     ts(mask9, mask, 2.0 ** -9, A.mult)
     ts(sub(mask2, 64, 64), mask, 2.0 ** -12, A.mult)
     cp(sub(xo2, 0, 4), sub(p8, 0, 4))
@@ -281,8 +303,8 @@ def rank_program(g, core, T, topo):
             def make(lo, n):
                 src, dst = ind(table(x), sub(off, lo // 16, n // 16)), view("gb%d" % x, at + lo, at + lo + n)
                 if q == "v":
-                    return lambda: g.vector.tensor_copy(dst[0], src[0]), [src], [dst], 50 + n * P["gather"] * P["cycle"]
-                return lambda: g.scalar.activation(dst[0], src[0], F.Copy), [src], [dst], 65 + n * P["gather"] * P["cycle"]
+                    return lambda: g.vector.tensor_copy(dst[0], src[0]), [src], [dst], 50 + n * P["gather"]
+                return lambda: g.scalar.activation(dst[0], src[0], F.Copy), [src], [dst], 65 + n * P["gather"]
             return make
 
         def scan(least):
@@ -295,11 +317,13 @@ def rank_program(g, core, T, topo):
             return make
         cut = HN - HELP.get((t, x, kind), 0)
         step = now["tag"]
-        for q, make, a, b, n, most, what in (("s", gather("s"), 0, cut, P["gpiece"], HN, ""), ("v", gather("v"), cut, HN, P["spiece"], HN, "help"),
-                                             ("v", scan(False), 0, HN, P["spiece"], MK, ""), ("v", scan(True), 0, HN, P["spiece"], MK, "min")):
+        ends = [c for c in CUTS.get(step, CUTS.get(step[1:], (1024,))) if c < cut] + [cut]
+        pieces = list(range(0, HN + 1, P["spiece"]))
+        for q, make, marks, most, what in (("s", gather("s"), [0] + ends, HN, ""), ("v", gather("v"), [cut] + [c for c in pieces if c > cut], HN, "help"),
+                                           ("v", scan(False), pieces, MK, ""), ("v", scan(True), pieces, MK, "min")):
             now["tag"] = step + what
-            for lo in range(a, b, n):
-                add(q, "op", *make(lo, min(n, b - lo)), join=(make, lo, min(n, b - lo), most))
+            for lo, hi in zip(marks, marks[1:]):
+                add(q, "op", *make(lo, hi - lo), join=(make, lo, hi - lo, most))
 
     def res(buf, x, k):
         return view("%s%d" % (buf, x), k * HN + 15, (k + 1) * HN, 16)
@@ -313,20 +337,19 @@ def rank_program(g, core, T, topo):
         return [(view("slb", o + h * HC, o + (h + 1) * HC, 1, 8), view("esl", (2 * x + h) * 112 + lo, (2 * x + h) * 112 + lo + n, 1, 8))
                 for h in range(2)]
 
-    def shifted(out, r, turn=0):
-        return [(view("shf", 16 - 16 * (b % 2), 48 - 16 * (b % 2)), view(r[1], r[2] + (b + 4 * turn) % 8, r[3], 8),
+    def shifted(out, r, turn=0, less=0):
+        return [(view("shf", 48 * less + 16 - 16 * (b % 2), 48 * less + 48 - 16 * (b % 2)), view(r[1], r[2] + (b + 4 * turn) % 8, r[3], 8),
                  view(out[1], out[2], out[3], 1, 32, 32 * (b // 2))) for b in range(8)]
+
+    def rounding(n):
+        return [(whole("up"), sub(ones, 0, n)), (whole("down"), sub(ones, 0, n))]
 
     def product(x, k, h):
         lo, n = (0, HC) if h is None else (64 * h, 64)
         y = half(res("mx", x, k), h)
-        hi, uc = view("hi%d" % x, lo, lo + n), view("uc%d" % x, HC * k + lo, HC * k + lo + n)
-        low, v = view("pu%d" % x, lo, lo + n), view("pq%d" % x, HC + lo, HC + lo + n)
-        weigh = [(whole("wh%d" % x), y), (whole("wl%d" % x), y)]
-        grouped(low, [(whole("chalf"), sub(ones, 0, n))] + weigh, 2)
-        mms(v, [(whole("c13"), sub(ones, 0, n))] + weigh, True, False)
-        ts(hi, low, 1.5 * 2.0 ** 23, A.add, -1.5 * 2.0 ** 23, A.add)
-        mms(v, [(whole("eyeh"), hi)], False, True)
+        uc, v = view("uc%d" % x, HC * k + lo, HC * k + lo + n), view("pq%d" % x, HC, HC + n) if h else view("pu%d" % x, 0, n)
+        one = sub(ones, 0, n)
+        grouped(v, [(whole("chalf"), one), (whole("wm%d" % x), y)] + rounding(n) + [(whole("c13"), one), (whole("wp%d" % x), y)], 5)
         tt(uc, v, sub(names(x, k), lo, n), A.mult)
         return uc
 
@@ -361,7 +384,7 @@ def rank_program(g, core, T, topo):
         tag("L0")
         look(t, x, "L0")
         tag("first")
-        for h in range(2):
+        for h in range(2) if (t, x) in P["halves"] else (None,):
             propose(t, x, 0, product(x, 0, h), h)
         send_list(t, 1, x)
         tag("L1")
@@ -397,16 +420,15 @@ def rank_program(g, core, T, topo):
         tag("decide")
         w2 = view("pu%d" % x, 128, 144)
         grouped(w2, slack(t, 1, x, 96, 16) + cut(rise[0], 16, 16) + [(whole("em2"), x12), (whole("beye"), ne0)] + cut(rise[2], 16, 16), 2)
-        fv, no, fy = sv("fv", 24, "smu"), sv("no", 8, "smu"), view("fy%d" % x, 0, HC)
-        fo, vo, d0 = sub(fv, 0, 8), sub(fv, 8, 8), sub(hd, 32, 8)
+        fv, fy = sv("fv", 32, "smu"), view("fy%d" % x, 0, HC)
+        no, fo, vo, d0 = sub(fv, 0, 8), sub(fv, 8, 8), sub(fv, 16, 8), sub(hd, 32, 8)
         early = t == R - 1 and x in P["early"]
         if early:
-            u3, ui, xa, xb, d1 = view("pl%d" % x, 16, 40), small("ui", 24, "smi"), small("xa", 16), small("xb", 16), small("d1", 16)
+            u3, ui, xa, xb, d1 = view("pl%d" % x, 16, 40), small("ui", 24), small("xa", 16), small("xb", 16), small("d1", 16)
             ra, rb, rc = (small(n, 128, "smb") for n in ("ra", "rb", "rc"))
-            for k in range(3):
-                mms(sub(u3, 8 * k, 8), [(res("mx", x, k), sv("w8", 8, "smb"))])
+            weigh = [[(res("mx", x, k), sv(w, 8, "smb"), sub(u3, 8 * k, 8)) for k in range(3)] for w in ("w8m", "w8p")]
+            grouped(u3, [(eye, sub(c716, 0, 24))] + weigh[0] + rounding(24) + weigh[1] + [(eye, sub(zb, 0, 24))], 7)
             ts(ui, u3, 8.0, A.mult)
-            ts(ui, ui, 7, A.bitwise_and)
             cp(sub(xa, 0, 8), d0)
             ts(sub(xb, 0, 8), d0, 2.0, A.mult)
             tt(sub(xb, 8, 8), sub(ui, 8, 8), sub(ui, 0, 8), A.subtract)
@@ -418,21 +440,23 @@ def rank_program(g, core, T, topo):
             tt(rb, ind(xb, xo2), mask2, A.mult)
             tt(d1, w2, spans(t, 1, x, "rin", True), A.is_lt)
             tt(rc, ind(sub(d1, 8, 8), xo), rb, A.mult)
-            at = view("pl%d" % x, 40, 56)
-            grouped(at, [(eye, sub(bases, 0, 16))] + shifted(at, ra) + shifted(at, rc) + [(eye, last)], 9)
+            at = view("pl%d" % x, 40, 64)
+            moves = [shifted(sub(at, 8, 16), v) + shifted(sub(at, 0, 8), sub(v, 0, 64), 0, 1) for v in (ra, rc)]
+            grouped(at, [(eye, sub(bases, 0, 24))] + moves[0] + moves[1] + [(eye, last)], 17)
             tag("pick")
-            cp(sub(fv, 0, 16), at)
+            cp(sub(fv, 0, 24), at)
         else:
             tt(view(both[1], both[2] + x, both[3], 2), w2, spans(t, 1, x, "rin", True), A.is_lt)
             tt(sel, view(both[1], both[2] + 16 + x, both[3], 2), d0, A.max)
             tt(r, ind(sel, sub(xo, 0, 4)), mask, A.mult)
-            at = view("pl%d" % x, 8, 16)
-            grouped(at, [(eye, at16)] + shifted(at, r) + [(eye, sub(last, 0, 8))], 9)
+            at = view("pl%d" % x, 8, 24)
+            moves = shifted(sub(at, 8, 8), r) + shifted(sub(at, 0, 8), r, 0, 1)
+            grouped(at, [(eye, sub(bases, 0, 16))] + moves + [(eye, sub(last, 0, 16))], 17)
             tag("pick")
-            cp(fo, at)
-        cp(fy, ind(view("mx%d" % x, 0, 3 * HN), fo))
+            cp(sub(fv, 0, 16), at)
+        pick = take if (t, x) in P["spick"] else cp
+        pick(fy, ind(view("mx%d" % x, 0, 3 * HN), fo))
         tag("names")
-        ts(no, fo, 15.0, A.subtract, 1.0 / 16, A.mult)
         picked = ind(view("nw%d" % x, 0, 3 * HC), no)
         if t < R - 1:
             cp(lists(t + 1, 0, x), picked)
@@ -440,23 +464,21 @@ def rank_program(g, core, T, topo):
             cp(names(x, 0), lists(t + 1, 0, x))
         else:
             y = view("uc%d" % x, 0, HC)
-            cp(y, picked)
+            (take if x in P["snames"] else cp)(y, picked)
             dma("y", "dyc%d" % x, [(T.yc[64 * x:64 * x + 64, h * HC:(h + 1) * HC], part(y, h)[0]) for h in range(2)], [y], [])
         tag("update")
         tab, xs, xh = table(x), view("xs%d" % x, 0, HC), view("xs%d" % x, HC, 2 * HC)
+        swap = t < R - 1 and x in P["swap"]
         if not early:
-            u8, rest, q8, at = view("pu%d" % x, 192, 256), view(z, 128, 192), view("hi%d" % x, 0, 64), view("pl%d" % x, 16, 24)
-            grouped(u8, [(eye, c716), (fy, sv("w8", 64, "smb"))], 1)
-            mms(rest, [(eye, c716), (fy, sv("w8", 64, "smb"))], True, False)
-            ts(q8, u8, 1.5 * 2.0 ** 23, A.add, -1.5 * 2.0 ** 23, A.add)
-            mms(rest, [(whole("eyeh"), q8)], False, True)
+            rest = view(z, 128, 192)
+            grouped(rest, [(eye, c716), (fy, sv("w8m", 64, "smb"))] + rounding(64) + [(fy, sv("w8p", 64, "smb"))], 4)
             tt(r, rest, mask9, A.mult)
-            n = 2 if t < R - 1 else 1
-            at, vo = view("pl%d" % x, 16, 16 + 8 * n), sub(fv, 8, 8 * n)
+            n = 2 if swap else 1
+            at, vo = view("pl%d" % x, 24, 24 + 8 * n), sub(fv, 16, 8 * n)
             moves = [m for h in range(n) for m in shifted(sub(at, 8 * h, 8), r, h)]
-            grouped(at, [(eye, sub(bases, 8, 8 * n))] + moves + [(eye, sub(c35, 0, 8 * n))], 8 * n + 1)
+            grouped(at, [(eye, sub(bases, 16, 8 * n))] + moves + [(eye, sub(zb, 0, 8 * n))], 8 * n + 1)
             cp(vo, at)
-        if t < R - 1:
+        if swap:
             old, xh = view("old%d" % x, 0, HC), whole("xs%d" % x)
             cp(old, ind(tab, sub(vo, 0, 8)))
             for h, turn in enumerate((eye, whole("swp"))):
@@ -466,9 +488,11 @@ def rank_program(g, core, T, topo):
             tt(xs, ind(tab, vo), fy, A.add)
             ts(xh, xs, 1, A.arith_shift_right)
         out = ind(tab, vo)
-        add("v", "op", lambda: g.vector.tensor_copy(out[0], xh[0]), [xh, vo], [tab], 50 + xh[4] * P["scatter"] * P["cycle"])
+        add("v", "op", lambda: g.vector.tensor_copy(out[0], xh[0]), [xh, vo], [tab], 50 + xh[4] * P["scatter"])
         if t == R - 1:
             dma("y", "dc%d" % x, [(T.yx[64 * x:64 * x + 64, 1024 * h:1024 * (h + 1)], part(half(tab, h), h)[0]) for h in range(2)], [tab], [])
+        elif not swap:
+            dma("y", "dc%d" % x, [(part(half(tab, h), 1 - h)[0], part(half(tab, h), h)[0]) for h in range(2)], [tab], [tab])
 
     for t in range(R):
         if t:
@@ -478,11 +502,24 @@ def rank_program(g, core, T, topo):
             now["x"] = x
             stream(t, x)
 
-    issue(g, T, topo, core, eng, plan(prog), {"inl": asker, "rin": partner})
+    issue(g, T, topo, core, eng, plan(prog, P), {"inl": asker, "rin": partner})
 
 
-def plan(prog):
-    P, n = PLAN, len(prog)
+def plan(prog, P):
+    if not TURN:
+        TURN.extend(arrange(prog, P))
+    out = []
+    for parts in TURN:
+        o = dict(prog[parts[0]])
+        if len(parts) > 1:
+            o.update(call=o["join"][0](o["join"][1], sum(prog[i]["join"][2] for i in parts))[0],
+                     reads=[v for i in parts for v in prog[i]["reads"]], writes=[v for i in parts for v in prog[i]["writes"]])
+        out.append(o)
+    return out
+
+
+def arrange(prog, P):
+    n = len(prog)
     pred, acc, last = [set() for _ in prog], {}, {}
     for i, o in enumerate(prog):
         for vs, w in ((o["reads"], False), (o["writes"], True)):
@@ -501,62 +538,178 @@ def plan(prog):
             if bank in last:
                 pred[i].add(last[bank])
             last[bank] = i
+    above = [0] * n
+    for i in range(n):
+        pred[i] = sorted(j for j in pred[i] if not any(above[k] >> j & 1 for k in pred[i]))
+        for j in pred[i]:
+            above[i] |= above[j] | 1 << j
     succ = [[] for _ in prog]
     for i in range(n):
         for j in pred[i]:
             succ[j].append(i)
-    rank = [0.0] * n
-    for i in range(n - 1, -1, -1):
-        rank[i] = prog[i]["ns"] + prog[i]["lag"] + max([P["wake"] + rank[j] for j in succ[i]], default=0.0)
+    true = [list(v) for v in pred], [list(v) for v in succ]
+    steps = ["%d%s" % (t, w) for t in range(R) for w in ORDER[t].split()]
+    looks = sorted((steps.index(o["tag"]), i) for i, o in enumerate(prog) if o["q"] == "s" and o["join"])
+    for (_, i), (_, j) in zip(looks, looks[1:]):
+        pred[j].append(i)
+        succ[i].append(j)
+    turn, left = [i for i in range(n) if not pred[i]], [len(v) for v in pred]
+    for i in turn:
+        for j in succ[i]:
+            left[j] -= 1
+            turn += [] if left[j] else [j]
+    ns, lag = [float(o["ns"][0]) for o in prog], [float(sum(o["lag"])[0]) + P["spare"] if o["lag"] else 0.0 for o in prog]
+    wake, rank = float(P["wake"][0]), [0.0] * n
+    for i in turn[::-1]:
+        rank[i] = ns[i] + lag[i] + max([(prog[j]["q"] != "s" or prog[i]["q"] != "s") * wake + rank[j] for j in succ[i]], default=0.0)
 
     def place(turn, first, back):
         at, gaps = [0.0] * n, {q: [[0.0, 1e12]] for q in "vstgy"}
         for i in turn:
-            o = prog[i]
-            t = max([at[j] + prog[j]["ns"] + P["wake"] + (0 if back else prog[j]["lag"]) for j in first[i]], default=0.0)
-            t += o["lag"] if back else 0
-            gs = gaps[o["q"]]
+            t = max([at[j] + ns[j] + (prog[j]["q"] != "s" or prog[i]["q"] != "s") * wake + (0 if back else lag[j]) for j in first[i]], default=0.0)
+            t += lag[i] if back else 0
+            gs = gaps[prog[i]["q"]]
             k = len(gs) - 1
             while k > 0 and gs[k - 1][1] > t:
                 k -= 1
-            while gs[k][1] - max(gs[k][0], t) < o["ns"]:
+            while gs[k][1] - max(gs[k][0], t) < ns[i]:
                 k += 1
             lo, hi = gs[k]
             at[i] = max(lo, t)
-            gs[k:k + 1] = [x for x in ([lo, at[i]], [at[i] + o["ns"], hi]) if x[1] - x[0] > 40]
+            gs[k:k + 1] = [x for x in ([lo, at[i]], [at[i] + ns[i], hi]) if x[1] - x[0] > 40]
         return at
 
-    if not TURN:
-        lead = [rank[i] + P["lead"] * (o["x"] == 0) + BIAS.get(o["tag"][1:] + " " + o["q"], 0)
-                for i, o in enumerate(prog)]
-        for i in range(n - 1, -1, -1):
-            lead[i] = max([lead[i]] + [lead[j] + 1 for j in succ[i]])
-        turn, best = sorted(range(n), key=lambda i: -lead[i]), None
-        for _ in range(P["passes"]):
-            at = place(turn, pred, False)
-            end = max(at[i] + prog[i]["ns"] + prog[i]["lag"] for i in range(n))
-            if best is None or end < best:
-                best = end
-                TURN[:] = [at, end]
-            late = place(sorted(range(n), key=lambda i: -(at[i] + prog[i]["ns"] + prog[i]["lag"])), succ, True)
-            turn = sorted(range(n), key=lambda i: -(late[i] + prog[i]["ns"]))
-    start = TURN[0]
-    order = sorted((start[i], i) for i in range(n))
-    done = [start[i] + prog[i]["ns"] + prog[i]["lag"] for i in range(n)]
-    ready = [max([done[j] + P["wake"] for j in pred[i]], default=0.0) for i in range(n)]
-    out, tail = [], {}
-    for at, i in order:
-        o, t = prog[i], tail.get(prog[i]["q"])
-        if t and o["join"] and t["join"] and t["join"][0] is o["join"][0] and sum(t["join"][1:3]) == o["join"][1] and ready[i] <= t["at"] \
-                and t["join"][2] + o["join"][2] <= o["join"][3] and all(start[j] >= done[i] for k in t["parts"] for j in succ[k]):
-            make, lo, m = t["join"][0], t["join"][1], t["join"][2] + o["join"][2]
-            call, reads, writes, _ = make(lo, m)
-            t.update(call=call, join=(make, lo, m), parts=t["parts"] + [i], reads=t["reads"] + o["reads"], writes=t["writes"] + o["writes"])
-        else:
-            t = dict(o, at=at, parts=[i])
-            tail[o["q"]] = t
-            out.append(t)
-    return out
+    lead = [rank[i] + (0 if o["join"] else P["lead"]) for i, o in enumerate(prog)]
+    for i in turn[::-1]:
+        lead[i] = max([lead[i]] + [lead[j] + 1 for j in succ[i]])
+    turn, best = sorted(range(n), key=lambda i: -lead[i]), None
+    for _ in range(P["passes"]):
+        at = place(turn, pred, False)
+        end = max(at[i] + ns[i] + lag[i] for i in range(n))
+        if best is None or end < best:
+            best, start = end, at
+        late = place(sorted(range(n), key=lambda i: -(at[i] + ns[i] + lag[i])), succ, True)
+        turn = sorted(range(n), key=lambda i: -(late[i] + ns[i]))
+    return improve(prog, P, true[0], true[1], [i for _, i in sorted((start[i], i) for i in range(n))])
+
+
+def improve(prog, P, pred, succ, order):
+    n, rng = len(prog), np.random.default_rng(P["seed"])
+    q, ns, lag, join = ([o[k] for o in prog] for k in ("q", "ns", "lag", "join"))
+    wake = [P["far"] if o["kind"] == "send" else P["wake"] for o in prog]
+    banks = [{v[1] for v in o["reads"] + o["writes"] if SCRATCH[v[1]][0] == "psum"} for o in prog]
+    parts, zero = [[i] for i in range(n)], 0 * P["cycle"]
+    load, glue, begin = P["goal"], [True], {"v": P["call"], "s": 65}
+
+    def follows(i, j):
+        return join[i] and join[j] and join[j][0] is join[i][0] and join[i][1] + join[i][2] == join[j][1] and join[i][2] + join[j][2] <= join[i][3]
+
+    def run(order, first, old):
+        start, end, ready, gate = (list(v) for v in old[:4])
+        tail, last = {}, None
+        for i in order[:first]:
+            tail[q[i]] = i
+            for b in banks[i]:
+                tail[b] = i
+        for i in order[:first][::-1]:
+            if lag[i]:
+                last = i
+                break
+        for i in order[first:]:
+            e = q[i]
+            j = tail.get(e)
+            t = zero if j is None else end[j]
+            waits = [j for j in pred[i] if e != "t" or q[j] != "t"]
+            for b in banks[i]:
+                k = tail.get(b)
+                if k is not None and q[k] != e:
+                    waits.append(k)
+                tail[b] = i
+            for k in waits:
+                t = np.maximum(t, ready[k])
+            start[i], gate[i], tail[e] = t, (j, waits), i
+            end[i] = t = t + (ns[i] - begin[e] if glue[0] and join[i] and j is not None and follows(j, i) else ns[i])
+            if lag[i]:
+                t = t + lag[i][0]
+                if last is not None:
+                    t = np.maximum(t, ready[last] - wake[last])
+                t, last = t + lag[i][1], i
+            ready[i] = t + wake[i]
+        final = [i for i in order[-40:] if not succ[i]]
+        time = np.max([ready[i] for i in final], 0)
+        return start, end, ready, gate, time, float(np.sum((time / load) ** P["power"])), final
+
+    def shift(order, a, b):
+        lo, hi, rel = (b, a, pred) if b < a else (a, b, succ)
+        drag = {order[a]}
+        for i in (order[lo:hi + 1][::-1] if b < a else order[lo:hi + 1]):
+            if i in drag:
+                drag.update(rel[i])
+        mine, rest = [i for i in order[lo:hi + 1] if i in drag], [i for i in order[lo:hi + 1] if i not in drag]
+        return order[:lo] + (mine + rest if b < a else rest + mine) + order[hi + 1:], lo
+
+    now = [[None] * n] * 4
+    for moves, glue[0], since in P["moves"]:
+        chain = None
+        now = run(order, 0, now)
+        for step in range(moves):
+            start, end, ready, gate, time, worth, final = now
+            if chain is None or step % 16 == 0:
+                weight = (time / load) ** P["power"]
+                c = int(rng.choice(len(load), p=weight / weight.sum()))
+                at = {i: k for k, i in enumerate(order)}
+                i, chain = max(final, key=lambda i: ready[i][c]), []
+                while i is not None and at[i] >= since * len(order):
+                    j, waits = gate[i]
+                    idle = j is None or end[j][c] < start[i][c] - 1
+                    chain.append((i, j, idle))
+                    i = max(waits, key=lambda k: ready[k][c], default=None) if idle else j
+                chain = [x for x in chain if x[1] is not None and (x[2] or gate[x[1]][0] is None or rng.random() < 0.3 or not join[x[0]])]
+            i, j, idle = chain[rng.integers(len(chain))]
+            same = [k for k in order[max(0, at[i] - 60):at[i] + 120] if q[k] == q[i]]
+            me = same.index(i)
+            if idle and me + 1 < len(same):
+                a, b = at[same[me + 1 + int(rng.integers(min(24, len(same) - me - 1)))]], at[i]
+            elif rng.random() < 0.5 or me + 1 == len(same):
+                a, b = at[i], at[same[max(0, me - 1 - int(rng.integers(6)))]]
+            else:
+                a, b = at[same[max(0, me - 1 - int(rng.integers(3)))]], at[same[me + int(rng.integers(min(4, len(same) - me)))]]
+            if a == b:
+                continue
+            other, first = shift(order, a, b)
+            new = run(other, first, now)
+            if new[5] <= worth * (1 + P["heat"] * (1 - step / moves) * rng.random()):
+                order, now, chain = other, new, None
+        k, glue[0] = 0, False
+        now = run(order, 0, now)
+        while k < len(order):
+            i = order[k]
+            j = next((j for j in order[k + 1:] if q[j] == q[i]), None) if join[i] else None
+            k += 1
+            if j is None or not follows(i, j):
+                continue
+            for a, b in ((order.index(j), k), (k - 1, order.index(j) - 1)):
+                other, first = shift(order, a, b) if a != b else (order, k - 1)
+                if other.index(j) != other.index(i) + 1:
+                    continue
+                keep = ns[i], join[i], pred[i], succ[i]
+                ns[i], join[i] = join[i][0](join[i][1], join[i][2] + join[j][2])[3], (join[i][0], join[i][1], join[i][2] + join[j][2], join[i][3])
+                pred[i], succ[i] = sorted(set(pred[i] + pred[j]) - {i}), sorted(set(succ[i] + succ[j]) - {j})
+                for m in succ[j]:
+                    pred[m] = [i if z == j else z for z in pred[m]]
+                other = [z for z in other if z != j]
+                new = run(other, min(first, other.index(i)), now)
+                if new[5] <= now[5]:
+                    for m in pred[j]:
+                        succ[m] = [i if z == j else z for z in succ[m]]
+                    parts[i] += parts[j]
+                    order, now, k = other, new, other.index(i)
+                    break
+                for m in succ[j]:
+                    pred[m] = [z for z in pred[m] if z != i or m in keep[3]] + [j]
+                ns[i], join[i], pred[i], succ[i] = keep
+    NOTE[:] = [now[4], load]
+    return [parts[i] for i in order]
 
 
 def issue(g, T, topo, core, eng, calls, sender):
@@ -598,8 +751,7 @@ def issue(g, T, topo, core, eng, calls, sender):
                 lst = acc.setdefault(v[1], [])
                 if region(v)[3]:
                     lst[:] = [a for a in lst if a[3] == q]
-                if w:
-                    lst[:] = [a for a in lst if not (v[2] <= a[0] and a[1] <= v[3])]
+                lst[:] = [a for a in lst if not (v[2] <= a[0] and a[1] <= v[3] and (w or a[4] == sem and not a[2]))]
                 lst.append((v[2], v[3], w, q, sem, val, ck))
 
     for o in calls:

@@ -8,23 +8,25 @@ BIG = 65536.0
 KINDS = ("L0", "P0", "L1", "P1", "L2", "P2")
 
 SCRATCH = {
-    "mkx": ("sbuf", [128, MK], "bfloat16"), "mkn": ("sbuf", [128, MK], "bfloat16"),
+    "ramp": ("sbuf", [128, HN], "float16"), "rmp": ("sbuf", [128, 256], "bfloat16"), "mkx": ("sbuf", [128, MK], "bfloat16"), "mkn": ("sbuf", [128, MK], "bfloat16"),
     "outl": ("sbuf", [128, R * 6 * HC], "uint16"), "inl": ("sbuf", [128, R * 6 * HC], "uint16"),
-    "ro": ("sbuf", [128, R * 128], "float32"), "rin": ("sbuf", [128, R * 128], "float32"),
+    "ro": ("sbuf", [128, R * 144], "float32"), "rin": ("sbuf", [128, R * 144], "float32"),
     "wti": ("sbuf", [128, 2], "int32"), "sli": ("sbuf", [128, 128], "int32"),
     "slc": ("sbuf", [128, 128], "bfloat16"), "slb": ("sbuf", [128, 2048], "bfloat16"),
     "sm": ("sbuf", [128, 640], "float32"), "smi": ("sbuf", [128, 512], "int32"), "smb": ("sbuf", [128, 1536], "bfloat16"),
-    "smu": ("sbuf", [128, 128], "uint16"), "esl": ("sbuf", [128, 448], "bfloat16"), "shf": ("sbuf", [128, 96], "bfloat16"),
+    "smu": ("sbuf", [128, 128], "uint16"), "esl": ("sbuf", [128, 448], "bfloat16"), "shf": ("sbuf", [128, 144], "bfloat16"),
 }
-for _k in ("ones", "blk", "eye", "c13", "chalf", "cp64", "zb", "beye", "ip", "im", "swp", "old0", "old1", "up", "down"):
+for _k in ("ones", "blk", "eye", "c13", "chalf", "cp64", "zb", "beye", "ip", "im", "swp", "old0", "old1", "up", "down", "meye", "e512"):
     SCRATCH[_k] = ("sbuf", [128, 128], "bfloat16")
-for _k in ("zf", "eyef", "em2"):
+for _k in ("zf", "em2"):
     SCRATCH[_k] = ("sbuf", [128, 128], "float32")
 for _x in "01":
     SCRATCH["tab" + _x] = ("sbuf", [128, 2048], "bfloat16")
     for _k in ("mx", "mn", "px", "pn"):
-        SCRATCH[_k + _x] = ("sbuf", [128, 3 * HN], "bfloat16")
-    SCRATCH["gb" + _x] = ("sbuf", [128, 6 * HN], "bfloat16")
+        SCRATCH[_k + _x] = ("sbuf", [128, 3 * HN], "bfloat16" if _k[0] == "m" else "float16")
+    SCRATCH["gb" + _x] = ("sbuf", [128, 6 * HN], "float16")
+    SCRATCH["lx" + _x] = SCRATCH["ln" + _x] = ("sbuf", [128, HN], "float16")
+    SCRATCH["hx" + _x] = ("sbuf", [128, 2 * HC], "float32")
     SCRATCH["nw" + _x] = ("sbuf", [128, 3 * HC], "int32")
     SCRATCH["ud" + _x] = ("sbuf", [128, HC], "int32")
     SCRATCH["uc" + _x] = ("sbuf", [128, 2 * HC], "float32")
@@ -34,37 +36,56 @@ for _x in "01":
     SCRATCH["wm" + _x] = ("sbuf", [128, 128], "float16")
     for _k in "uzql":
         SCRATCH["p" + _k + _x] = ("psum", [128, 512], "float32")
+BATCHES = [""] * R
+SIZES = set()
+for _t, _b in enumerate(BATCHES):
+    for _w in ("A.P0", "A.P2", "B.P0", "B.P2"):
+        SIZES.add(([1] + [_v.count("+") + 1 for _v in _b.split() if _w in _v])[-1])
+    for _s, _v in enumerate(_b.split()):
+        _n = _v.count("+") + 1
+        SCRATCH["gq%d%d" % (_n, _s)] = ("sbuf", [128, 8 * _n, 2, 128], "float16")
+        for _k in "xn":
+            SCRATCH["q%s%d%d" % (_k, _n, _s)] = ("sbuf", [128, 1024 * _n], "float16")
+SIZES = sorted(SIZES)
+for _n in SIZES:
+    SCRATCH["eyef%d" % _n] = ("sbuf", [128, 128], "float32")
 
 DMAS = ["dch0", "dch1", "dwt", "dsl", "dsb", "dx0", "dx1", "dc0", "dc1", "dyc0", "dyc1"]
+DMAS += ["da%d%d%d" % (x, k, j) for x in range(2) for k in range(4) for j in range(2)] + ["drm", "dsw"]
 SEMAPHORES = ["qv", "qs", "qt", "qg", "loc"] + DMAS
 SEMAPHORES += ["l%d%d%d" % (t, k, x) for t in range(R) for k in range(3) for x in range(2)]
 SEMAPHORES += ["r%d%d%d" % (t, k, x) for t in range(R) for k in range(2) for x in range(2)]
 
-CASES = dict(cycle=(0.83, 0.83, 0.86, 0.89, 1.04, 1.13, 1.16, 1.19, 0.83),
-             gather=(1.29, 1.29, 1.05, 1.54, 0.99, 1.23, 0.86, 1.66, 1.7),
-             scatter=(3.2, 3.7, 3.4, 3.9, 3.9, 3, 4.5, 1.5, 3.2),
-             call=(10, 1, 0, 14, 8, 13, 0, 7, 10),
-             wake=(170, 150, 150, 100, 270, 110, 170, 130, 170),
-             far=(170, 270, 450, 300, 260, 100, 420, 190, 170),
-             message=(2000, 3400, 1600, 2400, 2600, 1900, 2300, 1900, 2000),
-             first=(3000, 4500, 4600, 3000, 4900, 4800, 4200, 2700, 3000),
-             send=(300, 390, 460, 200, 150, 310, 390, 270, 300),
-             dma=(1500, 1700, 1500, 2200, 1600, 2400, 1900, 2000, 1500),
-             local=(3.4, 3.7, 2.7, 4.5, 4.1, 3.8, 3.2, 2.8, 3.4),
-             remote=(17, 11, 13, 23, 16, 19, 14, 31, 17),
-             goal=(148000, 150000, 136000, 172000, 182000, 171000, 171000, 181000, 184000))
-KB = dict(dch=64, dx0=512, dx1=512, dwt=1, dsl=64, dsb=32, dyc=64, dc0=256, dc1=256)
-PLAN = dict(lead=0, passes=2, spare=1000, moves=((0, False, 0), (8000, True, 0), (6000, True, 0.85), (4000, False, 0)), seed=3, heat=0.0001,
-            power=40, spiece=256, early=(), halves=[(t, x) for t in range(R) for x in range(2)], spick=[(3, 0), (3, 1)], snames=[0, 1],
+CASES = dict(cycle=(0.83, 0.83, 0.86, 0.89, 1.04, 1.13, 1.16, 1.19, 0.83, 1.245, 1.2, 1.1),
+             gather=(1.29, 1.29, 1.05, 1.54, 0.99, 1.23, 0.86, 1.66, 1.7, 1.73, 1.5, 1.8),
+             scatter=(3.2, 3.7, 3.4, 3.9, 3.9, 3, 4.5, 1.5, 3.2, 5, 4, 4),
+             call=(16, 14, 16, 18, 17, 20, 18, 20, 14, 20, 20, 18),
+             wake=(170, 150, 150, 100, 270, 110, 170, 130, 170, 200, 200, 200),
+             far=(170, 270, 450, 300, 260, 100, 420, 190, 170, 300, 300, 450),
+             message=(2000, 3400, 1600, 2400, 2600, 1900, 2300, 1900, 2000, 2400, 2400, 3400),
+             first=(3000, 4500, 4600, 3000, 4900, 4800, 4200, 2700, 3000, 4000, 4000, 4000),
+             send=(300, 390, 460, 200, 150, 310, 390, 270, 300, 350, 350, 450),
+             dma=(1500, 1700, 1500, 2200, 1600, 2400, 1900, 2000, 1500, 2000, 2400, 2400),
+             local=(3.4, 3.7, 2.7, 4.5, 4.1, 3.8, 3.2, 2.8, 3.4, 4.2, 4.5, 4.5),
+             remote=(17, 11, 13, 23, 16, 19, 14, 31, 17, 18, 25, 30),
+             adds=(1.3, 1.3, 1.4, 1.2, 1.3, 1.4, 1.5, 1.5, 1.3, 1.5, 1.6, 1.5),
+             gdma=(800, 900, 1000, 700, 700, 900, 900, 1000, 800, 1100, 1200, 1200),
+             goal=(143300, 151500, 137000, 167000, 174000, 170800, 174000, 180300, 178000, 197000, 192500, 199500))
+KB = dict(dsw=64, drm=448, dch=64, dx0=512, dx1=512, dwt=1, dsl=64, dsb=32, dyc=64, dc0=256, dc1=256)
+PLAN = dict(aim=0.6, ramped=False, both=0, behind={},
+            lift={"A.P0": (), "A.P1": (), "B.P0": (1024,), "3A.P2": (1024,), "0A.P1": (-1024,)}, ahead=0,
+            deal=(1, 40, (0.7, 0.3) + (0,) * 10), lead=0, passes=4, spare=1000,
+            moves=((7000, True, 0), (10000, True, 0), (3000, True, 0.85), (7000, False, 0), (28000, False, 0), (5000, False, 0.85)), seed=9, heat=0.0001,
+            power=40, spiece=256, early=((3, 1),), halves=[(t, x) for t in range(R) for x in range(2)], spick=[(3, 0), (3, 1)], snames=[0, 1],
             swap=[0, 1])
-HELP = {(t, 1, "L1"): 192 for t in range(R)}
-HELP.update({(t, 0, "L0"): 256 for t in range(1, R)})
-HELP.update({(0, 0, "L0"): 1024, (0, 0, "L1"): 512, (R - 1, 1, "P2"): 512})
-ORDER = ["A.L0 B.L0 A.L1 B.L1 A.P0 A.P1 B.P0 A.P2 A.L2 B.P1 B.P2 B.L2",
-         "A.L0 A.P0 A.L1 B.L0 A.P1 B.L1 A.P2 A.L2 B.P0 B.P1 B.P2 B.L2",
-         "A.L0 A.P0 A.L1 B.L0 A.P1 B.L1 A.P2 A.L2 B.P0 B.P1 B.P2 B.L2",
-         "A.L0 A.P0 A.L1 B.L0 A.P1 B.L1 A.P2 B.P0 B.P1 B.P2 A.L2 B.L2"]
-CUTS = {"3B.L2": (1024, 1536, 1792), "3A.L2": (1024, 1536), "3B.P2": (1024, 1536), "3A.P2": (1024, 1536)}
+HELP = {(t, x, k): n for t in (1, 2) for x, k, n in ((0, "P0", 256), (0, "P1", 256), (0, "P2", 512), (1, "P0", 512))}
+HELP.update({(0, x, k): n for x, k, n in ((0, "L0", 768), (0, "P0", 512), (0, "P1", 512), (1, "P0", 512), (1, "P2", 256))})
+HELP.update({(3, x, k): n for x, k, n in ((1, "L0", 256), (1, "L1", 256), (0, "P1", 256), (0, "P2", 256), (1, "P0", 512), (1, "P1", 512))})
+ORDER = ["A.L0 B.L0 A.L1 B.L1 A.P0 A.P1 A.P2 B.P0 A.L2 B.P1 B.P2 B.L2",
+         "A.L0 A.P0 A.L1 B.L0 A.P1 B.L1 A.P2 B.P0 A.L2 B.P1 B.P2 B.L2",
+         "A.L0 A.P0 A.L1 B.L0 A.P1 B.L1 A.P2 B.P0 A.L2 B.P1 B.P2 B.L2",
+         "A.L0 A.P0 A.L1 B.L0 A.P1 B.L1 B.P0 A.P2 B.P1 B.P2 A.L2 B.L2"]
+CUTS = {"3B.L2": (1024, 1536, 1792), "A.P0": (), "A.P1": (), "B.L2": (1280,), "A.P2": (), "0A.P1": (1024,)}
 NOTE = []
 TURN = []
 TAG = [None]
@@ -80,7 +101,7 @@ def rank_program(g, core, T, topo):
     prog, now = [], {"x": 1, "tag": "", "sent": 0}
 
     def view(name, lo, hi, step=1, parts=128, first=0):
-        return (T[name][first:first + parts, lo:hi:step], name, lo, hi, (hi - lo + step - 1) // step, step, parts)
+        return (T[name][first:first + parts, lo:hi:step], name, lo, hi, (hi - lo + step - 1) // step, step, parts, None)
 
     def sub(v, lo, n):
         return view(v[1], v[2] + lo, v[2] + lo + n)
@@ -93,6 +114,9 @@ def rank_program(g, core, T, topo):
 
     def part(v, h):
         return view(v[1], v[2], v[3], 1, 64, 64 * h)
+
+    def back(v):
+        return (T[v[1]][:, v[2] + (v[4] - 1) * v[5]:v[2] - 1 if v[2] else None:-v[5]],) + v[1:]
 
     def ind(win, off):
         return (win[0].indirect(off[0]), win, off)
@@ -115,7 +139,7 @@ def rank_program(g, core, T, topo):
             ns = 50 + out[4] * P["gather"]
         else:
             if rate is None:
-                rate = 0.5 if all(SCRATCH[v[1]][2] in ("bfloat16", "uint16") for v in [out] + ins) else 1
+                rate = 0.5 if all(SCRATCH[v[1]][2] in ("bfloat16", "uint16", "float16") for v in [out] + ins) else 1
             ns = P["call"] + max(64, rate * out[4]) * P["cycle"]
         add("v", "op", call, ins + list(more), [out], ns)
 
@@ -195,7 +219,7 @@ def rank_program(g, core, T, topo):
         return view(buf, lo, lo + HC)
 
     def spans(t, k, x, buf, zeros):
-        lo, n = (t * 2 + x) * 64 + 48 * k, 24 - 16 * k
+        lo, n = (t * 2 + x) * 72 + 56 * k, 24 - 16 * k
         return view(buf, lo + (0 if zeros else n), lo + 2 * n)
 
     def send_list(t, k, x, more=()):
@@ -213,7 +237,7 @@ def rank_program(g, core, T, topo):
     zeroed = small("zeroed", 8)
     for v, c in ((whole("ones"), 1.0), (whole("mkx"), 1.0), (view("mkx", 0, MK, 16), 0.0)):
         fill(v, c)
-    act(whole("rin"), view("mkx", 0, R * 128), 0.0, 0.0, [zeroed])
+    act(whole("rin"), view("mkx", 0, R * 144), 0.0, 0.0, [zeroed])
     for x in range(2):
         now["x"], now["tag"] = x, "0%s.start" % "AB"[x]
         dma("y", "dch%d" % x, [(T["nw%d" % x][64 * h:64 * h + 64, 0:HC], T.ch[64 * x:64 * x + 64, h * HC:(h + 1) * HC]) for h in range(2)],
@@ -230,38 +254,44 @@ def rank_program(g, core, T, topo):
 
     ones, blk, eye, zb, zf = (whole(n) for n in ("ones", "blk", "eye", "zb", "zf"))
     ip, im, sgn = view("ip", 0, 88), view("im", 0, 88), small("sgn", 112, "smb")
-    c716, last = small("c716", 64, "smb"), small("last", 24, "smb")
+    c716, last = small("c716", 64, "smb"), small("last", 32, "smb")
     for v, c in ((zb, 0.0), (c716, 7.0 / 16), (last, 0.0), (sub(last, 8, 8), 15.0),
                  (sgn, -1.0), (sub(sgn, 16, 16), 0.0), (sub(sgn, 96, 8), 1.0)):
         fill(v, c)
+    now["tag"] = "soon"
     act(whole("mkn"), whole("mkx"), -512.0, 512.0)
-    for v, c in ((whole("up"), 1.5 * 2.0 ** 16), (whole("down"), -1.5 * 2.0 ** 16), (whole("c13"), 2.0 ** -13), (whole("cp64"), 64.0), (zf, 0.0)):
+    for v, c in ((whole("up"), 1.5 * 2.0 ** 16), (whole("down"), -1.5 * 2.0 ** 16), (whole("c13"), 2.0 ** -13), (whole("cp64"), 64.0)):
         act(v, sub(ones, 0, 128), c)
-    act(whole("shf"), sub(ones, 0, 96), 0.0)
+    act(whole("shf"), view("mkx", 0, 144), 0.0)
+    now["tag"] = ""
     for h, c in enumerate((2.0 ** -7, -2.0 ** -19)):
         add("v", "op", lambda h=h, c=c: g.vector.memset(T.chalf[64 * h:64 * h + 64, :], c), [], [whole("chalf")], P["call"] + 64 * P["cycle"])
     pidx, i16, i8, i77 = (small(n, w, "smi") for n, w in (("pidx", 8), ("i16", 16), ("i8", 8), ("i77", 2)))
-    mask2, thr = small("mask", 128, "smb"), small("thr", 64, "smb")
-    mask = sub(mask2, 0, 64)
+    mask, thr = small("mask", 64, "smb"), small("thr", 64, "smb")
     iota(pidx, [[0, 8]], 0, 1)
     iota(i77, [[77, 2]], 0, 0)
     band(blk, ones, [[16, 8], [0, 16]])
     iota(i16, [[1, 16]], 0, 0)
     iota(i8, [[16, 8]], 0, 0)
     select(eye, sub(ones, 0, 128), [[-1, 128]], A.is_equal, 0, 1)
+    fill(zf, 0.0)
+    for name, zero, c in (("em2", zf, -2.0), ("eyef1", zf, 1.0), ("beye", zb, BIG), ("e512", zb, -512.0)):
+        select(whole(name), zero, [[-1, 128]], A.not_equal, 0, 1, c)
     band(ip, sub(ones, 0, 88), [[0, 11], [16, 8]])
     ts(im, ip, -1.0, A.mult)
     for a, b in ((ip, im), (im, ip)):
         select(sub(a, 16, 8), sub(b, 24, 8), [[0, 8]], A.is_ge, 0, 0)
     band(thr, sub(zb, 0, 64), [[16, 8], [0, 8]], -BIG)
-    band(mask, sub(ones, 0, 64), [[16, 8], [0, 8]])
+    ts(mask, thr, 0.0, A.is_equal)
+    ts(small("mask9", 64, "smb"), thr, 0.0, A.is_equal, 2.0 ** -9, A.mult)
     for x in range(2):
         for h in range(2):
             select(view("esl", (2 * x + h) * 112, (2 * x + h + 1) * 112), sgn, [[0, 14], [-100, 2], [-1, 4]], A.is_equal, 100 * h - 4 * x, 1)
-    for name, zero, c in (("eyef", zf, 1.0), ("em2", zf, -2.0), ("beye", zb, BIG)):
-        select(whole(name), zero, [[-1, 128]], A.not_equal, 0, 1, c)
-    select(whole("swp"), zb, [[-1, 128]], A.not_equal, -64, 1, 1.0)
-    select(whole("swp"), whole("swp"), [[-1, 128]], A.not_equal, 64, 1, 1.0)
+    dma("y", "dsw", [(T.swp[:, 64 * h:64 * h + 64], T.eye[:, 64 - 64 * h:128 - 64 * h]) for h in range(2)], [eye], [whole("swp")])
+    add("g", "op", lambda: g.iota(T.rmp[:], [[256, 16], [0, 16]], -2048, 0, allow_small_or_imprecise_dtypes=True),
+        [], [whole("rmp")], 130 + 512 * P["cycle"])
+    cp(view("ramp", 0, 256), whole("rmp"))
+    dma("y", "drm", [(T.ramp[:, lo:lo + 256], T.ramp[:, 0:256]) for lo in range(256, HN, 256)], [view("ramp", 0, 256)], [view("ramp", 256, HN)])
 
     wti, wi, wb = view("wti", 0, 2), small("wi", 8, "smi"), small("wb", 4)
     pm, p8 = small("pm", 8, "smi"), small("p8", 8, "smi")
@@ -280,7 +310,7 @@ def rank_program(g, core, T, topo):
     for k, m in enumerate((2047, 3, 2048, 4)):
         ts(sub(wi, 2 * k, 2), wti, m, A.bitwise_and)
     tt(wb, sub(wi, 0, 4), sub(wi, 4, 4), A.subtract)
-    for o, c in ((16, 4096.0), (64, 256.0)):
+    for o, c in ((16, 4096.0), (64, 256.0), (112, 8.0)):
         ts(view("shf", o, o + 16), i16, pf, A.is_equal, c, A.mult)
     ts(at16, i8, pf, A.add, 16.0, A.mult)
     ts(sub(bases, 0, 8), i8, pf, A.add)
@@ -290,10 +320,10 @@ def rank_program(g, core, T, topo):
         for sign, c in (("p", 1.0), ("m", -1.0)):
             ts(whole("w%s%d" % (sign, x)), blk, sub(wb, x, 1), A.mult, c / 4096, A.mult)
             ts(small("w8%s%d" % (sign, x), 64, "smb"), sub(ip, 24, 64), sub(wb, 2 + x, 1), A.mult, c / 8, A.mult)
-    ts(mask9, mask, 2.0 ** -9, A.mult)
-    ts(sub(mask2, 64, 64), mask, 2.0 ** -12, A.mult)
-    cp(sub(xo2, 0, 4), sub(p8, 0, 4))
-    ts(sub(xo2, 4, 4), sub(p8, 0, 4), 8.0, A.add)
+    both = small("both", 32)
+    fill(both, 0.0)
+    for x in range(2):
+        ts(sub(xo2, 4 * x, 4), sub(p8, 0, 4), 2.0, A.mult, 16.0 + x, A.add)
 
     def look(t, x, kind):
         k, own = int(kind[1]), kind[0] == "L"
@@ -302,6 +332,9 @@ def rank_program(g, core, T, topo):
         def gather(q):
             def make(lo, n):
                 src, dst = ind(table(x), sub(off, lo // 16, n // 16)), view("gb%d" % x, at + lo, at + lo + n)
+                if q == "v" and lift:
+                    ramp = view("ramp", 0, n)
+                    return lambda: g.vector.tensor_tensor(dst[0], src[0], ramp[0], A.add), [src, ramp], [dst], 50 + n * np.maximum(P["gather"], P["both"] * P["cycle"])
                 if q == "v":
                     return lambda: g.vector.tensor_copy(dst[0], src[0]), [src], [dst], 50 + n * P["gather"]
                 return lambda: g.scalar.activation(dst[0], src[0], F.Copy), [src], [dst], 65 + n * P["gather"]
@@ -313,24 +346,105 @@ def rank_program(g, core, T, topo):
             def make(lo, n):
                 d0, d1 = view("mkn" if least else "mkx", 0, n), view("gb%d" % x, at + lo, at + lo + n)
                 o = view(("m" if own else "p") + ("n%d" if least else "x%d") % x, k * HN + lo, k * HN + lo + n)
+                if least:
+                    d1, o = back(d1), back(o)
                 return lambda: g.vector.tensor_tensor_scan(o[0], d0[0], d1[0], 0.0, o0, o1), [d0, d1], [o], P["call"] + n / 2 * P["cycle"]
             return make
+
+        def twos(least, lo):
+            d0, d1 = (view("gb%d" % x, at + lo + h, at + lo + 255 + h, 2) for h in range(2))
+            base = lo if own else k * HN + lo
+            o = view("lp"[not own] + ("n%d" if least else "x%d") % x, base + 1 - least, base + 256 - least, 2)
+            if least:
+                d0, d1, o = back(d0), back(d1), back(o)
+            op = A.min if least else A.max
+            add("v", "op", lambda: g.vector.tensor_tensor_scan(o[0], d0[0], d1[0], 4096.0 if least else -4096.0, op, op), [d0, d1], [o],
+                P["call"] + 64 * P["cycle"], join=(None, 2 * len(prog), 1, 0))
+        if (t, x, kind) in member:
+            return levels(t, member[t, x, kind][0])
         cut = HN - HELP.get((t, x, kind), 0)
         step = now["tag"]
+        added = P["lift"].get(step, P["lift"].get(step[1:]))
+        lift = P["ramped"] and (not own or added is not None)
         ends = [c for c in CUTS.get(step, CUTS.get(step[1:], (1024,))) if c < cut] + [cut]
         pieces = list(range(0, HN + 1, P["spiece"]))
-        for q, make, marks, most, what in (("s", gather("s"), [0] + ends, HN, ""), ("v", gather("v"), [cut] + [c for c in pieces if c > cut], HN, "help"),
-                                           ("v", scan(False), pieces, MK, ""), ("v", scan(True), pieces, MK, "min")):
+        plain = [c for c in pieces if c <= cut] if lift else pieces
+        upto = HN
+        if added is not None:
+            upto = min([HN] + [-c for c in added if c < 0])
+            plain = [c for c in pieces if c >= upto]
+        for q, make, marks, most, what in (("s", gather("s"), [0] + ends if cut else [], HN, ""),
+                                           ("v", gather("v"), [cut] + [c for c in pieces if c > cut], MK if lift else HN, "help"),
+                                           ("v", scan(False), plain, MK, ""), ("v", scan(True), plain, MK, "min")):
             now["tag"] = step + what
             for lo, hi in zip(marks, marks[1:]):
                 add(q, "op", *make(lo, hi - lo), join=(make, lo, hi - lo, most))
+        cut = cut if lift else upto
+        if added is not None:
+            now["tag"] = step + "lift"
+            marks = [0] + [c for c in added if 0 < c < cut] + [cut] if cut else []
+            for j, (lo, hi) in enumerate(zip(marks, marks[1:])):
+                v, ramp = view("gb%d" % x, at + lo, at + hi), view("ramp", 0, hi - lo)
+                add("g", "dma", ("da%d%d%d" % (x, k + own, j), [(v[0], ramp[0], A.add)]), [v, ramp], [v], P["gdma"], (P["dma"], (hi - lo) / 4 * P["local"] * P["adds"]))
+            cut = 0
+        now["tag"] = step + "twos"
+        for lo in range(cut, upto, 256):
+            twos(0, lo)
+            twos(1, lo)
+        if own and added is not None:
+            y = view("pq%d" % x, 2 * HC, 3 * HC)
+            grouped(y, [(whole("meye"), view("ramp", 0, HN, 16)), (eye, res("lx", x, 0))], 1)
+            cp(res("mx", x, k), y)
 
-    def res(buf, x, k):
-        return view("%s%d" % (buf, x), k * HN + 15, (k + 1) * HN, 16)
+    member, done = {}, set()
+    for t in range(R):
+        for slot, batch in enumerate(BATCHES[t].split()):
+            for i, w in enumerate(batch.split("+")):
+                member[t, "AB".index(w[0]), w[2:]] = (slot, i, batch.count("+") + 1)
 
-    def span(side, x, k, sign, lo, n):
+    def levels(t, slot):
+        if (t, slot) in done:
+            return
+        done.add((t, slot))
+        keep, batch = dict(now), sorted((v[1], k[1], k[2]) for k, v in member.items() if k[0] == t and v[0] == slot)
+        n = len(batch)
+        gq, wide, each = "gq%d%d" % (n, slot), 8 * n, 16 // n
+        for i, x, kind in batch:
+            now["x"], step = x, "%d%s.%s" % (t, "AB"[x], kind)
+            off = lists(t, int(kind[1]), x, "inl")
+            for j in range(each):
+                m = n * j + i
+                src, dst = ind(table(x), sub(off, wide * j, wide)), (T[gq][:, :, :, 8 * m:8 * m + 8], gq, 0, n * HN, 16 * wide, 1, 128, m)
+                if (each - j) * 16 * wide <= HELP.get((t, x, kind), 0):
+                    now["tag"] = step + "help"
+                    add("v", "op", lambda src=src, dst=dst, m=m: g.vector.tensor_scalar(dst[0], src[0], 256.0 * m - 2048.0, None, A.add),
+                        [src], [dst], 50 + dst[4] * P["gather"], join=(None, 2 * len(prog), 1, 0))
+                else:
+                    now["tag"] = step
+                    add("s", "op", lambda src=src, dst=dst, m=m: g.scalar.activation(dst[0], src[0], F.Identity, 256.0 * m - 2048.0),
+                        [src], [dst], 65 + dst[4] * P["gather"], join=(None, 2 * len(prog), 1, 0))
+        now["tag"] = step + "scan"
+        for a in range(wide):
+            for buf, o, st in (("qx", A.max, 1), ("qn", A.min, -1)):
+                out = "%s%d%d" % (buf, n, slot)
+                d, ov = (None, gq, 256 * a, 256 * a + 256, 128, 1, 128, None), view(out, 128 * a, 128 * a + 128)
+                ov = ov if st > 0 else back(ov)
+                add("v", "op", lambda ov=ov, o=o, st=st, a=a: g.vector.tensor_tensor_scan(ov[0], T[gq][:, a, 0, ::st], T[gq][:, a, 1, ::st], -4096.0 * st, o, o),
+                    [d], [ov], P["call"] + 64 * P["cycle"], join=(None, 2 * len(prog), 1, 0))
+        now.update(keep)
+
+    def turned(t, x, k):
+        return member.get((t, x, "P%d" % k), (0, 0, 1))[2]
+
+    def res(buf, x, k, t=None):
+        if buf[0] == "p" and (t, x, "P%d" % k) in member:
+            slot, i, n = member[t, x, "P%d" % k]
+            return view("q%s%d%d" % (buf[1], n, slot), 8 * i + (7 if buf[1] == "x" else 0), n * 1024, 8 * n)
+        return view("%s%d" % (buf, x), k * HN + (15 if buf[1] == "x" else 0), (k + 1) * HN, 16)
+
+    def span(side, x, k, sign, lo, n, t=None):
         p, m = sub(ip, lo, n), sub(im, lo, n)
-        return [(res(side + "x", x, k), p if sign > 0 else m), (res(side + "n", x, k), m if sign > 0 else p)]
+        return [(res(side + "x", x, k, t), p if sign > 0 else m), (res(side + "n", x, k, t), m if sign > 0 else p)]
 
     def slack(t, j, x, lo, n):
         o = (t * 2 + j) * 2 * HC
@@ -359,8 +473,6 @@ def rank_program(g, core, T, topo):
         ts(new, raw, 6, A.arith_shift_right, 2047, A.bitwise_and)
         cp(half(lists(t, j + 1, x), h), new)
 
-    both = small("both", 32)
-
     def kappa():
         kv, kr, ne = small("kv", 16), small("kr", 1), small("ne", 16, "smb")
         tt(ne, sub(both, 0, 16), sub(both, 16, 16), A.is_equal)
@@ -377,7 +489,8 @@ def rank_program(g, core, T, topo):
         def tag(w):
             now["tag"] = "%d%s.%s" % (t, "AB"[x], w)
         z = "pz%d" % x
-        rise = span("m", x, 0, -1, 0, 88), span("m", x, 1, 1, 0, 88), span("m", x, 2, 1, 0, 88)
+        rise = span("m", x, 0, -1, 0, 88), span("m", x, 1, 1, 0, 88)
+        rise += (span("l", x, 0, 1, 0, 88) if P["lift"].get("%d%s.L2" % (t, "AB"[x]), P["lift"].get("AB"[x] + ".L2")) is not None else span("m", x, 2, 1, 0, 88),)
 
         def cut(pairs, lo, n):
             return [(l, sub(r, lo, n)) for l, r in pairs]
@@ -399,54 +512,80 @@ def rank_program(g, core, T, topo):
         ts(so, at, 1.0 / 32, A.mult)
         propose(t, x, 1, ind(whole("uc%d" % x), so), None)
         send_list(t, 2, x)
+        yield
         for kind in ("P0", "P1", "P2"):
             tag(kind)
             look(t, x, kind)
         tag("answer")
-        for k, out, pairs in ((0, view("pq%d" % x, 0, 24), span("p", x, 0, -1, 24, 24) + span("p", x, 1, 1, 24, 24)),
-                              (1, view("pq%d" % x, 32, 40), span("p", x, 0, 1, 24, 8) + span("p", x, 2, -1, 24, 8))):
-            v = spans(t, k, x, "ro", False)
+        o0, o2 = turned(t, x, 0), turned(t, x, 2)
+        sign = 1 if o2 == 1 else -1
+        if o0 == o2:
+            out = view("pq%d" % x, 0, 24)
+            pairs = span("p", x, 0, -1, 24, 24, t) + span("p", x, 1, 1, 24, 24, t), span("p", x, 0, sign, 24, 8, t)
+        else:
+            out = view("pq%d" % x, 0, 32)
+            low = span("p", x, 0, -1, 24, 32, t)
+            pairs = low[:1] + [p + (sub(out, 0, 24),) for p in span("p", x, 1, 1, 24, 24, t)] + low[1:], []
+        for k, out, pairs in ((0, out, pairs[0]), (1, view("pq%d" % x, 32, 40), pairs[1] + span("p", x, 2, -sign, 24, 8, t))):
+            v = sub(spans(t, k, x, "ro", False), 0, out[4])
             grouped(out, pairs, 1)
-            ts(v, out, float(k), A.add)
+            ts(v, out, float(k * sign), A.add)
             send(asker(t), v, "rin", "r%d%d%d" % (t, k, x))
         tag("L2")
         look(t, x, "L2")
         tag("truth")
         z2, hd, x12, sel, ne0 = view(z, 64, 112), sv("hd", 48), sv("x12", 16), sv("sel", 8), sv("ne0", 16, "smb")
-        grouped(z2, slack(t, 0, x, 0, 48) + cut(rise[0] + rise[1], 0, 48) + [(whole("eyef"), spans(t, 0, x, "rin", True))], 1)
+        grouped(z2, slack(t, 0, x, 0, 48) + cut(rise[0] + rise[1], 0, 48) + [(whole("eyef%d" % o0), spans(t, 0, x, "rin", True))], 1)
         ts(hd, z2, 0.0, A.is_le, 0.5, A.mult)
         tt(x12, sub(z2, 16, 16), sub(hd, 0, 16), A.mult)
         tt(ne0, sub(hd, 0, 16), sub(hd, 32, 16), A.not_equal)
         tag("decide")
         w2 = view("pu%d" % x, 128, 144)
-        grouped(w2, slack(t, 1, x, 96, 16) + cut(rise[0], 16, 16) + [(whole("em2"), x12), (whole("beye"), ne0)] + cut(rise[2], 16, 16), 2)
-        fv, fy = sv("fv", 32, "smu"), view("fy%d" % x, 0, HC)
-        no, fo, vo, d0 = sub(fv, 0, 8), sub(fv, 8, 8), sub(fv, 16, 8), sub(hd, 32, 8)
-        early = t == R - 1 and x in P["early"]
-        if early:
-            u3, ui, xa, xb, d1 = view("pl%d" % x, 16, 40), small("ui", 24), small("xa", 16), small("xb", 16), small("d1", 16)
-            ra, rb, rc = (small(n, 128, "smb") for n in ("ra", "rb", "rc"))
-            weigh = [[(res("mx", x, k), sv(w, 8, "smb"), sub(u3, 8 * k, 8)) for k in range(3)] for w in ("w8m", "w8p")]
-            grouped(u3, [(eye, sub(c716, 0, 24))] + weigh[0] + rounding(24) + weigh[1] + [(eye, sub(zb, 0, 24))], 7)
-            ts(ui, u3, 8.0, A.mult)
-            cp(sub(xa, 0, 8), d0)
-            ts(sub(xb, 0, 8), d0, 2.0, A.mult)
-            tt(sub(xb, 8, 8), sub(ui, 8, 8), sub(ui, 0, 8), A.subtract)
-            tt(sub(xb, 8, 8), sub(xb, 8, 8), sub(xb, 0, 8), A.mult)
-            tt(sub(xa, 8, 8), sub(xb, 8, 8), sub(ui, 0, 8), A.add)
-            tt(sub(xb, 8, 8), sub(ui, 16, 8), sub(xa, 8, 8), A.subtract)
-            ts(sub(xb, 0, 8), d0, -1.0, A.mult, 1.0, A.add)
-            tt(ra, ind(xa, xo2), mask2, A.mult)
-            tt(rb, ind(xb, xo2), mask2, A.mult)
-            tt(d1, w2, spans(t, 1, x, "rin", True), A.is_lt)
-            tt(rc, ind(sub(d1, 8, 8), xo), rb, A.mult)
-            at = view("pl%d" % x, 40, 64)
-            moves = [shifted(sub(at, 8, 16), v) + shifted(sub(at, 0, 8), sub(v, 0, 64), 0, 1) for v in (ra, rc)]
-            grouped(at, [(eye, sub(bases, 0, 24))] + moves[0] + moves[1] + [(eye, last)], 17)
-            tag("pick")
-            cp(sub(fv, 0, 24), at)
+        pairs = slack(t, 1, x, 96, 16) + cut(rise[0], 16, 16)
+        if o0 != o2:
+            pairs += [(whole("eyef%d" % o0), sub(spans(t, 0, x, "rin", False), 24, 8), sub(w2, 8, 8))]
+        pairs += [(whole("em2"), x12), (whole("beye"), ne0)]
+        if o2 == 1:
+            grouped(w2, pairs + cut(rise[2], 16, 16), 2)
         else:
+            mms(w2, pairs, True, False)
+            mms(w2, cut(rise[2], 16, 16), False, False)
+            mms(w2, [(whole("eyef%d" % o2), spans(t, 1, x, "rin", True))], False, True)
+        fv, fy = sv("fv", 32, "smu"), view("fy%d" % x, 0, HC)
+        no, fo, d0 = sub(fv, 0, 8), sub(fv, 8, 8), sub(hd, 32, 8)
+        early, swap = (t, x) in P["early"], t < R - 1 and x in P["swap"]
+        n = 2 if swap else 1
+        vo = sub(fv, 16, 8 * n)
+
+        def low(out, y, more=()):
+            grouped(out, [(eye, c716), (y, sv("w8m", 64, "smb"))] + rounding(64) + list(more) + [(y, sv("w8p", 64, "smb"))], 4 + len(more))
+        if early:
+            tag("early")
+            r0, ra, dm, rc = (sv(w, 64, "smb") for w in ("r0", "ra", "dm", "rc"))
+            at, ya, rq = view("pl%d" % x, 40, 48), view("old%d" % x, 0, HC), view(z, 192, 256)
+            tt(r0, ind(d0, sub(xo, 0, 4)), mask, A.mult)
+            grouped(at, [(eye, at16)] + shifted(at, r0) + [(eye, sub(last, 8, 8))], 9)
+            cp(fo, at)
+            cp(ya, ind(view("mx%d" % x, 0, 2 * HN), fo))
+            low(view(z, 128, 192), ya)
+            tt(ra, view(z, 128, 192), mask9, A.mult)
+            low(rq, res("mx", x, 2), [(whole("e512"), ra)])
+            tag("decide")
             tt(view(both[1], both[2] + x, both[3], 2), w2, spans(t, 1, x, "rin", True), A.is_lt)
+            tt(dm, ind(both, sub(xo2, 4 * x, 4)), mask, A.mult)
+            tt(rc, rq, dm, A.mult)
+            tt(r, dm, r0, A.max)
+            at = view("pl%d" % x, 48, 64 + 8 * n)
+            moves = [[m for h in range(n) for m in shifted(sub(at, 16 + 8 * h, 8), v, h, less)] for v, less in ((ra, 0), (rc, 2))]
+            moves[1] += shifted(sub(at, 8, 8), r) + shifted(sub(at, 0, 8), r, 0, 1)
+            grouped(at, [(eye, sub(bases, 0, at[4]))] + moves[0] + moves[1] + [(eye, sub(last, 0, at[4]))], len(moves[1]) + 1)
+            tag("pick")
+            cp(sub(fv, 0, at[4]), at)
+        else:
+            if o2 == 1:
+                tt(view(both[1], both[2] + x, both[3], 2), w2, spans(t, 1, x, "rin", True), A.is_lt)
+            else:
+                ts(view(both[1], both[2] + x, both[3], 2), w2, 0.0, A.is_lt)
             tt(sel, view(both[1], both[2] + 16 + x, both[3], 2), d0, A.max)
             tt(r, ind(sel, sub(xo, 0, 4)), mask, A.mult)
             at = view("pl%d" % x, 8, 24)
@@ -455,7 +594,13 @@ def rank_program(g, core, T, topo):
             tag("pick")
             cp(sub(fv, 0, 16), at)
         pick = take if (t, x) in P["spick"] else cp
-        pick(fy, ind(view("mx%d" % x, 0, 3 * HN), fo))
+        last_pick = early and t == R - 1
+        if last_pick:
+            ts(view("hx%d" % x, 0, HC), ind(view("mx%d" % x, 0, 3 * HN), fo), 0.5, A.mult)
+            src, dst = ind(table(x), vo), view("hx%d" % x, HC, 2 * HC)
+            add("s", "op", lambda: g.scalar.activation(dst[0], src[0], F.Identity, -0.25, 0.5), [src], [dst], 65 + HC * P["gather"])
+        else:
+            pick(fy, ind(view("mx%d" % x, 0, 3 * HN), fo))
         tag("names")
         picked = ind(view("nw%d" % x, 0, 3 * HC), no)
         if t < R - 1:
@@ -468,13 +613,11 @@ def rank_program(g, core, T, topo):
             dma("y", "dyc%d" % x, [(T.yc[64 * x:64 * x + 64, h * HC:(h + 1) * HC], part(y, h)[0]) for h in range(2)], [y], [])
         tag("update")
         tab, xs, xh = table(x), view("xs%d" % x, 0, HC), view("xs%d" % x, HC, 2 * HC)
-        swap = t < R - 1 and x in P["swap"]
         if not early:
             rest = view(z, 128, 192)
-            grouped(rest, [(eye, c716), (fy, sv("w8m", 64, "smb"))] + rounding(64) + [(fy, sv("w8p", 64, "smb"))], 4)
+            low(rest, fy)
             tt(r, rest, mask9, A.mult)
-            n = 2 if swap else 1
-            at, vo = view("pl%d" % x, 24, 24 + 8 * n), sub(fv, 16, 8 * n)
+            at = view("pl%d" % x, 24, 24 + 8 * n)
             moves = [m for h in range(n) for m in shifted(sub(at, 8 * h, 8), r, h)]
             grouped(at, [(eye, sub(bases, 16, 8 * n))] + moves + [(eye, sub(zb, 0, 8 * n))], 8 * n + 1)
             cp(vo, at)
@@ -484,6 +627,8 @@ def rank_program(g, core, T, topo):
             for h, turn in enumerate((eye, whole("swp"))):
                 grouped(view(z, (2 + h) * HC, (3 + h) * HC), [(turn, fy), (turn, old)], 1)
             ts(xh, view(z, 2 * HC, 4 * HC), 0.5, A.mult, -0.25, A.add)
+        elif last_pick:
+            tt(xh, view("hx%d" % x, 0, HC), view("hx%d" % x, HC, 2 * HC), A.add)
         else:
             tt(xs, ind(tab, vo), fy, A.add)
             ts(xh, xs, 1, A.arith_shift_right)
@@ -498,9 +643,11 @@ def rank_program(g, core, T, topo):
         if t:
             now["x"], now["tag"] = 0, "%dkappa" % t
             kappa()
-        for x in range(2):
-            now["x"] = x
-            stream(t, x)
+        runs = [stream(t, x) for x in range(2)]
+        for _ in range(2):
+            for x in range(2):
+                now["x"] = x
+                next(runs[x], None)
 
     issue(g, T, topo, core, eng, plan(prog, P), {"inl": asker, "rin": partner})
 
@@ -524,15 +671,15 @@ def arrange(prog, P):
     for i, o in enumerate(prog):
         for vs, w in ((o["reads"], False), (o["writes"], True)):
             for v in vs:
-                for lo, hi, aw, j in acc.get(v[1], ()):
-                    if lo < v[3] and v[2] < hi and (w or aw) and j != i:
+                for lo, hi, aw, j, c in acc.get(v[1], ()):
+                    if lo < v[3] and v[2] < hi and (w or aw) and j != i and (c is None or v[7] is None or c == v[7]):
                         pred[i].add(j)
         for vs, w in ((o["reads"], False), (o["writes"], True)):
             for v in vs:
                 lst = acc.setdefault(v[1], [])
                 if w:
-                    lst[:] = [a for a in lst if not (v[2] <= a[0] and a[1] <= v[3])]
-                lst.append((v[2], v[3], w, i))
+                    lst[:] = [a for a in lst if not (v[2] <= a[0] and a[1] <= v[3] and v[7] in (None, a[4]))]
+                lst.append((v[2], v[3], w, i, v[7]))
         if o["q"] == "t":
             bank = o["writes"][0][1]
             if bank in last:
@@ -550,7 +697,11 @@ def arrange(prog, P):
     true = [list(v) for v in pred], [list(v) for v in succ]
     steps = ["%d%s" % (t, w) for t in range(R) for w in ORDER[t].split()]
     looks = sorted((steps.index(o["tag"]), i) for i, o in enumerate(prog) if o["q"] == "s" and o["join"])
-    for (_, i), (_, j) in zip(looks, looks[1:]):
+    pairs = [(i, j) for (_, i), (_, j) in zip(looks, looks[1:])]
+    last = {o["tag"]: i for i, o in enumerate(prog) if o["q"] == "g"}
+    pairs += [(last[w[0] + P["behind"][w[1:]]], i) for w, i in last.items() if w[1:] in P["behind"] and w[0] != "0"]
+    P["soft"] = set(pairs)
+    for i, j in pairs:
         pred[j].append(i)
         succ[i].append(j)
     turn, left = [i for i in range(n) if not pred[i]], [len(v) for v in pred]
@@ -579,6 +730,8 @@ def arrange(prog, P):
             gs[k:k + 1] = [x for x in ([lo, at[i]], [at[i] + ns[i], hi]) if x[1] - x[0] > 40]
         return at
 
+    if P["deal"]:
+        return improve(prog, P, true[0], true[1], deal(prog, P, pred, succ, turn))
     lead = [rank[i] + (0 if o["join"] else P["lead"]) for i, o in enumerate(prog)]
     for i in turn[::-1]:
         lead[i] = max([lead[i]] + [lead[j] + 1 for j in succ[i]])
@@ -593,6 +746,121 @@ def arrange(prog, P):
     return improve(prog, P, true[0], true[1], [i for _, i in sorted((start[i], i) for i in range(n))])
 
 
+def deal(prog, P, pred, succ, turn):
+    n, rng = len(prog), np.random.default_rng(P["seed"])
+    q, join, tags = ([o[k] for o in prog] for k in ("q", "join", "tag"))
+    banks = [{v[1] for v in o["reads"] + o["writes"] if SCRATCH[v[1]][0] == "psum"} for o in prog]
+    tries, fit, mix = P["deal"]
+    mix, ahead = np.array(mix, float), dict(v=0, s=P["ahead"], t=P["ahead"], g=P["ahead"], y=P["ahead"])
+
+    def mean(v):
+        return float(np.dot(v + 0 * mix, mix))
+    ns, lag = [mean(o["ns"]) for o in prog], [(mean(o["lag"][0]), mean(o["lag"][1])) if o["lag"] else None for o in prog]
+    wake, begin = [mean(P["far"] if o["kind"] == "send" else P["wake"]) for o in prog], {"v": mean(P["call"]), "s": 0}
+    loose = [[j for j in pred[i] if (q[i] != "t" or q[j] != "t") and (j, i) not in P["soft"]] for i in range(n)]
+
+    def backwards(urge):
+        left, end, free = [len(v) for v in succ], [0.0] * n, {e: 0.0 for e in "vstgy"}
+        can, since = {e: [] for e in free}, [sum(lag[i] or ()) for i in range(n)]
+        for i in range(n):
+            if not left[i]:
+                can[q[i]].append(i)
+        for _ in range(n):
+            t, e = min((max(free[e], min([since[i] for i in cs])), e) for e, cs in can.items() if cs)
+            near = [(urge[i], i, since[i]) for i in can[e] if since[i] <= t + 1000]
+            top = max(near)
+            if top[2] > t:
+                top = max([x for x in near if max(x[2], t) + ns[x[1]] <= top[2] + fit], default=top)
+            i = top[1]
+            can[e].remove(i)
+            free[e] = end[i] = max(t, top[2]) + ns[i]
+            for k in pred[i]:
+                left[k] -= 1
+                if not left[k]:
+                    since[k] = max([end[j] + (k in loose[j]) * wake[k] for j in succ[k]]) + sum(lag[k] or ())
+                    can[q[k]].append(k)
+        return end
+
+    chainlen = [0.0] * n
+    for i in turn[::-1]:
+        chainlen[i] = ns[i] + sum(lag[i] or ()) + max([(i in loose[j]) * wake[i] + chainlen[j] for j in succ[i]], default=0.0)
+
+    def once(boost, base):
+        rank = [r + boost.get(w, 0) + (w == "soon") * 1e6 for r, w in zip(base, tags)]
+        left, ready, gate = [len(v) for v in pred], [0.0] * n, [None] * n
+        free, tail, last, order = {e: 0.0 for e in "vstgy"}, {}, None, []
+        can, since = {e: [] for e in free}, [0.0] * n
+        for i in range(n):
+            if not left[i]:
+                can[q[i]].append(i)
+
+        def first(i):
+            t = since[i]
+            for b in banks[i]:
+                k = tail.get(b)
+                if k is not None and q[k] != q[i] and ready[k] > t:
+                    t = ready[k]
+            return t
+        for _ in range(n):
+            best = None
+            for e, cs in can.items():
+                if cs:
+                    at = [first(i) for i in cs]
+                    t = max(free[e], min(at))
+                    if best is None or t - ahead[e] < best[4]:
+                        best = t, e, cs, at, t - ahead[e]
+            t, e, cs, at, _ = best
+            near = [(rank[i], -i, a) for i, a in zip(cs, at) if a <= t + 1000]
+            top = max(near)
+            if top[2] > t:
+                top = max([x for x in near if max(x[2], t) + ns[-x[1]] <= top[2] + fit], default=top)
+            i = -top[1]
+            cs.remove(i)
+            j = tail.get(e)
+            t = max(t, top[2])
+            gate[i] = j if j is not None and free[e] >= top[2] else max(loose[i] + [tail[b] for b in banks[i] if b in tail], key=lambda k: ready[k], default=None)
+            glued = j is not None and join[i] and join[j] and join[j][0] is join[i][0] and join[j][1] + join[j][2] == join[i][1]
+            free[e] = t = t + ns[i] - (begin[e] if glued else 0)
+            tail[e] = i
+            for b in banks[i]:
+                tail[b] = i
+            if lag[i]:
+                t += lag[i][0]
+                if last is not None:
+                    t = max(t, ready[last] - wake[last])
+                t, last = t + lag[i][1], i
+            ready[i] = t + wake[i]
+            order.append(i)
+            for k in succ[i]:
+                left[k] -= 1
+                if not left[k]:
+                    since[k] = max([ready[j] for j in loose[k]], default=0.0)
+                    can[q[k]].append(k)
+        return max(ready), order, gate, ready
+
+    boost, best, base = {}, None, chainlen
+    for _ in range(P["passes"]):
+        end, order, gate, ready = once({}, base)
+        if best is None or end < best[0]:
+            best = end, base
+        base = backwards([r - w - sum(l or ()) for r, w, l in zip(ready, wake, lag)])
+    best, base = None, best[1]
+    names = sorted(set(tags))
+    for step in range(tries):
+        trial = dict(boost)
+        for _ in range(min(step, 1 + int(rng.integers(3)))):
+            w = names[rng.integers(len(names))] if rng.random() < 0.5 else chain[rng.integers(len(chain))]
+            trial[w] = trial.get(w, 0) + float(rng.normal()) * 1500
+        end, order, gate, ready = once(trial, base)
+        if best is None or end <= best[0]:
+            best, boost = (end, order), trial
+            i, chain = max(range(n), key=lambda k: ready[k]), []
+            while i is not None:
+                chain.append(tags[i])
+                i = gate[i]
+    return best[1]
+
+
 def improve(prog, P, pred, succ, order):
     n, rng = len(prog), np.random.default_rng(P["seed"])
     q, ns, lag, join = ([o[k] for o in prog] for k in ("q", "ns", "lag", "join"))
@@ -604,18 +872,41 @@ def improve(prog, P, pred, succ, order):
     def follows(i, j):
         return join[i] and join[j] and join[j][0] is join[i][0] and join[i][1] + join[i][2] == join[j][1] and join[i][2] + join[j][2] <= join[i][3]
 
-    def run(order, first, old):
+    def tails(order, gate):
+        rest, after, behind = [zero] * n, [zero] * n, zero
+        for i in order[::-1]:
+            t = after[i] + wake[i]
+            if lag[i]:
+                behind = np.maximum(t, behind) + lag[i][1]
+                t = behind + lag[i][0]
+            j, waits = gate[i]
+            t = np.maximum(t, rest[i]) + ns[i]
+            if j is not None:
+                rest[j] = t = t - begin[q[i]] if glue[0] and join[i] and follows(j, i) else t
+            rest[i] = t
+            for k in waits:
+                after[k] = np.maximum(after[k], t)
+        return rest, after
+
+    def run(order, first, old, moved=None):
         start, end, ready, gate = (list(v) for v in old[:4])
         tail, last = {}, None
         for i in order[:first]:
             tail[q[i]] = i
             for b in banks[i]:
                 tail[b] = i
-        for i in order[:first][::-1]:
             if lag[i]:
                 last = i
-                break
-        for i in order[first:]:
+        reach, bad, low, same = 0, set(), zero, zero
+        for k, i in enumerate(order[first:], first):
+            if moved and k > moved[0]:
+                if k == moved[0] + 1:
+                    was = {r: j for j in moved[1][first:k] for r in uses[j]}
+                    bad.update(r for r, j in was.items() if (last if r == "dma" else tail[r]) != j)
+                if not bad and k > reach:
+                    return start, end, ready, gate, old[4], old[5], old[6]
+                if (k - moved[0]) % 30 == 0 and float(np.sum((np.where(same > old[4] - 30, low, np.maximum(low, old[4])) / load) ** P["power"])) > moved[4]:
+                    return None
             e = q[i]
             j = tail.get(e)
             t = zero if j is None else end[j]
@@ -634,7 +925,17 @@ def improve(prog, P, pred, succ, order):
                 if last is not None:
                     t = np.maximum(t, ready[last] - wake[last])
                 t, last = t + lag[i][1], i
-            ready[i] = t + wake[i]
+            ready[i] = t = t + wake[i]
+            if moved:
+                if k > moved[0] + 180:
+                    moved = None
+                elif t.tobytes() != old[2][i].tobytes():
+                    bad.update(uses[i])
+                    reach = max([reach] + [moved[2][j] for j in succ[i]])
+                    if k > moved[0]:
+                        low, same = np.maximum(low, start[i] + moved[3][i]), np.maximum(same, old[0][i] + moved[3][i])
+                elif k > moved[0]:
+                    bad.difference_update(uses[i])
         final = [i for i in order[-40:] if not succ[i]]
         time = np.max([ready[i] for i in final], 0)
         return start, end, ready, gate, time, float(np.sum((time / load) ** P["power"])), final
@@ -649,15 +950,18 @@ def improve(prog, P, pred, succ, order):
         return order[:lo] + (mine + rest if b < a else rest + mine) + order[hi + 1:], lo
 
     now = [[None] * n] * 4
+    uses = [[q[i]] + list(banks[i]) + (["dma"] if lag[i] else []) for i in range(n)]
     for moves, glue[0], since in P["moves"]:
-        chain = None
+        chain, stale = None, 99
         now = run(order, 0, now)
+        at = {i: k for k, i in enumerate(order)}
         for step in range(moves):
             start, end, ready, gate, time, worth, final = now
+            if stale >= 12:
+                (rest, after), stale = tails(order, gate), 0
             if chain is None or step % 16 == 0:
                 weight = (time / load) ** P["power"]
                 c = int(rng.choice(len(load), p=weight / weight.sum()))
-                at = {i: k for k, i in enumerate(order)}
                 i, chain = max(final, key=lambda i: ready[i][c]), []
                 while i is not None and at[i] >= since * len(order):
                     j, waits = gate[i]
@@ -667,8 +971,27 @@ def improve(prog, P, pred, succ, order):
                 chain = [x for x in chain if x[1] is not None and (x[2] or gate[x[1]][0] is None or rng.random() < 0.3 or not join[x[0]])]
             i, j, idle = chain[rng.integers(len(chain))]
             same = [k for k in order[max(0, at[i] - 60):at[i] + 120] if q[k] == q[i]]
-            me = same.index(i)
-            if idle and me + 1 < len(same):
+            me, pick = same.index(i), rng.random()
+            if pick < P["aim"]:
+                share = (time / load) ** P["power"]
+                if pick < P["aim"] / 2 and not idle:
+                    low = max([at[k] for k in pred[i]], default=-1)
+                    spots = [k for k in range(1, me) if at[same[k]] > low]
+                    if not spots:
+                        continue
+                    can = np.max([zero] + [ready[k] for k in pred[i]], 0)
+                    late = np.array([np.maximum(can, end[same[k - 1]]) + ns[i] + rest[same[k]] for k in spots]) - time
+                    a, b = at[i], at[same[spots[int(np.argmin(np.maximum(late, 0) @ share + rng.random(len(spots)) * share.sum() * 20))]]]
+                else:
+                    j = same[max(0, me - 1 - int(rng.integers(3)))]
+                    high = min([at[k] for k in succ[j]], default=n)
+                    spots = [k for k in range(me, len(same) - 1) if at[same[k]] < high]
+                    if not spots or j == i:
+                        continue
+                    own = ns[j] + wake[j] + after[j] + (lag[j][0] + lag[j][1] if lag[j] else 0)
+                    late = np.array([end[same[k]] + np.maximum(own, ns[j] + rest[same[k + 1]]) for k in spots]) - time
+                    a, b = at[j], at[same[spots[int(np.argmin(np.maximum(late, 0) @ share + rng.random(len(spots)) * share.sum() * 20))]]]
+            elif idle and me + 1 < len(same):
                 a, b = at[same[me + 1 + int(rng.integers(min(24, len(same) - me - 1)))]], at[i]
             elif rng.random() < 0.5 or me + 1 == len(same):
                 a, b = at[i], at[same[max(0, me - 1 - int(rng.integers(6)))]]
@@ -677,9 +1000,12 @@ def improve(prog, P, pred, succ, order):
             if a == b:
                 continue
             other, first = shift(order, a, b)
-            new = run(other, first, now)
-            if new[5] <= worth * (1 + P["heat"] * (1 - step / moves) * rng.random()):
-                order, now, chain = other, new, None
+            most = worth * (1 + P["heat"] * (1 - step / moves) * rng.random())
+            new = run(other, first, now, (max(a, b), order, at, rest, most))
+            if new and new[5] <= most:
+                stale += 1 if new[5] == worth else 4
+                order, now, chain = other, new, chain if new[5] == worth else None
+                at.update((i, k) for k, i in enumerate(order[first:max(a, b) + 1], first))
         k, glue[0] = 0, False
         now = run(order, 0, now)
         while k < len(order):
@@ -732,7 +1058,7 @@ def issue(g, T, topo, core, eng, calls, sender):
             for v in vs:
                 ps = region(v)[3]
                 for a in acc.get(v[1], ()):
-                    if ps and a[3] != q or (a[0] < v[3] and v[2] < a[1] and (w or a[2]) and not (ps and q == "t")):
+                    if ps and a[3] != q or (a[0] < v[3] and v[2] < a[1] and (w or a[2]) and not (ps and q == "t") and (v[7] is None or a[7] in (None, v[7]))):
                         need[a[4]] = max(need.get(a[4], 0), a[5])
                         cks.append((a[4], a[6]))
         for s in sorted(need):
@@ -751,14 +1077,14 @@ def issue(g, T, topo, core, eng, calls, sender):
                 lst = acc.setdefault(v[1], [])
                 if region(v)[3]:
                     lst[:] = [a for a in lst if a[3] == q]
-                lst[:] = [a for a in lst if not (v[2] <= a[0] and a[1] <= v[3] and (w or a[4] == sem and not a[2]))]
-                lst.append((v[2], v[3], w, q, sem, val, ck))
+                lst[:] = [a for a in lst if not (v[2] <= a[0] and a[1] <= v[3] and v[7] in (None, a[7]) and (w or a[4] == sem and not a[2]))]
+                lst.append((v[2], v[3], w, q, sem, val, ck, v[7]))
 
     for o in calls:
         if o["kind"] == "send":
             _, src, land, sem = o["call"]
             n = len(engines(T.cores[sender[land](int(sem[1]))], core))
-            acc.setdefault(land, []).append((src[2], src[3], True, "x", sem, n, {sem: n}))
+            acc.setdefault(land, []).append((src[2], src[3], True, "x", sem, n, {sem: n}, None))
     for o in calls:
         q = o["q"]
         if TAG[0]:
@@ -774,8 +1100,8 @@ def issue(g, T, topo, core, eng, calls, sender):
         before(q, o["reads"], o["writes"])
         if o["kind"] == "dma":
             sem, pairs = o["call"]
-            for out, in_ in pairs:
-                eng[q].dma_start(out, in_).then_inc(T.sem[sem], 16)
+            for out, in_, *op in pairs:
+                (g.dma_start(out, in_, accum_op=op[0]) if op else eng[q].dma_start(out, in_)).then_inc(T.sem[sem], 16)
             total[sem] += 16 * len(pairs)
             after(q, o["reads"], o["writes"], sem, total[sem])
         else:

import numpy as np
from concourse.mybir import AluOpType, ActivationFunctionType

R, HC = 4, 128
HN = 16 * HC
MK = 1024
BIG = 65536.0
KINDS = ("L0", "P0", "L1", "P1", "L2", "P2")

SCRATCH = {
    "ramp": ("sbuf", [128, HN], "float16"), "rmp": ("sbuf", [128, 256], "bfloat16"), "mkx": ("sbuf", [128, MK], "bfloat16"), "mkn": ("sbuf", [128, MK], "bfloat16"),
    "outl": ("sbuf", [128, R * 6 * HC], "uint16"), "inl": ("sbuf", [128, R * 6 * HC], "uint16"),
    "ro": ("sbuf", [128, R * 144], "float32"), "rin": ("sbuf", [128, R * 144], "float32"),
    "wti": ("sbuf", [128, 2], "int32"), "sli": ("sbuf", [128, 128], "int32"),
    "slc": ("sbuf", [128, 128], "bfloat16"), "slb": ("sbuf", [128, 2048], "bfloat16"),
    "sm": ("sbuf", [128, 640], "float32"), "smi": ("sbuf", [128, 512], "int32"), "smb": ("sbuf", [128, 1536], "bfloat16"),
    "smu": ("sbuf", [128, 128], "uint16"), "esl": ("sbuf", [128, 448], "bfloat16"), "shf": ("sbuf", [128, 144], "bfloat16"),
}
for _k in ("ones", "blk", "eye", "c13", "chalf", "cp64", "zb", "beye", "ip", "im", "swp", "old0", "old1", "up", "down", "meye", "e512"):
    SCRATCH[_k] = ("sbuf", [128, 128], "bfloat16")
for _k in ("zf", "em2"):
    SCRATCH[_k] = ("sbuf", [128, 128], "float32")
for _x in "01":
    SCRATCH["tab" + _x] = ("sbuf", [128, 2048], "bfloat16")
    for _k in ("mx", "mn", "px", "pn"):
        SCRATCH[_k + _x] = ("sbuf", [128, 3 * HN], "bfloat16" if _k[0] == "m" else "float16")
    SCRATCH["gb" + _x] = ("sbuf", [128, 6 * HN], "float16")
    SCRATCH["lx" + _x] = SCRATCH["ln" + _x] = ("sbuf", [128, HN], "float16")
    SCRATCH["hx" + _x] = ("sbuf", [128, 2 * HC], "float32")
    SCRATCH["nw" + _x] = ("sbuf", [128, 3 * HC], "int32")
    SCRATCH["ud" + _x] = ("sbuf", [128, HC], "int32")
    SCRATCH["uc" + _x] = ("sbuf", [128, 2 * HC], "float32")
    SCRATCH["fy" + _x] = ("sbuf", [128, HC], "bfloat16")
    SCRATCH["xs" + _x] = ("sbuf", [128, 2 * HC], "int32")
    SCRATCH["wp" + _x] = ("sbuf", [128, 128], "float16")
    SCRATCH["wm" + _x] = ("sbuf", [128, 128], "float16")
    for _k in "uzql":
        SCRATCH["p" + _k + _x] = ("psum", [128, 512], "float32")
BATCHES = [""] * R
SIZES = set()
for _t, _b in enumerate(BATCHES):
    for _w in ("A.P0", "A.P2", "B.P0", "B.P2"):
        SIZES.add(([1] + [_v.count("+") + 1 for _v in _b.split() if _w in _v])[-1])
    for _s, _v in enumerate(_b.split()):
        _n = _v.count("+") + 1
        SCRATCH["gq%d%d" % (_n, _s)] = ("sbuf", [128, 8 * _n, 2, 128], "float16")
        for _k in "xn":
            SCRATCH["q%s%d%d" % (_k, _n, _s)] = ("sbuf", [128, 1024 * _n], "float16")
SIZES = sorted(SIZES)
for _n in SIZES:
    SCRATCH["eyef%d" % _n] = ("sbuf", [128, 128], "float32")

DMAS = ["dch0", "dch1", "dwt", "dsl", "dsb", "dx0", "dx1", "dc0", "dc1", "dyc0", "dyc1"]
DMAS += ["da%d%d%d" % (x, k, j) for x in range(2) for k in range(4) for j in range(2)] + ["drm", "dsw"]
SEMAPHORES = ["qv", "qs", "qt", "qg", "loc"] + DMAS
SEMAPHORES += ["l%d%d%d" % (t, k, x) for t in range(R) for k in range(3) for x in range(2)]
SEMAPHORES += ["r%d%d%d" % (t, k, x) for t in range(R) for k in range(2) for x in range(2)]

CASES = dict(cycle=(0.83, 0.83, 0.86, 0.89, 1.04, 1.13, 1.16, 1.19, 0.83, 1.245, 1.2, 1.1),
             gather=(1.29, 1.29, 1.05, 1.54, 0.99, 1.23, 0.86, 1.66, 1.7, 1.73, 1.5, 1.8),
             scatter=(3.2, 3.7, 3.4, 3.9, 3.9, 3, 4.5, 1.5, 3.2, 5, 4, 4),
             call=(16, 14, 16, 18, 17, 20, 18, 20, 14, 20, 20, 18),
             wake=(170, 150, 150, 100, 270, 110, 170, 130, 170, 200, 200, 200),
             far=(170, 270, 450, 300, 260, 100, 420, 190, 170, 300, 300, 450),
             message=(2000, 3400, 1600, 2400, 2600, 1900, 2300, 1900, 2000, 2400, 2400, 3400),
             first=(3000, 4500, 4600, 3000, 4900, 4800, 4200, 2700, 3000, 4000, 4000, 4000),
             send=(300, 390, 460, 200, 150, 310, 390, 270, 300, 350, 350, 450),
             dma=(1500, 1700, 1500, 2200, 1600, 2400, 1900, 2000, 1500, 2000, 2400, 2400),
             local=(3.4, 3.7, 2.7, 4.5, 4.1, 3.8, 3.2, 2.8, 3.4, 4.2, 4.5, 4.5),
             remote=(17, 11, 13, 23, 16, 19, 14, 31, 17, 18, 25, 30),
             adds=(1.3, 1.3, 1.4, 1.2, 1.3, 1.4, 1.5, 1.5, 1.3, 1.5, 1.6, 1.5),
             gdma=(800, 900, 1000, 700, 700, 900, 900, 1000, 800, 1100, 1200, 1200),
             goal=(143300, 151500, 137000, 167000, 174000, 170800, 174000, 180300, 178000, 197000, 192500, 199500))
KB = dict(dsw=64, drm=448, dch=64, dx0=512, dx1=512, dwt=1, dsl=64, dsb=32, dyc=64, dc0=256, dc1=256)
PLAN = dict(aim=0.6, ramped=False, both=0, behind={},
            lift={"A.P0": (), "A.P1": (), "B.P0": (1024,), "3A.P2": (1024,), "0A.P1": (-1024,)}, ahead=0,
            deal=(1, 40, (0.7, 0.3) + (0,) * 10), lead=0, passes=4, spare=1000,
            moves=((7000, True, 0), (10000, True, 0), (3000, True, 0.85), (7000, False, 0), (28000, False, 0), (5000, False, 0.85)), seed=9, heat=0.0001,
            power=40, spiece=256, early=((3, 1),), halves=[(t, x) for t in range(R) for x in range(2)], spick=[(3, 0), (3, 1)], snames=[0, 1],
            swap=[0, 1])
HELP = {(t, x, k): n for t in (1, 2) for x, k, n in ((0, "P0", 256), (0, "P1", 256), (0, "P2", 512), (1, "P0", 512))}
HELP.update({(0, x, k): n for x, k, n in ((0, "L0", 768), (0, "P0", 512), (0, "P1", 512), (1, "P0", 512), (1, "P2", 256))})
HELP.update({(3, x, k): n for x, k, n in ((1, "L0", 256), (1, "L1", 256), (0, "P1", 256), (0, "P2", 256), (1, "P0", 512), (1, "P1", 512))})
ORDER = ["A.L0 B.L0 A.L1 B.L1 A.P0 A.P1 A.P2 B.P0 A.L2 B.P1 B.P2 B.L2",
         "A.L0 A.P0 A.L1 B.L0 A.P1 B.L1 A.P2 B.P0 A.L2 B.P1 B.P2 B.L2",
         "A.L0 A.P0 A.L1 B.L0 A.P1 B.L1 A.P2 B.P0 A.L2 B.P1 B.P2 B.L2",
         "A.L0 A.P0 A.L1 B.L0 A.P1 B.L1 B.P0 A.P2 B.P1 B.P2 A.L2 B.L2"]
CUTS = {"3B.L2": (1024, 1536, 1792), "A.P0": (), "A.P1": (), "B.L2": (1280,), "A.P2": (), "0A.P1": (1024,)}
NOTE = []
TURN = []
TAG = [None]


def rank_program(g, core, T, topo):
    rank = T.rank_of(core)
    if rank is None:
        return
    A, F, P = AluOpType, ActivationFunctionType, dict(PLAN, **{k: np.array(v, float) for k, v in CASES.items()})
    N = len(T.cores)
    eng = {"v": g.vector, "s": g.scalar, "t": g.tensor, "g": g, "y": g.sync}
    prog, now = [], {"x": 1, "tag": "", "sent": 0}

    def view(name, lo, hi, step=1, parts=128, first=0):
        return (T[name][first:first + parts, lo:hi:step], name, lo, hi, (hi - lo + step - 1) // step, step, parts, None)

    def sub(v, lo, n):
        return view(v[1], v[2] + lo, v[2] + lo + n)

    def half(v, h):
        if h is None:
            return v
        lo = v[2] + v[4] // 2 * v[5] * h
        return view(v[1], lo, lo + (v[4] // 2 - 1) * v[5] + 1, v[5], v[6])

    def part(v, h):
        return view(v[1], v[2], v[3], 1, 64, 64 * h)

    def back(v):
        return (T[v[1]][:, v[2] + (v[4] - 1) * v[5]:v[2] - 1 if v[2] else None:-v[5]],) + v[1:]

    def ind(win, off):
        return (win[0].indirect(off[0]), win, off)

    def flat(vs):
        out = []
        for v in vs:
            out += [v[1], v[2]] if len(v) == 3 else [v]
        return out

    def psum(v):
        return SCRATCH[v[1]][0] == "psum"

    def add(q, kind, call, reads, writes, ns, lag=None, join=None):
        prog.append(dict(q=q, kind=kind, call=call, reads=flat(reads), writes=flat(writes), ns=ns + 0 * P["cycle"], lag=lag, join=join,
                         x=now["x"], tag=now["tag"]))

    def vec(call, out, ins, more=(), rate=None):
        if len(ins[0]) == 3:
            ns = 50 + out[4] * P["gather"]
        else:
            if rate is None:
                rate = 0.5 if all(SCRATCH[v[1]][2] in ("bfloat16", "uint16", "float16") for v in [out] + ins) else 1
            ns = P["call"] + max(64, rate * out[4]) * P["cycle"]
        add("v", "op", call, ins + list(more), [out], ns)

    def cp(out, in_):
        vec(lambda: g.vector.tensor_copy(out[0], in_[0]), out, [in_])

    def tt(out, a, b, o):
        vec(lambda: g.vector.tensor_tensor(out[0], a[0], b[0], o), out, [a, b], rate=1 if len(a) == 3 or psum(a) or psum(b) else 2)

    def ts(out, a, s1, o1, s2=None, o2=None):
        x1, x2 = (s[0] if isinstance(s, tuple) else s for s in (s1, s2))
        more = [s for s in (s1, s2) if isinstance(s, tuple)]
        if o2 is None:
            vec(lambda: g.vector.tensor_scalar(out[0], a[0], x1, None, o1), out, [a], more)
        else:
            vec(lambda: g.vector.tensor_scalar(out[0], a[0], x1, x2, o1, o2), out, [a], more)

    def fill(out, c):
        add("v", "op", lambda: g.vector.memset(out[0], c), [], [out], P["call"] + max(64, out[4] / 2) * P["cycle"])

    def act(out, in_, scale, bias=0.0, token=()):
        add("s", "op", lambda: g.scalar.activation(out[0], in_[0], F.Identity, bias, scale), [in_], list(token) or [out],
            60 + max(64, out[4]) * P["cycle"])

    def take(out, in_):
        add("s", "op", lambda: g.scalar.activation(out[0], in_[0], F.Copy), [in_], [out], 65 + out[4] * P["gather"])

    def iota(out, pattern, base, mul):
        add("g", "op", lambda: g.iota(out[0], pattern, base, mul), [], [out], 130 + 2 * out[4] * P["cycle"])

    def select(out, in_, pattern, o, base, mul, rest=0.0):
        add("g", "op", lambda: g.affine_select(out[0], in_[0], pattern, o, rest, base, mul), [in_], [out], 170 + 2 * out[4] * P["cycle"])

    def band(out, in_, pattern, rest=0.0):
        select(out, in_, [[-s, n] for s, n in pattern], A.is_ge, 0, 1, rest)
        select(out, out, pattern, A.is_ge, 15, -1, rest)

    def mms(out, pairs, start=True, stop=True):
        def call():
            ins = None
            for k, p in enumerate(pairs):
                ins = g.tensor.matmul((p + (out,))[2][0], p[0][0], p[1][0], start and k == 0, stop and k == len(pairs) - 1)
            return ins
        ns = sum(max(min(64, p[0][4]), out[4]) * (4 if SCRATCH[p[0][1]][2] == "float32" else 1) for p in pairs) * P["cycle"]
        add("t", "op", call, [p[0] for p in pairs] + [p[1] for p in pairs], [out], ns)

    def grouped(out, pairs, last):
        mms(out, pairs[:-last], True, False)
        mms(out, pairs[-last:], False, True)

    def dma(q, sem, pairs, reads, writes):
        add(q, "dma", (sem, pairs), reads, writes, 60 * len(pairs), (P["dma"], KB[sem[:3]] * P["local"]))

    def send(dst, src, land, sem, more=()):
        kb = src[4] / (4 if land == "inl" else 2)
        add("g", "send", (dst, src, land, sem), [src] + list(more), [view(land, src[2], src[3])], P["send"] + (0 if now["sent"] else P["first"]),
            (P["message"], kb * P["remote"]))
        now["sent"] = 1

    cols, nxt = {}, {}

    def small(name, n, buf="sm"):
        if name not in cols:
            cols[name] = (buf, nxt.get(buf, 0))
            nxt[buf] = nxt.get(buf, 0) + (n + 7) // 8 * 8
        b, o = cols[name]
        return view(b, o, o + n)

    def partner(t):
        return (rank + 1 + t % (N - 1)) % N

    def asker(t):
        return (rank - 1 - t % (N - 1)) % N

    def lists(t, k, x, buf="outl"):
        lo = ((t * 3 + k) * 2 + x) * HC
        return view(buf, lo, lo + HC)

    def spans(t, k, x, buf, zeros):
        lo, n = (t * 2 + x) * 72 + 56 * k, 24 - 16 * k
        return view(buf, lo + (0 if zeros else n), lo + 2 * n)

    def send_list(t, k, x, more=()):
        send(partner(t), lists(t, k, x), "inl", "l%d%d%d" % (t, k, x), more)

    def names(x, slot):
        return view("nw%d" % x, slot * HC, (slot + 1) * HC)

    def table(x):
        return view("tab%d" % x, 0, 2048)

    def whole(name):
        return view(name, 0, SCRATCH[name][1][1])

    zeroed = small("zeroed", 8)
    for v, c in ((whole("ones"), 1.0), (whole("mkx"), 1.0), (view("mkx", 0, MK, 16), 0.0)):
        fill(v, c)
    act(whole("rin"), view("mkx", 0, R * 144), 0.0, 0.0, [zeroed])
    for x in range(2):
        now["x"], now["tag"] = x, "0%s.start" % "AB"[x]
        dma("y", "dch%d" % x, [(T["nw%d" % x][64 * h:64 * h + 64, 0:HC], T.ch[64 * x:64 * x + 64, h * HC:(h + 1) * HC]) for h in range(2)],
            [], [names(x, 0)])
        dma("sy"[x], "dx%d" % x, [(T["tab%d" % x][64 * h:64 * h + 64, :], T.xt[64 * x:64 * x + 64, :]) for h in range(2)], [], [table(x)])
        cp(lists(0, 0, x), names(x, 0))
        send_list(0, 0, x, [zeroed])
    now["x"], now["tag"] = 0, ""
    dma("y", "dwt", [(T.wti[64 * h:64 * h + 64, z:z + 1], T.wt[64 * z:64 * z + 64, :]) for z in range(2) for h in range(2)],
        [], [view("wti", 0, 2)])
    dma("s", "dsl", [(T.sli[:], T.sl[:])], [], [view("sli", 0, 128)])
    cp(view("slc", 0, 128), view("sli", 0, 128))
    dma("y", "dsb", [(T.slb[0:8, :], T.slc[:])], [view("slc", 0, 128)], [view("slb", 0, 2048)])

    ones, blk, eye, zb, zf = (whole(n) for n in ("ones", "blk", "eye", "zb", "zf"))
    ip, im, sgn = view("ip", 0, 88), view("im", 0, 88), small("sgn", 112, "smb")
    c716, last = small("c716", 64, "smb"), small("last", 32, "smb")
    for v, c in ((zb, 0.0), (c716, 7.0 / 16), (last, 0.0), (sub(last, 8, 8), 15.0),
                 (sgn, -1.0), (sub(sgn, 16, 16), 0.0), (sub(sgn, 96, 8), 1.0)):
        fill(v, c)
    now["tag"] = "soon"
    act(whole("mkn"), whole("mkx"), -512.0, 512.0)
    for v, c in ((whole("up"), 1.5 * 2.0 ** 16), (whole("down"), -1.5 * 2.0 ** 16), (whole("c13"), 2.0 ** -13), (whole("cp64"), 64.0)):
        act(v, sub(ones, 0, 128), c)
    act(whole("shf"), view("mkx", 0, 144), 0.0)
    now["tag"] = ""
    for h, c in enumerate((2.0 ** -7, -2.0 ** -19)):
        add("v", "op", lambda h=h, c=c: g.vector.memset(T.chalf[64 * h:64 * h + 64, :], c), [], [whole("chalf")], P["call"] + 64 * P["cycle"])
    pidx, i16, i8, i77 = (small(n, w, "smi") for n, w in (("pidx", 8), ("i16", 16), ("i8", 8), ("i77", 2)))
    mask, thr = small("mask", 64, "smb"), small("thr", 64, "smb")
    iota(pidx, [[0, 8]], 0, 1)
    iota(i77, [[77, 2]], 0, 0)
    band(blk, ones, [[16, 8], [0, 16]])
    iota(i16, [[1, 16]], 0, 0)
    iota(i8, [[16, 8]], 0, 0)
    select(eye, sub(ones, 0, 128), [[-1, 128]], A.is_equal, 0, 1)
    fill(zf, 0.0)
    for name, zero, c in (("em2", zf, -2.0), ("eyef1", zf, 1.0), ("beye", zb, BIG), ("e512", zb, -512.0)):
        select(whole(name), zero, [[-1, 128]], A.not_equal, 0, 1, c)
    band(ip, sub(ones, 0, 88), [[0, 11], [16, 8]])
    ts(im, ip, -1.0, A.mult)
    for a, b in ((ip, im), (im, ip)):
        select(sub(a, 16, 8), sub(b, 24, 8), [[0, 8]], A.is_ge, 0, 0)
    band(thr, sub(zb, 0, 64), [[16, 8], [0, 8]], -BIG)
    ts(mask, thr, 0.0, A.is_equal)
    ts(small("mask9", 64, "smb"), thr, 0.0, A.is_equal, 2.0 ** -9, A.mult)
    for x in range(2):
        for h in range(2):
            select(view("esl", (2 * x + h) * 112, (2 * x + h + 1) * 112), sgn, [[0, 14], [-100, 2], [-1, 4]], A.is_equal, 100 * h - 4 * x, 1)
    dma("y", "dsw", [(T.swp[:, 64 * h:64 * h + 64], T.eye[:, 64 - 64 * h:128 - 64 * h]) for h in range(2)], [eye], [whole("swp")])
    add("g", "op", lambda: g.iota(T.rmp[:], [[256, 16], [0, 16]], -2048, 0, allow_small_or_imprecise_dtypes=True),
        [], [whole("rmp")], 130 + 512 * P["cycle"])
    cp(view("ramp", 0, 256), whole("rmp"))
    dma("y", "drm", [(T.ramp[:, lo:lo + 256], T.ramp[:, 0:256]) for lo in range(256, HN, 256)], [view("ramp", 0, 256)], [view("ramp", 256, HN)])

    wti, wi, wb = view("wti", 0, 2), small("wi", 8, "smi"), small("wb", 4)
    pm, p8 = small("pm", 8, "smi"), small("p8", 8, "smi")
    kc, c01, pf, pk, ph = small("kc", 2), small("c01", 2), small("pf", 1), small("pk", 1), small("ph", 2)
    bases, mask9, xo, xo2 = small("bases", 32, "smb"), small("mask9", 64, "smb"), small("xo", 8, "smu"), small("xo2", 8, "smu")
    at16 = sub(bases, 8, 8)
    ts(pm, pidx, 15, A.bitwise_and)
    ts(p8, pidx, 7, A.bitwise_and)
    for h, o in enumerate((A.is_ge, A.is_lt)):
        ts(sub(ph, h, 1), sub(pidx, 0, 1), 64.0, o, 1024.0, A.mult)
    ts(pk, sub(pm, 0, 1), 613.0, A.mult)
    cp(pf, sub(pm, 0, 1))
    cp(xo, p8)
    ts(c01, i77, pk, A.add, 64.0, A.mult)
    ts(kc, c01, 992.0, A.add)
    for k, m in enumerate((2047, 3, 2048, 4)):
        ts(sub(wi, 2 * k, 2), wti, m, A.bitwise_and)
    tt(wb, sub(wi, 0, 4), sub(wi, 4, 4), A.subtract)
    for o, c in ((16, 4096.0), (64, 256.0), (112, 8.0)):
        ts(view("shf", o, o + 16), i16, pf, A.is_equal, c, A.mult)
    ts(at16, i8, pf, A.add, 16.0, A.mult)
    ts(sub(bases, 0, 8), i8, pf, A.add)
    for h in range(2):
        ts(sub(bases, 16 + 8 * h, 8), at16, 0.5, A.mult, sub(ph, h, 1), A.add)
    for x in range(2):
        for sign, c in (("p", 1.0), ("m", -1.0)):
            ts(whole("w%s%d" % (sign, x)), blk, sub(wb, x, 1), A.mult, c / 4096, A.mult)
            ts(small("w8%s%d" % (sign, x), 64, "smb"), sub(ip, 24, 64), sub(wb, 2 + x, 1), A.mult, c / 8, A.mult)
    both = small("both", 32)
    fill(both, 0.0)
    for x in range(2):
        ts(sub(xo2, 4 * x, 4), sub(p8, 0, 4), 2.0, A.mult, 16.0 + x, A.add)

    def look(t, x, kind):
        k, own = int(kind[1]), kind[0] == "L"
        at, off = KINDS.index(kind) * HN, lists(t, k, x, "outl" if own else "inl")

        def gather(q):
            def make(lo, n):
                src, dst = ind(table(x), sub(off, lo // 16, n // 16)), view("gb%d" % x, at + lo, at + lo + n)
                if q == "v" and lift:
                    ramp = view("ramp", 0, n)
                    return lambda: g.vector.tensor_tensor(dst[0], src[0], ramp[0], A.add), [src, ramp], [dst], 50 + n * np.maximum(P["gather"], P["both"] * P["cycle"])
                if q == "v":
                    return lambda: g.vector.tensor_copy(dst[0], src[0]), [src], [dst], 50 + n * P["gather"]
                return lambda: g.scalar.activation(dst[0], src[0], F.Copy), [src], [dst], 65 + n * P["gather"]
            return make

        def scan(least):
            o0, o1 = (A.max, A.min) if least else (A.mult, A.max)

            def make(lo, n):
                d0, d1 = view("mkn" if least else "mkx", 0, n), view("gb%d" % x, at + lo, at + lo + n)
                o = view(("m" if own else "p") + ("n%d" if least else "x%d") % x, k * HN + lo, k * HN + lo + n)
                if least:
                    d1, o = back(d1), back(o)
                return lambda: g.vector.tensor_tensor_scan(o[0], d0[0], d1[0], 0.0, o0, o1), [d0, d1], [o], P["call"] + n / 2 * P["cycle"]
            return make

        def twos(least, lo):
            d0, d1 = (view("gb%d" % x, at + lo + h, at + lo + 255 + h, 2) for h in range(2))
            base = lo if own else k * HN + lo
            o = view("lp"[not own] + ("n%d" if least else "x%d") % x, base + 1 - least, base + 256 - least, 2)
            if least:
                d0, d1, o = back(d0), back(d1), back(o)
            op = A.min if least else A.max
            add("v", "op", lambda: g.vector.tensor_tensor_scan(o[0], d0[0], d1[0], 4096.0 if least else -4096.0, op, op), [d0, d1], [o],
                P["call"] + 64 * P["cycle"], join=(None, 2 * len(prog), 1, 0))
        if (t, x, kind) in member:
            return levels(t, member[t, x, kind][0])
        cut = HN - HELP.get((t, x, kind), 0)
        step = now["tag"]
        added = P["lift"].get(step, P["lift"].get(step[1:]))
        lift = P["ramped"] and (not own or added is not None)
        ends = [c for c in CUTS.get(step, CUTS.get(step[1:], (1024,))) if c < cut] + [cut]
        pieces = list(range(0, HN + 1, P["spiece"]))
        plain = [c for c in pieces if c <= cut] if lift else pieces
        upto = HN
        if added is not None:
            upto = min([HN] + [-c for c in added if c < 0])
            plain = [c for c in pieces if c >= upto]
        for q, make, marks, most, what in (("s", gather("s"), [0] + ends if cut else [], HN, ""),
                                           ("v", gather("v"), [cut] + [c for c in pieces if c > cut], MK if lift else HN, "help"),
                                           ("v", scan(False), plain, MK, ""), ("v", scan(True), plain, MK, "min")):
            now["tag"] = step + what
            for lo, hi in zip(marks, marks[1:]):
                add(q, "op", *make(lo, hi - lo), join=(make, lo, hi - lo, most))
        cut = cut if lift else upto
        if added is not None:
            now["tag"] = step + "lift"
            marks = [0] + [c for c in added if 0 < c < cut] + [cut] if cut else []
            for j, (lo, hi) in enumerate(zip(marks, marks[1:])):
                v, ramp = view("gb%d" % x, at + lo, at + hi), view("ramp", 0, hi - lo)
                add("g", "dma", ("da%d%d%d" % (x, k + own, j), [(v[0], ramp[0], A.add)]), [v, ramp], [v], P["gdma"], (P["dma"], (hi - lo) / 4 * P["local"] * P["adds"]))
            cut = 0
        now["tag"] = step + "twos"
        for lo in range(cut, upto, 256):
            twos(0, lo)
            twos(1, lo)
        if own and added is not None:
            y = view("pq%d" % x, 2 * HC, 3 * HC)
            grouped(y, [(whole("meye"), view("ramp", 0, HN, 16)), (eye, res("lx", x, 0))], 1)
            cp(res("mx", x, k), y)

    member, done = {}, set()
    for t in range(R):
        for slot, batch in enumerate(BATCHES[t].split()):
            for i, w in enumerate(batch.split("+")):
                member[t, "AB".index(w[0]), w[2:]] = (slot, i, batch.count("+") + 1)

    def levels(t, slot):
        if (t, slot) in done:
            return
        done.add((t, slot))
        keep, batch = dict(now), sorted((v[1], k[1], k[2]) for k, v in member.items() if k[0] == t and v[0] == slot)
        n = len(batch)
        gq, wide, each = "gq%d%d" % (n, slot), 8 * n, 16 // n
        for i, x, kind in batch:
            now["x"], step = x, "%d%s.%s" % (t, "AB"[x], kind)
            off = lists(t, int(kind[1]), x, "inl")
            for j in range(each):
                m = n * j + i
                src, dst = ind(table(x), sub(off, wide * j, wide)), (T[gq][:, :, :, 8 * m:8 * m + 8], gq, 0, n * HN, 16 * wide, 1, 128, m)
                if (each - j) * 16 * wide <= HELP.get((t, x, kind), 0):
                    now["tag"] = step + "help"
                    add("v", "op", lambda src=src, dst=dst, m=m: g.vector.tensor_scalar(dst[0], src[0], 256.0 * m - 2048.0, None, A.add),
                        [src], [dst], 50 + dst[4] * P["gather"], join=(None, 2 * len(prog), 1, 0))
                else:
                    now["tag"] = step
                    add("s", "op", lambda src=src, dst=dst, m=m: g.scalar.activation(dst[0], src[0], F.Identity, 256.0 * m - 2048.0),
                        [src], [dst], 65 + dst[4] * P["gather"], join=(None, 2 * len(prog), 1, 0))
        now["tag"] = step + "scan"
        for a in range(wide):
            for buf, o, st in (("qx", A.max, 1), ("qn", A.min, -1)):
                out = "%s%d%d" % (buf, n, slot)
                d, ov = (None, gq, 256 * a, 256 * a + 256, 128, 1, 128, None), view(out, 128 * a, 128 * a + 128)
                ov = ov if st > 0 else back(ov)
                add("v", "op", lambda ov=ov, o=o, st=st, a=a: g.vector.tensor_tensor_scan(ov[0], T[gq][:, a, 0, ::st], T[gq][:, a, 1, ::st], -4096.0 * st, o, o),
                    [d], [ov], P["call"] + 64 * P["cycle"], join=(None, 2 * len(prog), 1, 0))
        now.update(keep)

    def turned(t, x, k):
        return member.get((t, x, "P%d" % k), (0, 0, 1))[2]

    def res(buf, x, k, t=None):
        if buf[0] == "p" and (t, x, "P%d" % k) in member:
            slot, i, n = member[t, x, "P%d" % k]
            return view("q%s%d%d" % (buf[1], n, slot), 8 * i + (7 if buf[1] == "x" else 0), n * 1024, 8 * n)
        return view("%s%d" % (buf, x), k * HN + (15 if buf[1] == "x" else 0), (k + 1) * HN, 16)

    def span(side, x, k, sign, lo, n, t=None):
        p, m = sub(ip, lo, n), sub(im, lo, n)
        return [(res(side + "x", x, k, t), p if sign > 0 else m), (res(side + "n", x, k, t), m if sign > 0 else p)]

    def slack(t, j, x, lo, n):
        o = (t * 2 + j) * 2 * HC
        return [(view("slb", o + h * HC, o + (h + 1) * HC, 1, 8), view("esl", (2 * x + h) * 112 + lo, (2 * x + h) * 112 + lo + n, 1, 8))
                for h in range(2)]

    def shifted(out, r, turn=0, less=0):
        return [(view("shf", 48 * less + 16 - 16 * (b % 2), 48 * less + 48 - 16 * (b % 2)), view(r[1], r[2] + (b + 4 * turn) % 8, r[3], 8),
                 view(out[1], out[2], out[3], 1, 32, 32 * (b // 2))) for b in range(8)]

    def rounding(n):
        return [(whole("up"), sub(ones, 0, n)), (whole("down"), sub(ones, 0, n))]

    def product(x, k, h):
        lo, n = (0, HC) if h is None else (64 * h, 64)
        y = half(res("mx", x, k), h)
        uc, v = view("uc%d" % x, HC * k + lo, HC * k + lo + n), view("pq%d" % x, HC, HC + n) if h else view("pu%d" % x, 0, n)
        one = sub(ones, 0, n)
        grouped(v, [(whole("chalf"), one), (whole("wm%d" % x), y)] + rounding(n) + [(whole("c13"), one), (whole("wp%d" % x), y)], 5)
        tt(uc, v, sub(names(x, k), lo, n), A.mult)
        return uc

    def propose(t, x, j, uc, h):
        raw, new = half(whole("ud%d" % x), h), half(names(x, j + 1), h)
        ts(raw, uc, 4096.0, A.mult, sub(c01, j, 1), A.add)
        ts(new, raw, 6, A.arith_shift_right, 2047, A.bitwise_and)
        cp(half(lists(t, j + 1, x), h), new)

    def kappa():
        kv, kr, ne = small("kv", 16), small("kr", 1), small("ne", 16, "smb")
        tt(ne, sub(both, 0, 16), sub(both, 16, 16), A.is_equal)
        d0, d1 = sub(ones, 0, 16), view("pq0", 64, 80)
        mms(d1, [(whole("cp64"), ne)])
        vec(lambda: g.vector.tensor_tensor_scan(kv[0], d0[0], d1[0], -992.0, A.mult, A.add), kv, [d0, d1])
        ts(kr, sub(kv, 15, 1), 1.5 * 2.0 ** 34, A.add, -1.5 * 2.0 ** 34, A.add)
        ts(c01, kc, sub(kv, 15, 1), A.add, kr, A.subtract)

    def stream(t, x):
        def sv(name, n, buf="sm"):
            return small("%s%d" % (name, x), n, buf)

        def tag(w):
            now["tag"] = "%d%s.%s" % (t, "AB"[x], w)
        z = "pz%d" % x
        rise = span("m", x, 0, -1, 0, 88), span("m", x, 1, 1, 0, 88)
        rise += (span("l", x, 0, 1, 0, 88) if P["lift"].get("%d%s.L2" % (t, "AB"[x]), P["lift"].get("AB"[x] + ".L2")) is not None else span("m", x, 2, 1, 0, 88),)

        def cut(pairs, lo, n):
            return [(l, sub(r, lo, n)) for l, r in pairs]
        tag("L0")
        look(t, x, "L0")
        tag("first")
        for h in range(2) if (t, x) in P["halves"] else (None,):
            propose(t, x, 0, product(x, 0, h), h)
        send_list(t, 1, x)
        tag("L1")
        look(t, x, "L1")
        tag("second")
        r, so = sv("rb", 64, "smb"), sv("so", 8, "smu")
        product(x, 1, None)
        at = view("pl%d" % x, 0, 8)
        grouped(view(z, 0, 64), slack(t, 0, x, 32, 64) + cut(rise[0] + rise[1], 24, 64), 1)
        tt(r, view(z, 0, 64), thr, A.is_le)
        grouped(at, [(eye, at16)] + shifted(at, r) + [(eye, at16)], 9)
        ts(so, at, 1.0 / 32, A.mult)
        propose(t, x, 1, ind(whole("uc%d" % x), so), None)
        send_list(t, 2, x)
        yield
        for kind in ("P0", "P1", "P2"):
            tag(kind)
            look(t, x, kind)
        tag("answer")
        o0, o2 = turned(t, x, 0), turned(t, x, 2)
        sign = 1 if o2 == 1 else -1
        if o0 == o2:
            out = view("pq%d" % x, 0, 24)
            pairs = span("p", x, 0, -1, 24, 24, t) + span("p", x, 1, 1, 24, 24, t), span("p", x, 0, sign, 24, 8, t)
        else:
            out = view("pq%d" % x, 0, 32)
            low = span("p", x, 0, -1, 24, 32, t)
            pairs = low[:1] + [p + (sub(out, 0, 24),) for p in span("p", x, 1, 1, 24, 24, t)] + low[1:], []
        for k, out, pairs in ((0, out, pairs[0]), (1, view("pq%d" % x, 32, 40), pairs[1] + span("p", x, 2, -sign, 24, 8, t))):
            v = sub(spans(t, k, x, "ro", False), 0, out[4])
            grouped(out, pairs, 1)
            ts(v, out, float(k * sign), A.add)
            send(asker(t), v, "rin", "r%d%d%d" % (t, k, x))
        tag("L2")
        look(t, x, "L2")
        tag("truth")
        z2, hd, x12, sel, ne0 = view(z, 64, 112), sv("hd", 48), sv("x12", 16), sv("sel", 8), sv("ne0", 16, "smb")
        grouped(z2, slack(t, 0, x, 0, 48) + cut(rise[0] + rise[1], 0, 48) + [(whole("eyef%d" % o0), spans(t, 0, x, "rin", True))], 1)
        ts(hd, z2, 0.0, A.is_le, 0.5, A.mult)
        tt(x12, sub(z2, 16, 16), sub(hd, 0, 16), A.mult)
        tt(ne0, sub(hd, 0, 16), sub(hd, 32, 16), A.not_equal)
        tag("decide")
        w2 = view("pu%d" % x, 128, 144)
        pairs = slack(t, 1, x, 96, 16) + cut(rise[0], 16, 16)
        if o0 != o2:
            pairs += [(whole("eyef%d" % o0), sub(spans(t, 0, x, "rin", False), 24, 8), sub(w2, 8, 8))]
        pairs += [(whole("em2"), x12), (whole("beye"), ne0)]
        if o2 == 1:
            grouped(w2, pairs + cut(rise[2], 16, 16), 2)
        else:
            mms(w2, pairs, True, False)
            mms(w2, cut(rise[2], 16, 16), False, False)
            mms(w2, [(whole("eyef%d" % o2), spans(t, 1, x, "rin", True))], False, True)
        fv, fy = sv("fv", 32, "smu"), view("fy%d" % x, 0, HC)
        no, fo, d0 = sub(fv, 0, 8), sub(fv, 8, 8), sub(hd, 32, 8)
        early, swap = (t, x) in P["early"], t < R - 1 and x in P["swap"]
        n = 2 if swap else 1
        vo = sub(fv, 16, 8 * n)

        def low(out, y, more=()):
            grouped(out, [(eye, c716), (y, sv("w8m", 64, "smb"))] + rounding(64) + list(more) + [(y, sv("w8p", 64, "smb"))], 4 + len(more))
        if early:
            tag("early")
            r0, ra, dm, rc = (sv(w, 64, "smb") for w in ("r0", "ra", "dm", "rc"))
            at, ya, rq = view("pl%d" % x, 40, 48), view("old%d" % x, 0, HC), view(z, 192, 256)
            tt(r0, ind(d0, sub(xo, 0, 4)), mask, A.mult)
            grouped(at, [(eye, at16)] + shifted(at, r0) + [(eye, sub(last, 8, 8))], 9)
            cp(fo, at)
            cp(ya, ind(view("mx%d" % x, 0, 2 * HN), fo))
            low(view(z, 128, 192), ya)
            tt(ra, view(z, 128, 192), mask9, A.mult)
            low(rq, res("mx", x, 2), [(whole("e512"), ra)])
            tag("decide")
            tt(view(both[1], both[2] + x, both[3], 2), w2, spans(t, 1, x, "rin", True), A.is_lt)
            tt(dm, ind(both, sub(xo2, 4 * x, 4)), mask, A.mult)
            tt(rc, rq, dm, A.mult)
            tt(r, dm, r0, A.max)
            at = view("pl%d" % x, 48, 64 + 8 * n)
            moves = [[m for h in range(n) for m in shifted(sub(at, 16 + 8 * h, 8), v, h, less)] for v, less in ((ra, 0), (rc, 2))]
            moves[1] += shifted(sub(at, 8, 8), r) + shifted(sub(at, 0, 8), r, 0, 1)
            grouped(at, [(eye, sub(bases, 0, at[4]))] + moves[0] + moves[1] + [(eye, sub(last, 0, at[4]))], len(moves[1]) + 1)
            tag("pick")
            cp(sub(fv, 0, at[4]), at)
        else:
            if o2 == 1:
                tt(view(both[1], both[2] + x, both[3], 2), w2, spans(t, 1, x, "rin", True), A.is_lt)
            else:
                ts(view(both[1], both[2] + x, both[3], 2), w2, 0.0, A.is_lt)
            tt(sel, view(both[1], both[2] + 16 + x, both[3], 2), d0, A.max)
            tt(r, ind(sel, sub(xo, 0, 4)), mask, A.mult)
            at = view("pl%d" % x, 8, 24)
            moves = shifted(sub(at, 8, 8), r) + shifted(sub(at, 0, 8), r, 0, 1)
            grouped(at, [(eye, sub(bases, 0, 16))] + moves + [(eye, sub(last, 0, 16))], 17)
            tag("pick")
            cp(sub(fv, 0, 16), at)
        pick = take if (t, x) in P["spick"] else cp
        last_pick = early and t == R - 1
        if last_pick:
            ts(view("hx%d" % x, 0, HC), ind(view("mx%d" % x, 0, 3 * HN), fo), 0.5, A.mult)
            src, dst = ind(table(x), vo), view("hx%d" % x, HC, 2 * HC)
            add("s", "op", lambda: g.scalar.activation(dst[0], src[0], F.Identity, -0.25, 0.5), [src], [dst], 65 + HC * P["gather"])
        else:
            pick(fy, ind(view("mx%d" % x, 0, 3 * HN), fo))
        tag("names")
        picked = ind(view("nw%d" % x, 0, 3 * HC), no)
        if t < R - 1:
            cp(lists(t + 1, 0, x), picked)
            send_list(t + 1, 0, x)
            cp(names(x, 0), lists(t + 1, 0, x))
        else:
            y = view("uc%d" % x, 0, HC)
            (take if x in P["snames"] else cp)(y, picked)
            dma("y", "dyc%d" % x, [(T.yc[64 * x:64 * x + 64, h * HC:(h + 1) * HC], part(y, h)[0]) for h in range(2)], [y], [])
        tag("update")
        tab, xs, xh = table(x), view("xs%d" % x, 0, HC), view("xs%d" % x, HC, 2 * HC)
        if not early:
            rest = view(z, 128, 192)
            low(rest, fy)
            tt(r, rest, mask9, A.mult)
            at = view("pl%d" % x, 24, 24 + 8 * n)
            moves = [m for h in range(n) for m in shifted(sub(at, 8 * h, 8), r, h)]
            grouped(at, [(eye, sub(bases, 16, 8 * n))] + moves + [(eye, sub(zb, 0, 8 * n))], 8 * n + 1)
            cp(vo, at)
        if swap:
            old, xh = view("old%d" % x, 0, HC), whole("xs%d" % x)
            cp(old, ind(tab, sub(vo, 0, 8)))
            for h, turn in enumerate((eye, whole("swp"))):
                grouped(view(z, (2 + h) * HC, (3 + h) * HC), [(turn, fy), (turn, old)], 1)
            ts(xh, view(z, 2 * HC, 4 * HC), 0.5, A.mult, -0.25, A.add)
        elif last_pick:
            tt(xh, view("hx%d" % x, 0, HC), view("hx%d" % x, HC, 2 * HC), A.add)
        else:
            tt(xs, ind(tab, vo), fy, A.add)
            ts(xh, xs, 1, A.arith_shift_right)
        out = ind(tab, vo)
        add("v", "op", lambda: g.vector.tensor_copy(out[0], xh[0]), [xh, vo], [tab], 50 + xh[4] * P["scatter"])
        if t == R - 1:
            dma("y", "dc%d" % x, [(T.yx[64 * x:64 * x + 64, 1024 * h:1024 * (h + 1)], part(half(tab, h), h)[0]) for h in range(2)], [tab], [])
        elif not swap:
            dma("y", "dc%d" % x, [(part(half(tab, h), 1 - h)[0], part(half(tab, h), h)[0]) for h in range(2)], [tab], [tab])

    for t in range(R):
        if t:
            now["x"], now["tag"] = 0, "%dkappa" % t
            kappa()
        runs = [stream(t, x) for x in range(2)]
        for _ in range(2):
            for x in range(2):
                now["x"] = x
                next(runs[x], None)

    issue(g, T, topo, core, eng, plan(prog, P), {"inl": asker, "rin": partner})


def plan(prog, P):
    if not TURN:
        TURN.extend(arrange(prog, P))
    out = []
    for parts in TURN:
        o = dict(prog[parts[0]])
        if len(parts) > 1:
            o.update(call=o["join"][0](o["join"][1], sum(prog[i]["join"][2] for i in parts))[0],
                     reads=[v for i in parts for v in prog[i]["reads"]], writes=[v for i in parts for v in prog[i]["writes"]])
        out.append(o)
    return out


def arrange(prog, P):
    n = len(prog)
    pred, acc, last = [set() for _ in prog], {}, {}
    for i, o in enumerate(prog):
        for vs, w in ((o["reads"], False), (o["writes"], True)):
            for v in vs:
                for lo, hi, aw, j, c in acc.get(v[1], ()):
                    if lo < v[3] and v[2] < hi and (w or aw) and j != i and (c is None or v[7] is None or c == v[7]):
                        pred[i].add(j)
        for vs, w in ((o["reads"], False), (o["writes"], True)):
            for v in vs:
                lst = acc.setdefault(v[1], [])
                if w:
                    lst[:] = [a for a in lst if not (v[2] <= a[0] and a[1] <= v[3] and v[7] in (None, a[4]))]
                lst.append((v[2], v[3], w, i, v[7]))
        if o["q"] == "t":
            bank = o["writes"][0][1]
            if bank in last:
                pred[i].add(last[bank])
            last[bank] = i
    above = [0] * n
    for i in range(n):
        pred[i] = sorted(j for j in pred[i] if not any(above[k] >> j & 1 for k in pred[i]))
        for j in pred[i]:
            above[i] |= above[j] | 1 << j
    succ = [[] for _ in prog]
    for i in range(n):
        for j in pred[i]:
            succ[j].append(i)
    true = [list(v) for v in pred], [list(v) for v in succ]
    steps = ["%d%s" % (t, w) for t in range(R) for w in ORDER[t].split()]
    looks = sorted((steps.index(o["tag"]), i) for i, o in enumerate(prog) if o["q"] == "s" and o["join"])
    pairs = [(i, j) for (_, i), (_, j) in zip(looks, looks[1:])]
    last = {o["tag"]: i for i, o in enumerate(prog) if o["q"] == "g"}
    pairs += [(last[w[0] + P["behind"][w[1:]]], i) for w, i in last.items() if w[1:] in P["behind"] and w[0] != "0"]
    P["soft"] = set(pairs)
    for i, j in pairs:
        pred[j].append(i)
        succ[i].append(j)
    turn, left = [i for i in range(n) if not pred[i]], [len(v) for v in pred]
    for i in turn:
        for j in succ[i]:
            left[j] -= 1
            turn += [] if left[j] else [j]
    ns, lag = [float(o["ns"][0]) for o in prog], [float(sum(o["lag"])[0]) + P["spare"] if o["lag"] else 0.0 for o in prog]
    wake, rank = float(P["wake"][0]), [0.0] * n
    for i in turn[::-1]:
        rank[i] = ns[i] + lag[i] + max([(prog[j]["q"] != "s" or prog[i]["q"] != "s") * wake + rank[j] for j in succ[i]], default=0.0)

    def place(turn, first, back):
        at, gaps = [0.0] * n, {q: [[0.0, 1e12]] for q in "vstgy"}
        for i in turn:
            t = max([at[j] + ns[j] + (prog[j]["q"] != "s" or prog[i]["q"] != "s") * wake + (0 if back else lag[j]) for j in first[i]], default=0.0)
            t += lag[i] if back else 0
            gs = gaps[prog[i]["q"]]
            k = len(gs) - 1
            while k > 0 and gs[k - 1][1] > t:
                k -= 1
            while gs[k][1] - max(gs[k][0], t) < ns[i]:
                k += 1
            lo, hi = gs[k]
            at[i] = max(lo, t)
            gs[k:k + 1] = [x for x in ([lo, at[i]], [at[i] + ns[i], hi]) if x[1] - x[0] > 40]
        return at

    if P["deal"]:
        return improve(prog, P, true[0], true[1], deal(prog, P, pred, succ, turn))
    lead = [rank[i] + (0 if o["join"] else P["lead"]) for i, o in enumerate(prog)]
    for i in turn[::-1]:
        lead[i] = max([lead[i]] + [lead[j] + 1 for j in succ[i]])
    turn, best = sorted(range(n), key=lambda i: -lead[i]), None
    for _ in range(P["passes"]):
        at = place(turn, pred, False)
        end = max(at[i] + ns[i] + lag[i] for i in range(n))
        if best is None or end < best:
            best, start = end, at
        late = place(sorted(range(n), key=lambda i: -(at[i] + ns[i] + lag[i])), succ, True)
        turn = sorted(range(n), key=lambda i: -(late[i] + ns[i]))
    return improve(prog, P, true[0], true[1], [i for _, i in sorted((start[i], i) for i in range(n))])


def deal(prog, P, pred, succ, turn):
    n, rng = len(prog), np.random.default_rng(P["seed"])
    q, join, tags = ([o[k] for o in prog] for k in ("q", "join", "tag"))
    banks = [{v[1] for v in o["reads"] + o["writes"] if SCRATCH[v[1]][0] == "psum"} for o in prog]
    tries, fit, mix = P["deal"]
    mix, ahead = np.array(mix, float), dict(v=0, s=P["ahead"], t=P["ahead"], g=P["ahead"], y=P["ahead"])

    def mean(v):
        return float(np.dot(v + 0 * mix, mix))
    ns, lag = [mean(o["ns"]) for o in prog], [(mean(o["lag"][0]), mean(o["lag"][1])) if o["lag"] else None for o in prog]
    wake, begin = [mean(P["far"] if o["kind"] == "send" else P["wake"]) for o in prog], {"v": mean(P["call"]), "s": 0}
    loose = [[j for j in pred[i] if (q[i] != "t" or q[j] != "t") and (j, i) not in P["soft"]] for i in range(n)]

    def backwards(urge):
        left, end, free = [len(v) for v in succ], [0.0] * n, {e: 0.0 for e in "vstgy"}
        can, since = {e: [] for e in free}, [sum(lag[i] or ()) for i in range(n)]
        for i in range(n):
            if not left[i]:
                can[q[i]].append(i)
        for _ in range(n):
            t, e = min((max(free[e], min([since[i] for i in cs])), e) for e, cs in can.items() if cs)
            near = [(urge[i], i, since[i]) for i in can[e] if since[i] <= t + 1000]
            top = max(near)
            if top[2] > t:
                top = max([x for x in near if max(x[2], t) + ns[x[1]] <= top[2] + fit], default=top)
            i = top[1]
            can[e].remove(i)
            free[e] = end[i] = max(t, top[2]) + ns[i]
            for k in pred[i]:
                left[k] -= 1
                if not left[k]:
                    since[k] = max([end[j] + (k in loose[j]) * wake[k] for j in succ[k]]) + sum(lag[k] or ())
                    can[q[k]].append(k)
        return end

    chainlen = [0.0] * n
    for i in turn[::-1]:
        chainlen[i] = ns[i] + sum(lag[i] or ()) + max([(i in loose[j]) * wake[i] + chainlen[j] for j in succ[i]], default=0.0)

    def once(boost, base):
        rank = [r + boost.get(w, 0) + (w == "soon") * 1e6 for r, w in zip(base, tags)]
        left, ready, gate = [len(v) for v in pred], [0.0] * n, [None] * n
        free, tail, last, order = {e: 0.0 for e in "vstgy"}, {}, None, []
        can, since = {e: [] for e in free}, [0.0] * n
        for i in range(n):
            if not left[i]:
                can[q[i]].append(i)

        def first(i):
            t = since[i]
            for b in banks[i]:
                k = tail.get(b)
                if k is not None and q[k] != q[i] and ready[k] > t:
                    t = ready[k]
            return t
        for _ in range(n):
            best = None
            for e, cs in can.items():
                if cs:
                    at = [first(i) for i in cs]
                    t = max(free[e], min(at))
                    if best is None or t - ahead[e] < best[4]:
                        best = t, e, cs, at, t - ahead[e]
            t, e, cs, at, _ = best
            near = [(rank[i], -i, a) for i, a in zip(cs, at) if a <= t + 1000]
            top = max(near)
            if top[2] > t:
                top = max([x for x in near if max(x[2], t) + ns[-x[1]] <= top[2] + fit], default=top)
            i = -top[1]
            cs.remove(i)
            j = tail.get(e)
            t = max(t, top[2])
            gate[i] = j if j is not None and free[e] >= top[2] else max(loose[i] + [tail[b] for b in banks[i] if b in tail], key=lambda k: ready[k], default=None)
            glued = j is not None and join[i] and join[j] and join[j][0] is join[i][0] and join[j][1] + join[j][2] == join[i][1]
            free[e] = t = t + ns[i] - (begin[e] if glued else 0)
            tail[e] = i
            for b in banks[i]:
                tail[b] = i
            if lag[i]:
                t += lag[i][0]
                if last is not None:
                    t = max(t, ready[last] - wake[last])
                t, last = t + lag[i][1], i
            ready[i] = t + wake[i]
            order.append(i)
            for k in succ[i]:
                left[k] -= 1
                if not left[k]:
                    since[k] = max([ready[j] for j in loose[k]], default=0.0)
                    can[q[k]].append(k)
        return max(ready), order, gate, ready

    boost, best, base = {}, None, chainlen
    for _ in range(P["passes"]):
        end, order, gate, ready = once({}, base)
        if best is None or end < best[0]:
            best = end, base
        base = backwards([r - w - sum(l or ()) for r, w, l in zip(ready, wake, lag)])
    best, base = None, best[1]
    names = sorted(set(tags))
    for step in range(tries):
        trial = dict(boost)
        for _ in range(min(step, 1 + int(rng.integers(3)))):
            w = names[rng.integers(len(names))] if rng.random() < 0.5 else chain[rng.integers(len(chain))]
            trial[w] = trial.get(w, 0) + float(rng.normal()) * 1500
        end, order, gate, ready = once(trial, base)
        if best is None or end <= best[0]:
            best, boost = (end, order), trial
            i, chain = max(range(n), key=lambda k: ready[k]), []
            while i is not None:
                chain.append(tags[i])
                i = gate[i]
    return best[1]


def improve(prog, P, pred, succ, order):
    n, rng = len(prog), np.random.default_rng(P["seed"])
    q, ns, lag, join = ([o[k] for o in prog] for k in ("q", "ns", "lag", "join"))
    wake = [P["far"] if o["kind"] == "send" else P["wake"] for o in prog]
    banks = [{v[1] for v in o["reads"] + o["writes"] if SCRATCH[v[1]][0] == "psum"} for o in prog]
    parts, zero = [[i] for i in range(n)], 0 * P["cycle"]
    load, glue, begin = P["goal"], [True], {"v": P["call"], "s": 65}

    def follows(i, j):
        return join[i] and join[j] and join[j][0] is join[i][0] and join[i][1] + join[i][2] == join[j][1] and join[i][2] + join[j][2] <= join[i][3]

    def tails(order, gate):
        rest, after, behind = [zero] * n, [zero] * n, zero
        for i in order[::-1]:
            t = after[i] + wake[i]
            if lag[i]:
                behind = np.maximum(t, behind) + lag[i][1]
                t = behind + lag[i][0]
            j, waits = gate[i]
            t = np.maximum(t, rest[i]) + ns[i]
            if j is not None:
                rest[j] = t = t - begin[q[i]] if glue[0] and join[i] and follows(j, i) else t
            rest[i] = t
            for k in waits:
                after[k] = np.maximum(after[k], t)
        return rest, after

    def run(order, first, old, moved=None):
        start, end, ready, gate = (list(v) for v in old[:4])
        tail, last = {}, None
        for i in order[:first]:
            tail[q[i]] = i
            for b in banks[i]:
                tail[b] = i
            if lag[i]:
                last = i
        reach, bad, low, same = 0, set(), zero, zero
        for k, i in enumerate(order[first:], first):
            if moved and k > moved[0]:
                if k == moved[0] + 1:
                    was = {r: j for j in moved[1][first:k] for r in uses[j]}
                    bad.update(r for r, j in was.items() if (last if r == "dma" else tail[r]) != j)
                if not bad and k > reach:
                    return start, end, ready, gate, old[4], old[5], old[6]
                if (k - moved[0]) % 30 == 0 and float(np.sum((np.where(same > old[4] - 30, low, np.maximum(low, old[4])) / load) ** P["power"])) > moved[4]:
                    return None
            e = q[i]
            j = tail.get(e)
            t = zero if j is None else end[j]
            waits = [j for j in pred[i] if e != "t" or q[j] != "t"]
            for b in banks[i]:
                k = tail.get(b)
                if k is not None and q[k] != e:
                    waits.append(k)
                tail[b] = i
            for k in waits:
                t = np.maximum(t, ready[k])
            start[i], gate[i], tail[e] = t, (j, waits), i
            end[i] = t = t + (ns[i] - begin[e] if glue[0] and join[i] and j is not None and follows(j, i) else ns[i])
            if lag[i]:
                t = t + lag[i][0]
                if last is not None:
                    t = np.maximum(t, ready[last] - wake[last])
                t, last = t + lag[i][1], i
            ready[i] = t = t + wake[i]
            if moved:
                if k > moved[0] + 180:
                    moved = None
                elif t.tobytes() != old[2][i].tobytes():
                    bad.update(uses[i])
                    reach = max([reach] + [moved[2][j] for j in succ[i]])
                    if k > moved[0]:
                        low, same = np.maximum(low, start[i] + moved[3][i]), np.maximum(same, old[0][i] + moved[3][i])
                elif k > moved[0]:
                    bad.difference_update(uses[i])
        final = [i for i in order[-40:] if not succ[i]]
        time = np.max([ready[i] for i in final], 0)
        return start, end, ready, gate, time, float(np.sum((time / load) ** P["power"])), final

    def shift(order, a, b):
        lo, hi, rel = (b, a, pred) if b < a else (a, b, succ)
        drag = {order[a]}
        for i in (order[lo:hi + 1][::-1] if b < a else order[lo:hi + 1]):
            if i in drag:
                drag.update(rel[i])
        mine, rest = [i for i in order[lo:hi + 1] if i in drag], [i for i in order[lo:hi + 1] if i not in drag]
        return order[:lo] + (mine + rest if b < a else rest + mine) + order[hi + 1:], lo

    now = [[None] * n] * 4
    uses = [[q[i]] + list(banks[i]) + (["dma"] if lag[i] else []) for i in range(n)]
    for moves, glue[0], since in P["moves"]:
        chain, stale = None, 99
        now = run(order, 0, now)
        at = {i: k for k, i in enumerate(order)}
        for step in range(moves):
            start, end, ready, gate, time, worth, final = now
            if stale >= 12:
                (rest, after), stale = tails(order, gate), 0
            if chain is None or step % 16 == 0:
                weight = (time / load) ** P["power"]
                c = int(rng.choice(len(load), p=weight / weight.sum()))
                i, chain = max(final, key=lambda i: ready[i][c]), []
                while i is not None and at[i] >= since * len(order):
                    j, waits = gate[i]
                    idle = j is None or end[j][c] < start[i][c] - 1
                    chain.append((i, j, idle))
                    i = max(waits, key=lambda k: ready[k][c], default=None) if idle else j
                chain = [x for x in chain if x[1] is not None and (x[2] or gate[x[1]][0] is None or rng.random() < 0.3 or not join[x[0]])]
            i, j, idle = chain[rng.integers(len(chain))]
            same = [k for k in order[max(0, at[i] - 60):at[i] + 120] if q[k] == q[i]]
            me, pick = same.index(i), rng.random()
            if pick < P["aim"]:
                share = (time / load) ** P["power"]
                if pick < P["aim"] / 2 and not idle:
                    low = max([at[k] for k in pred[i]], default=-1)
                    spots = [k for k in range(1, me) if at[same[k]] > low]
                    if not spots:
                        continue
                    can = np.max([zero] + [ready[k] for k in pred[i]], 0)
                    late = np.array([np.maximum(can, end[same[k - 1]]) + ns[i] + rest[same[k]] for k in spots]) - time
                    a, b = at[i], at[same[spots[int(np.argmin(np.maximum(late, 0) @ share + rng.random(len(spots)) * share.sum() * 20))]]]
                else:
                    j = same[max(0, me - 1 - int(rng.integers(3)))]
                    high = min([at[k] for k in succ[j]], default=n)
                    spots = [k for k in range(me, len(same) - 1) if at[same[k]] < high]
                    if not spots or j == i:
                        continue
                    own = ns[j] + wake[j] + after[j] + (lag[j][0] + lag[j][1] if lag[j] else 0)
                    late = np.array([end[same[k]] + np.maximum(own, ns[j] + rest[same[k + 1]]) for k in spots]) - time
                    a, b = at[j], at[same[spots[int(np.argmin(np.maximum(late, 0) @ share + rng.random(len(spots)) * share.sum() * 20))]]]
            elif idle and me + 1 < len(same):
                a, b = at[same[me + 1 + int(rng.integers(min(24, len(same) - me - 1)))]], at[i]
            elif rng.random() < 0.5 or me + 1 == len(same):
                a, b = at[i], at[same[max(0, me - 1 - int(rng.integers(6)))]]
            else:
                a, b = at[same[max(0, me - 1 - int(rng.integers(3)))]], at[same[me + int(rng.integers(min(4, len(same) - me)))]]
            if a == b:
                continue
            other, first = shift(order, a, b)
            most = worth * (1 + P["heat"] * (1 - step / moves) * rng.random())
            new = run(other, first, now, (max(a, b), order, at, rest, most))
            if new and new[5] <= most:
                stale += 1 if new[5] == worth else 4
                order, now, chain = other, new, chain if new[5] == worth else None
                at.update((i, k) for k, i in enumerate(order[first:max(a, b) + 1], first))
        k, glue[0] = 0, False
        now = run(order, 0, now)
        while k < len(order):
            i = order[k]
            j = next((j for j in order[k + 1:] if q[j] == q[i]), None) if join[i] else None
            k += 1
            if j is None or not follows(i, j):
                continue
            for a, b in ((order.index(j), k), (k - 1, order.index(j) - 1)):
                other, first = shift(order, a, b) if a != b else (order, k - 1)
                if other.index(j) != other.index(i) + 1:
                    continue
                keep = ns[i], join[i], pred[i], succ[i]
                ns[i], join[i] = join[i][0](join[i][1], join[i][2] + join[j][2])[3], (join[i][0], join[i][1], join[i][2] + join[j][2], join[i][3])
                pred[i], succ[i] = sorted(set(pred[i] + pred[j]) - {i}), sorted(set(succ[i] + succ[j]) - {j})
                for m in succ[j]:
                    pred[m] = [i if z == j else z for z in pred[m]]
                other = [z for z in other if z != j]
                new = run(other, min(first, other.index(i)), now)
                if new[5] <= now[5]:
                    for m in pred[j]:
                        succ[m] = [i if z == j else z for z in succ[m]]
                    parts[i] += parts[j]
                    order, now, k = other, new, other.index(i)
                    break
                for m in succ[j]:
                    pred[m] = [z for z in pred[m] if z != i or m in keep[3]] + [j]
                ns[i], join[i], pred[i], succ[i] = keep
    NOTE[:] = [now[4], load]
    return [parts[i] for i in order]


def issue(g, T, topo, core, eng, calls, sender):
    count = {"v": 0, "s": 0, "t": 0, "g": 0}
    clock = {q: {} for q in eng}
    acc = {}
    total = {s: 0 for s in DMAS + ["loc"]}

    def engines(src, dst):
        return topo.engines(src, dst)[:8]

    def region(v):
        if SCRATCH[v[1]][0] == "psum":
            return v[1], 0, 512, True
        return v[1], v[2], v[3], False

    def before(q, reads, writes):
        need, cks = {}, []
        for vs, w in ((reads, False), (writes, True)):
            for v in vs:
                ps = region(v)[3]
                for a in acc.get(v[1], ()):
                    if ps and a[3] != q or (a[0] < v[3] and v[2] < a[1] and (w or a[2]) and not (ps and q == "t") and (v[7] is None or a[7] in (None, v[7]))):
                        need[a[4]] = max(need.get(a[4], 0), a[5])
                        cks.append((a[4], a[6]))
        for s in sorted(need):
            if clock[q].get(s, 0) < need[s] and not any(o != s and ck.get(s, 0) >= need[s] for o, ck in cks):
                eng[q].wait_ge(T.sem[s], need[s])
                clock[q][s] = need[s]
        for _, ck in cks:
            for s, v in ck.items():
                clock[q][s] = max(clock[q].get(s, 0), v)

    def after(q, reads, writes, sem, val):
        ck = dict(clock[q])
        ck[sem] = val
        for vs, w in ((reads, False), (writes, True)):
            for v in vs:
                lst = acc.setdefault(v[1], [])
                if region(v)[3]:
                    lst[:] = [a for a in lst if a[3] == q]
                lst[:] = [a for a in lst if not (v[2] <= a[0] and a[1] <= v[3] and v[7] in (None, a[7]) and (w or a[4] == sem and not a[2]))]
                lst.append((v[2], v[3], w, q, sem, val, ck, v[7]))

    for o in calls:
        if o["kind"] == "send":
            _, src, land, sem = o["call"]
            n = len(engines(T.cores[sender[land](int(sem[1]))], core))
            acc.setdefault(land, []).append((src[2], src[3], True, "x", sem, n, {sem: n}, None))
    for o in calls:
        q = o["q"]
        if TAG[0]:
            TAG[0][0] = o["tag"]
        if o["kind"] == "send":
            dst, src, land, sem = o["call"]
            before(q, o["reads"], [])
            es = engines(core, T.cores[dst])
            rid, pid = topo.addr(T.cores[dst], core)
            g.remote_dma(T[land][:, src[2]:src[3]], src[0], T.sem[sem], T.sem.loc, pid, rid, sum(1 << e for e in es))
            total["loc"] += len(es)
            continue
        before(q, o["reads"], o["writes"])
        if o["kind"] == "dma":
            sem, pairs = o["call"]
            for out, in_, *op in pairs:
                (g.dma_start(out, in_, accum_op=op[0]) if op else eng[q].dma_start(out, in_)).then_inc(T.sem[sem], 16)
            total[sem] += 16 * len(pairs)
            after(q, o["reads"], o["writes"], sem, total[sem])
        else:
            count[q] += 1
            o["call"]().then_inc(T.sem["q" + q], 1)
            after(q, o["reads"], o["writes"], "q" + q, count[q])
    for q in count:
        g.wait_ge(T.sem["q" + q], count[q])
    for s in total:
        if total[s]:
            g.wait_ge(T.sem[s], total[s])
